import numpy as np
import ml_dtypes


def mxq(x, axis, fmt="e4m3"):
    dtype, down = {"e4m3": (ml_dtypes.float8_e4m3fn, 7), "e5m2": (ml_dtypes.float8_e5m2, 14)}[fmt]
    v = np.moveaxis(np.asarray(x, np.float32).astype(ml_dtypes.bfloat16).astype(np.float64), axis, -1)
    blocks = v.reshape(v.shape[:-1] + (-1, 32))
    amax = np.abs(blocks).max(-1, keepdims=True)
    byte = np.maximum(np.where(amax > 0, np.frexp(amax)[1] - 1 + 127, 0) - down, 1)
    scale = np.exp2(byte - 127.0)
    codes = (blocks / scale).astype(np.float32).astype(dtype).astype(np.float64)
    return np.moveaxis((codes * scale).reshape(v.shape), -1, axis)


WIDE = False


def mx_kscale(k):
    if not WIDE:
        return np.ones(k)
    levels = np.array([10, -10, 5, -5, 0])
    if k % 512:
        return np.exp2(np.random.permutation(np.resize(levels, k // 32))).repeat(32)
    a = np.empty((k // 512, 16))
    for p in range(k // 512):
        a[p, :8] = np.random.permutation(np.resize(levels, 8))
        for g in range(8):
            far = levels[np.abs(levels - a[p, g]) >= 10]
            a[p, g + 8] = far[np.random.randint(len(far))]
    return np.exp2(a.ravel()).repeat(32)


def f64(x):
    return np.asarray(x).astype(np.float64)


def striped(idx):
    return np.tile(idx.reshape(-1, 16).T, (8, 1)).astype(np.uint16)


def unstriped(offs):
    return offs[:16].T.reshape(-1).astype(np.int64)


E2M1 = np.array([0.0, 0.5, 1.0, 1.5, 2.0, 3.0, 4.0, 6.0, -0.0, -0.5, -1.0, -1.5, -2.0, -3.0, -4.0, -6.0])


def pack_weight(w, fmt):
    k, n = w.shape
    w = f64(np.asarray(w, np.float32).astype(ml_dtypes.bfloat16)).reshape(k // 32, 32, n)
    amax = np.abs(w).max(1)
    if fmt == "e4m3":
        byte = np.frexp(amax)[1] - 1 + 127 - 7
    else:
        mant, ex = np.frexp(amax / 6.0)
        byte = np.where(mant > 0.5, ex, ex - 1) + 127
    byte = np.clip(np.where(amax > 0, byte, 1), 1, 254)
    scaled = (w * np.exp2(127.0 - byte)[:, None, :]).reshape(k, n).astype(np.float32)
    by_word = np.ascontiguousarray(scaled.reshape(k // 512, 128, 4, n).transpose(0, 1, 3, 2))
    if fmt == "e4m3":
        words = by_word.astype(ml_dtypes.float8_e4m3fn).view(np.uint8)
    else:
        c = by_word.astype(ml_dtypes.float4_e2m1fn).view(np.uint8) & 0xF
        words = (c[..., 0::2] | (c[..., 1::2] << 4)).reshape(k // 512, 128, 2 * n)
    return np.ascontiguousarray(words), np.ascontiguousarray(byte.astype(np.uint8).reshape(k // 512, 16, n))


def unpack_weight(words, scales, fmt):
    g, _, n = scales.shape
    words = np.ascontiguousarray(words).reshape(g, 128, n, -1)
    if fmt == "e4m3":
        vals = words.view(ml_dtypes.float8_e4m3fn).astype(np.float64)
    else:
        nib = np.empty((g, 128, n, 4), np.uint8)
        nib[..., 0::2] = words & 0xF
        nib[..., 1::2] = words >> 4
        vals = E2M1[nib]
    vals = vals * np.repeat(np.exp2(scales.astype(np.float64) - 127.0), 8, axis=1)[..., None]
    return vals.transpose(0, 1, 3, 2).reshape(g * 512, n)


def gelu(v):
    return 0.5 * v * (1.0 + np.tanh(np.sqrt(2.0 / np.pi) * (v + 0.044715 * v**3)))


K, C, H, N, T, S = 1024, 1536, 512, 768, 2048, 1024

def setup_inputs():
    n = np.random.standard_normal
    s = mx_kscale(K)[:, None]
    c = mx_kscale(C)[:, None]
    u = mx_kscale(H)[:, None]
    tab_words, tab_scales = pack_weight(n((K, T)) * s, "e4m3")
    tab2_words, tab2_scales = pack_weight(n((C, T)) * c, "e4m3")
    a2_words, a2_scales = pack_weight(n((K, H)) / np.sqrt(K) / s, "e2m1")
    bd_words, bd_scales = pack_weight(n((C, H)) / np.sqrt(C) / c * u.T, "e4m3")
    return {
        "tab_words": tab_words, "tab_scales": tab_scales,
        "tab2_words": tab2_words, "tab2_scales": tab2_scales,
        "offs": striped(np.random.permutation(T)[:S]),
        "offs2": striped(np.random.permutation(T)[:S]),
        "a1": (n((K, H)) / np.sqrt(K) / s * u.T).astype(np.float32),
        "a2_words": a2_words, "a2_scales": a2_scales,
        "bd_words": bd_words, "bd_scales": bd_scales,
        "gT": (1.0 / (1.0 + np.exp(-1.5 * n((H, T))))).astype(np.float32),
        "w": (1.5 * n((H, N)) / np.sqrt(H) / u).astype(np.float32),
        "by": (0.3 * n(N)).astype(np.float32),
    }

def reference(tab_words, tab_scales, tab2_words, tab2_scales, offs, offs2, a1, a2_words, a2_scales, bd_words, bd_scales, gT, w, by):
    v = unpack_weight(tab_words, tab_scales, "e4m3")[:, unstriped(offs)]
    v2 = unpack_weight(tab2_words, tab2_scales, "e4m3")[:, unstriped(offs2)]
    g = f64(gT)[:, unstriped(offs)]
    p = mxq(f64(a1), 0, "e4m3").T @ v
    q = unpack_weight(a2_words, a2_scales, "e2m1").T @ v
    d = unpack_weight(bd_words, bd_scales, "e4m3").T @ v2
    h = (p * q + d) * g
    y = mxq(f64(w), 0, "e4m3").T @ mxq(h, 0, "e4m3")
    return y + f64(by)[:, None]

@@ -1,0 +1,270 @@
+from contextlib import ExitStack
+
+import concourse.mybir as mybir
+from concourse.masks import make_identity
+
+K, C, H, N, T, S = 1024, 1536, 512, 768, 2048, 1024
+FLOPS = 2 * S * H * (2 * K + C + N)
+
+F32 = mybir.dt.float32
+BF16 = mybir.dt.bfloat16
+I32 = mybir.dt.int32
+U32 = mybir.dt.uint32
+U16 = mybir.dt.uint16
+U8 = mybir.dt.uint8
+FP8X4 = mybir.dt.float8_e4m3fn_x4
+FP4X4 = mybir.dt.float4_e2m1fn_x4
+COPY = mybir.ActivationFunctionType.Copy
+IDENTITY = mybir.ActivationFunctionType.Identity
+MULT = mybir.AluOpType.mult
+ADD = mybir.AluOpType.add
+
+P = 128
+PACK = 4
+K_PASS = P * PACK
+KP = K // K_PASS
+CP = C // K_PASS
+HALF = S // 2
+TILES = S // P
+GROUP = 256
+GROUPS = S // GROUP
+W_CHUNK = 256
+W_CHUNKS = N // W_CHUNK
+LIST = 16
+GATE_BUFS = 3
+
+
+def tile_list_gated_bilinear_decoder_kernel(
+    tc, tab_words, tab_scales, tab2_words, tab2_scales, offs, offs2, a1,
+    a2_words, a2_scales, bd_words, bd_scales, gT, w, by, out,
+):
+    nc = tc.nc
+    with ExitStack() as ctx:
+        keep = ctx.enter_context(tc.tile_pool(name="keep", bufs=1))
+        ring = ctx.enter_context(tc.tile_pool(name="ring", bufs=2))
+        psum = ctx.enter_context(tc.psum_pool(name="psum", bufs=2))
+
+        def held(name, shape, dtype):
+            return keep.tile(shape, dtype, name=name, align_bytes=64)
+
+        idx = held("idx", [P, S // LIST], U16)
+        idx2 = held("idx2", [P, S // LIST], U16)
+        v_scale_win = held("v_scale_win", [P, T], U8)
+        v2_scale_win = held("v2_scale_win", [P, T], U8)
+        a2_sc = held("a2_sc", [P, KP, H], U8)
+        bd_sc = held("bd_sc", [P, H], U8)
+        v_sc = held("v_sc", [P, S], U8)
+        v_sc_low = held("v_sc_low", [P, S], U8)
+        v2_sc = held("v2_sc", [P, S], U8)
+        v_win = [held("v_win%d" % a, [P, T], I32) for a in range(KP)]
+        v2_win = [held("v2_win%d" % a, [P, T], I32) for a in range(CP)]
+        g_win = [held("g_win%d" % t, [P, T], F32) for t in range(PACK)]
+        a1_raw = [held("a1_raw%d" % a, [P, PACK, H], F32) for a in range(KP)]
+        w_raw = [held("w_raw%d" % c, [P, PACK, W_CHUNK], F32) for c in range(W_CHUNKS)]
+        a2_w = held("a2_w", [P, KP, 2 * H], U8)
+        bd_w = held("bd_w", [P, CP, H], I32)
+        bias = held("bias", [P, N // P], F32)
+        ident = held("ident", [P, P], F32)
+
+        nc.gpsimd.memset(v_scale_win[:].bitcast(I32), 0)
+        for plane in (a2_sc[:], v2_scale_win[:], v_sc_low[:], bd_sc[:]):
+            nc.vector.memset(plane.bitcast(I32), 0)
+        make_identity(nc, ident[:])
+
+        def words(src):
+            return src.rearrange("p t i -> p (t i)").bitcast(I32)
+
+        def load_w(c):
+            cols = slice(c * W_CHUNK, (c + 1) * W_CHUNK)
+            nc.sync.dma_start(out=w_raw[c][:], in_=w[:, cols].rearrange("(p j) n -> p j n", j=PACK))
+
+        def load_a1(a):
+            rows = slice(a * K_PASS, (a + 1) * K_PASS)
+            nc.sync.dma_start(out=a1_raw[a][:], in_=a1[rows, :].rearrange("(p j) r -> p j r", j=PACK))
+
+        gate_rows = gT.rearrange("(p t) s -> p t s", t=PACK)
+
+        nc.sync.dma_start(idx[:], offs)
+        nc.sync.dma_start(idx2[:], offs2)
+        for a in range(KP):
+            nc.sync.dma_start(out=v_win[a][:], in_=words(tab_words[a]))
+        load_a1(0)
+        nc.sync.dma_start(out=a2_w[:].bitcast(I32), in_=a2_words.rearrange("a p e -> p a e").bitcast(I32))
+        nc.sync.dma_start(out=v2_win[0][:], in_=words(tab2_words[0]))
+        load_a1(1)
+        for a in range(1, CP):
+            nc.sync.dma_start(out=v2_win[a][:], in_=words(tab2_words[a]))
+        nc.sync.dma_start(out=bd_w[:], in_=bd_words.rearrange("a p e i -> p a (e i)").bitcast(I32))
+        for t in range(PACK):
+            nc.sync.dma_start(out=g_win[t][:], in_=gate_rows[:, t, :])
+        for c in range(W_CHUNKS):
+            load_w(c)
+
+        for Q in range(4):
+            nc.scalar.dma_start(
+                out=v_scale_win[32 * Q : 32 * Q + 4 * KP, :].bitcast(I32),
+                in_=tab_scales[:, 4 * Q : 4 * Q + 4, :].bitcast(I32),
+            )
+        for Q in range(4):
+            nc.scalar.dma_start(
+                out=a2_sc[32 * Q : 32 * Q + 4, :, :].bitcast(I32),
+                in_=a2_scales[:, 4 * Q : 4 * Q + 4, :].rearrange("a r e -> r a e").bitcast(I32),
+            )
+        nc.vector.tensor_copy(v_sc[:], v_scale_win[:].indirect(idx[:]))
+        nc.scalar.dma_start(out=v_sc_low[0:112, :].bitcast(I32), in_=v_sc[4:116, :].bitcast(I32))
+        for Q in range(4):
+            nc.scalar.dma_start(
+                out=v2_scale_win[32 * Q + 4 : 32 * Q + 4 + 4 * CP, :].bitcast(I32),
+                in_=tab2_scales[:, 4 * Q : 4 * Q + 4, :].bitcast(I32),
+            )
+        for Q in range(4):
+            nc.gpsimd.dma_start(
+                out=bd_sc[32 * Q + 4 : 32 * Q + 4 + 4 * CP, :].bitcast(I32),
+                in_=bd_scales[:, 4 * Q : 4 * Q + 4, :].bitcast(I32),
+            )
+        with nc.allow_non_contiguous_dma(reason="one bias value for each partition"):
+            nc.gpsimd.dma_start(out=bias[:], in_=by.rearrange("(c p) -> p c", p=P))
+
+        def entries(lst, first, count):
+            return lst[:, first // LIST : (first + count) // LIST]
+
+        def gather_words(name, win, lst):
+            halves = []
+            for u in range(2):
+                picked = held("%s_%d" % (name, u), [P, HALF], U32)
+                nc.vector.tensor_copy(picked[:], win[:].bitcast(U32).indirect(entries(lst, u * HALF, HALF)))
+                halves.append(picked)
+            return halves
+
+        def token_tile(halves, j):
+            u, first = divmod(j * P, HALF)
+            return halves[u][:, first : first + P].bitcast(FP8X4)
+
+        def rounded_tile(width):
+            return ring.tile([P, width, PACK], BF16, name="rounded", bufs=W_CHUNKS, align_bytes=64)
+
+        def quantize_rows(name, raw, grouped):
+            width = grouped.shape[1]
+            nc.scalar.activation(
+                grouped[:].rearrange("p (c i) t -> p c t i", i=4),
+                raw[:].rearrange("p t (c i) -> p c t i", i=4),
+                COPY,
+            )
+            codes = held(name + "_codes", [P, width], U32)
+            scales = held(name + "_scales", [P, width], U8)
+            nc.vector.quantize_mx(
+                out=codes[:].bitcast(FP8X4), scales=scales[:], in_=grouped[:].rearrange("p w t -> p (w t)")
+            )
+            return codes, scales
+
+        v = [gather_words("v%d" % a, v_win[a], idx) for a in range(KP)]
+        nc.vector.tensor_copy(v2_sc[:], v2_scale_win[:].indirect(idx2[:]))
+
+        def dealt(bank):
+            return bank[:].rearrange("p (m t) -> p t m", t=PACK)
+
+        q_sb = []
+        for j in range(TILES):
+            cols = slice(j * P, (j + 1) * P)
+            acc = psum.tile([P, H], F32, name="acc", bufs=6)
+            for a, plane in enumerate((v_sc, v_sc_low)):
+                nc.tensor.matmul_mx(
+                    out=acc[:], lhsT=token_tile(v[a], j), lhsT_scale=plane[:, cols],
+                    rhs=a2_w[:, a, :].bitcast(FP4X4), rhs_scale=a2_sc[:, a, :],
+                    start=(a == 0), stop=(a == KP - 1),
+                )
+            q = held("q%d" % j, [P, PACK, P], F32)
+            nc.scalar.activation(q[:], dealt(acc), COPY)
+            q_sb.append(q)
+
+        a1_mx = [quantize_rows("a1_%d" % a, a1_raw[a], held("a1_bf%d" % a, [P, H, PACK], BF16)) for a in range(KP)]
+
+        pq_sb = []
+        for j in range(TILES):
+            cols = slice(j * P, (j + 1) * P)
+            acc = psum.tile([P, H], F32, name="acc", bufs=6)
+            for a, (codes, scales) in enumerate(a1_mx):
+                nc.tensor.matmul_mx(
+                    out=acc[:], lhsT=token_tile(v[a], j), lhsT_scale=v_sc[4 * a :, cols],
+                    rhs=codes[:].bitcast(FP8X4), rhs_scale=scales[:],
+                    start=(a == 0), stop=(a == KP - 1),
+                )
+            nc.vector.tensor_tensor(q_sb[j][:], dealt(acc), q_sb[j][:], MULT)
+            pq_sb.append(q_sb[j])
+
+        v2 = [gather_words("v2_%d" % a, v2_win[a], idx2) for a in range(CP)]
+        d_sb = []
+        for j in range(TILES):
+            cols = slice(j * P, (j + 1) * P)
+            acc = psum.tile([P, H], F32, name="acc", bufs=6)
+            for a in range(CP):
+                nc.tensor.matmul_mx(
+                    out=acc[:], lhsT=token_tile(v2[a], j), lhsT_scale=v2_sc[4 * (a + 1) :, cols],
+                    rhs=bd_w[:, a, :].bitcast(FP8X4), rhs_scale=bd_sc[4 * (a + 1) :, :],
+                    start=(a == 0), stop=(a == CP - 1),
+                )
+            d = held("d%d" % j, [P, PACK, P], F32)
+            nc.scalar.activation(d[:], dealt(acc), COPY)
+            d_sb.append(d)
+
+        w_mx = [quantize_rows("w%d" % c, w_raw[c], rounded_tile(W_CHUNK)) for c in range(W_CHUNKS)]
+
+        def gated_tiles(first_tile, count, gate):
+            h = rounded_tile(count * P)
+            for jj in range(count):
+                j = first_tile + jj
+                total = psum.tile([P, PACK, P], F32, name="acc", bufs=6)
+                for t in range(PACK):
+                    for term, first in ((pq_sb[j], True), (d_sb[j], False)):
+                        nc.tensor.matmul(
+                            total[:, t, :], lhsT=term[:, t, :], rhs=ident[:],
+                            is_transpose=True, start=first, stop=not first,
+                        )
+                in_gate = (j * P) % GROUP
+                nc.vector.tensor_tensor(
+                    h[:, jj * P : (jj + 1) * P, :].rearrange("p (c i) t -> p c t i", i=4),
+                    total[:].rearrange("p t (c i) -> p c t i", i=4),
+                    gate[:, :, in_gate : in_gate + P].rearrange("p t (c i) -> p c t i", i=4),
+                    MULT,
+                )
+            h_codes = ring.tile([P, count * P], U32, name="h_codes", align_bytes=64)
+            h_scales = ring.tile([P, count * P], U8, name="h_scales", align_bytes=64)
+            nc.vector.quantize_mx(
+                out=h_codes[:].bitcast(FP8X4), scales=h_scales[:], in_=h[:].rearrange("p s t -> p (s t)")
+            )
+            return h_codes, h_scales
+
+        def project(first_tile, count, h_mx, per_bank, share_with_vector):
+            h_codes, h_scales = h_mx
+            tokens = slice(first_tile * P, (first_tile + count) * P)
+            for b in range(N // P // per_bank):
+                y = psum.tile([P, per_bank, count * P], F32, name="y")
+                staged = ring.tile([P, per_bank, count * P], F32, name="staged", bufs=6)
+                n_tiles = range(b * per_bank, (b + 1) * per_bank)
+                for e, n_tile in enumerate(n_tiles):
+                    codes, scales = w_mx[n_tile * P // W_CHUNK]
+                    in_chunk = (n_tile * P) % W_CHUNK
+                    chans = slice(in_chunk, in_chunk + P)
+                    nc.tensor.matmul_mx(
+                        out=y[:, e, :], lhsT=codes[:, chans].bitcast(FP8X4), lhsT_scale=scales[:, chans],
+                        rhs=h_codes[:].bitcast(FP8X4), rhs_scale=h_scales[:], start=True, stop=True,
+                    )
+                if share_with_vector and b % 2 == 1:
+                    spread = bias[:, n_tiles.start : n_tiles.stop].unsqueeze(2).to_broadcast([P, per_bank, count * P])
+                    nc.vector.tensor_tensor(staged[:], y[:], spread, ADD)
+                else:
+                    for e, n_tile in enumerate(n_tiles):
+                        nc.scalar.activation(staged[:, e, :], y[:, e, :], IDENTITY, bias=bias[:, n_tile : n_tile + 1])
+                rows = slice(n_tiles.start * P, n_tiles.stop * P)
+                nc.sync.dma_start(out=out[rows, tokens].rearrange("(e p) s -> p e s", p=P), in_=staged[:])
+
+        per_group = GROUP // P
+        for grp in range(GROUPS):
+            gate = ring.tile([P, PACK, GROUP], F32, name="gate", bufs=GATE_BUFS)
+            for t in range(PACK):
+                nc.vector.tensor_copy(gate[:, t, :], g_win[t][:].indirect(entries(idx, grp * GROUP, GROUP)))
+            if grp < GROUPS - 1:
+                project(grp * per_group, per_group, gated_tiles(grp * per_group, per_group, gate), 2, False)
+            else:
+                for j in range(grp * per_group, TILES):
+                    project(j, 1, gated_tiles(j, 1, gate), 3, j == TILES - 1)

@@ -95,9 +95,11 @@ def tile_list_gated_bilinear_decoder_kernel(
         for a in range(1, CP):
             nc.sync.dma_start(out=v2_win[a][:], in_=words(tab2_words[a]))
         nc.sync.dma_start(out=bd_w[:], in_=bd_words.rearrange("a p e i -> p a (e i)").bitcast(I32))
-        for t in range(PACK):
+        for t in range(PACK - 1):
             nc.sync.dma_start(out=g_win[t][:], in_=gate_rows[:, t, :])
-        for c in range(W_CHUNKS):
+        load_w(0)
+        nc.sync.dma_start(out=g_win[PACK - 1][:], in_=gate_rows[:, PACK - 1, :])
+        for c in range(1, W_CHUNKS):
             load_w(c)
 
         for Q in range(4):
@@ -146,8 +148,8 @@ def tile_list_gated_bilinear_decoder_kernel(
         def quantize_rows(name, raw, grouped):
             width = grouped.shape[1]
             nc.scalar.activation(
-                grouped[:].rearrange("p (c i) t -> p c t i", i=4),
-                raw[:].rearrange("p t (c i) -> p c t i", i=4),
+                grouped[:].rearrange("p (c i) t -> p c t i", i=2),
+                raw[:].rearrange("p t (c i) -> p c t i", i=2),
                 COPY,
             )
             codes = held(name + "_codes", [P, width], U32)
@@ -222,9 +224,9 @@ def tile_list_gated_bilinear_decoder_kernel(
                         )
                 in_gate = (j * P) % GROUP
                 nc.vector.tensor_tensor(
-                    h[:, jj * P : (jj + 1) * P, :].rearrange("p (c i) t -> p c t i", i=4),
-                    total[:].rearrange("p t (c i) -> p c t i", i=4),
-                    gate[:, :, in_gate : in_gate + P].rearrange("p t (c i) -> p c t i", i=4),
+                    h[:, jj * P : (jj + 1) * P, :].rearrange("p (c i) t -> p c t i", i=2),
+                    total[:].rearrange("p t (c i) -> p c t i", i=2),
+                    gate[:, :, in_gate : in_gate + P].rearrange("p t (c i) -> p c t i", i=2),
                     MULT,
                 )
             h_codes = ring.tile([P, count * P], U32, name="h_codes", align_bytes=64)

@@ -52,7 +52,7 @@ def tile_list_gated_bilinear_decoder_kernel(
         v_scale_win = held("v_scale_win", [P, T], U8)
         v2_scale_win = held("v2_scale_win", [P, T], U8)
         a2_sc = held("a2_sc", [P, KP, H], U8)
-        bd_sc = held("bd_sc", [P, H], U8)
+        bd_sc = held("bd_sc", [P, CP, H], U8)
         v_sc = held("v_sc", [P, S], U8)
         v_sc_low = held("v_sc_low", [P, S], U8)
         v2_sc = held("v2_sc", [P, S], U8)
@@ -67,7 +67,7 @@ def tile_list_gated_bilinear_decoder_kernel(
         ident = held("ident", [P, P], F32)
 
         nc.gpsimd.memset(v_scale_win[:].bitcast(I32), 0)
-        for plane in (a2_sc[:], v2_scale_win[:], v_sc_low[:], bd_sc[:]):
+        for plane in (v2_scale_win[:], v_sc_low[:], a2_sc[:], bd_sc[:]):
             nc.vector.memset(plane.bitcast(I32), 0)
         make_identity(nc, ident[:])
 
@@ -88,15 +88,22 @@ def tile_list_gated_bilinear_decoder_kernel(
         nc.sync.dma_start(idx2[:], offs2)
         for a in range(KP):
             nc.sync.dma_start(out=v_win[a][:], in_=words(tab_words[a]))
-        load_a1(0)
+        for a in range(KP):
+            load_a1(a)
         nc.sync.dma_start(out=a2_w[:].bitcast(I32), in_=a2_words.rearrange("a p e -> p a e").bitcast(I32))
-        nc.sync.dma_start(out=v2_win[0][:], in_=words(tab2_words[0]))
-        load_a1(1)
-        for a in range(1, CP):
+        for a in range(CP):
             nc.sync.dma_start(out=v2_win[a][:], in_=words(tab2_words[a]))
+            if a < 2:
+                for Q in (2 * a, 2 * a + 1):
+                    nc.sync.dma_start(
+                        out=bd_sc[32 * Q : 32 * Q + 4, :, :].bitcast(I32),
+                        in_=bd_scales[:, 4 * Q : 4 * Q + 4, :].rearrange("a r e -> r a e").bitcast(I32),
+                    )
         nc.sync.dma_start(out=bd_w[:], in_=bd_words.rearrange("a p e i -> p a (e i)").bitcast(I32))
         for t in range(PACK - 1):
             nc.sync.dma_start(out=g_win[t][:], in_=gate_rows[:, t, :])
+        with nc.allow_non_contiguous_dma(reason="one bias value for each partition"):
+            nc.sync.dma_start(out=bias[:], in_=by.rearrange("(c p) -> p c", p=P))
         load_w(0)
         nc.sync.dma_start(out=g_win[PACK - 1][:], in_=gate_rows[:, PACK - 1, :])
         for c in range(1, W_CHUNKS):
@@ -109,38 +116,32 @@ def tile_list_gated_bilinear_decoder_kernel(
             )
         for Q in range(4):
             nc.scalar.dma_start(
-                out=a2_sc[32 * Q : 32 * Q + 4, :, :].bitcast(I32),
-                in_=a2_scales[:, 4 * Q : 4 * Q + 4, :].rearrange("a r e -> r a e").bitcast(I32),
+                out=v2_scale_win[32 * Q + 4 : 32 * Q + 4 + 4 * CP, :].bitcast(I32),
+                in_=tab2_scales[:, 4 * Q : 4 * Q + 4, :].bitcast(I32),
             )
         nc.vector.tensor_copy(v_sc[:], v_scale_win[:].indirect(idx[:]))
         nc.scalar.dma_start(out=v_sc_low[0:112, :].bitcast(I32), in_=v_sc[4:116, :].bitcast(I32))
         for Q in range(4):
             nc.scalar.dma_start(
-                out=v2_scale_win[32 * Q + 4 : 32 * Q + 4 + 4 * CP, :].bitcast(I32),
-                in_=tab2_scales[:, 4 * Q : 4 * Q + 4, :].bitcast(I32),
+                out=a2_sc[32 * Q : 32 * Q + 4, :, :].bitcast(I32),
+                in_=a2_scales[:, 4 * Q : 4 * Q + 4, :].rearrange("a r e -> r a e").bitcast(I32),
             )
-        for Q in range(4):
-            nc.gpsimd.dma_start(
-                out=bd_sc[32 * Q + 4 : 32 * Q + 4 + 4 * CP, :].bitcast(I32),
-                in_=bd_scales[:, 4 * Q : 4 * Q + 4, :].bitcast(I32),
-            )
-        with nc.allow_non_contiguous_dma(reason="one bias value for each partition"):
-            nc.gpsimd.dma_start(out=bias[:], in_=by.rearrange("(c p) -> p c", p=P))
 
         def entries(lst, first, count):
             return lst[:, first // LIST : (first + count) // LIST]
 
-        def gather_words(name, win, lst):
-            halves = []
-            for u in range(2):
-                picked = held("%s_%d" % (name, u), [P, HALF], U32)
-                nc.vector.tensor_copy(picked[:], win[:].bitcast(U32).indirect(entries(lst, u * HALF, HALF)))
-                halves.append(picked)
-            return halves
+        def gather_words(name, win, lst, pieces):
+            count = S // pieces
+            parts = []
+            for u in range(pieces):
+                picked = held("%s_%d" % (name, u), [P, count], U32)
+                nc.vector.tensor_copy(picked[:], win[:].bitcast(U32).indirect(entries(lst, u * count, count)))
+                parts.append(picked)
+            return parts
 
-        def token_tile(halves, j):
-            u, first = divmod(j * P, HALF)
-            return halves[u][:, first : first + P].bitcast(FP8X4)
+        def token_tile(parts, j):
+            u, first = divmod(j * P, S // len(parts))
+            return parts[u][:, first : first + P].bitcast(FP8X4)
 
         def rounded_tile(width):
             return ring.tile([P, width, PACK], BF16, name="rounded", bufs=W_CHUNKS, align_bytes=64)
@@ -159,42 +160,38 @@ def tile_list_gated_bilinear_decoder_kernel(
             )
             return codes, scales
 
-        v = [gather_words("v%d" % a, v_win[a], idx) for a in range(KP)]
         nc.vector.tensor_copy(v2_sc[:], v2_scale_win[:].indirect(idx2[:]))
+        v = [gather_words("v%d" % a, v_win[a], idx, 2 if a == KP - 1 else 1) for a in range(KP)]
 
         def dealt(bank):
             return bank[:].rearrange("p (m t) -> p t m", t=PACK)
-
-        q_sb = []
-        for j in range(TILES):
-            cols = slice(j * P, (j + 1) * P)
-            acc = psum.tile([P, H], F32, name="acc", bufs=6)
-            for a, plane in enumerate((v_sc, v_sc_low)):
-                nc.tensor.matmul_mx(
-                    out=acc[:], lhsT=token_tile(v[a], j), lhsT_scale=plane[:, cols],
-                    rhs=a2_w[:, a, :].bitcast(FP4X4), rhs_scale=a2_sc[:, a, :],
-                    start=(a == 0), stop=(a == KP - 1),
-                )
-            q = held("q%d" % j, [P, PACK, P], F32)
-            nc.scalar.activation(q[:], dealt(acc), COPY)
-            q_sb.append(q)
 
         a1_mx = [quantize_rows("a1_%d" % a, a1_raw[a], held("a1_bf%d" % a, [P, H, PACK], BF16)) for a in range(KP)]
 
         pq_sb = []
         for j in range(TILES):
             cols = slice(j * P, (j + 1) * P)
-            acc = psum.tile([P, H], F32, name="acc", bufs=6)
+            q_acc = psum.tile([P, H], F32, name="acc", bufs=6)
+            for a, plane in enumerate((v_sc, v_sc_low)):
+                nc.tensor.matmul_mx(
+                    out=q_acc[:], lhsT=token_tile(v[a], j), lhsT_scale=plane[:, cols],
+                    rhs=a2_w[:, a, :].bitcast(FP4X4), rhs_scale=a2_sc[:, a, :],
+                    start=(a == 0), stop=(a == KP - 1),
+                )
+            q = ring.tile([P, PACK, P], F32, name="q", bufs=3)
+            nc.scalar.activation(q[:], dealt(q_acc), COPY)
+            p_acc = psum.tile([P, H], F32, name="acc", bufs=6)
             for a, (codes, scales) in enumerate(a1_mx):
                 nc.tensor.matmul_mx(
-                    out=acc[:], lhsT=token_tile(v[a], j), lhsT_scale=v_sc[4 * a :, cols],
+                    out=p_acc[:], lhsT=token_tile(v[a], j), lhsT_scale=v_sc[4 * a :, cols],
                     rhs=codes[:].bitcast(FP8X4), rhs_scale=scales[:],
                     start=(a == 0), stop=(a == KP - 1),
                 )
-            nc.vector.tensor_tensor(q_sb[j][:], dealt(acc), q_sb[j][:], MULT)
-            pq_sb.append(q_sb[j])
+            pq = held("pq%d" % j, [P, PACK, P], F32)
+            nc.vector.tensor_tensor(pq[:], dealt(p_acc), q[:], MULT)
+            pq_sb.append(pq)
 
-        v2 = [gather_words("v2_%d" % a, v2_win[a], idx2) for a in range(CP)]
+        v2 = [gather_words("v2_%d" % a, v2_win[a], idx2, 2 if a == CP - 1 else 1) for a in range(CP)]
         d_sb = []
         for j in range(TILES):
             cols = slice(j * P, (j + 1) * P)
@@ -202,7 +199,7 @@ def tile_list_gated_bilinear_decoder_kernel(
             for a in range(CP):
                 nc.tensor.matmul_mx(
                     out=acc[:], lhsT=token_tile(v2[a], j), lhsT_scale=v2_sc[4 * (a + 1) :, cols],
-                    rhs=bd_w[:, a, :].bitcast(FP8X4), rhs_scale=bd_sc[4 * (a + 1) :, :],
+                    rhs=bd_w[:, a, :].bitcast(FP8X4), rhs_scale=bd_sc[:, a, :],
                     start=(a == 0), stop=(a == CP - 1),
                 )
             d = held("d%d" % j, [P, PACK, P], F32)

@@ -32,6 +32,7 @@ W_CHUNK = 256
 W_CHUNKS = N // W_CHUNK
 LIST = 16
 GATE_BUFS = 3
+RING = 6
 
 
 def tile_list_gated_bilinear_decoder_kernel(
@@ -44,8 +45,8 @@ def tile_list_gated_bilinear_decoder_kernel(
         ring = ctx.enter_context(tc.tile_pool(name="ring", bufs=2))
         psum = ctx.enter_context(tc.psum_pool(name="psum", bufs=2))
 
-        def held(name, shape, dtype):
-            return keep.tile(shape, dtype, name=name, align_bytes=64)
+        def held(name, shape, dtype, tag=""):
+            return keep.tile(shape, dtype, name=name, tag=tag or name, align_bytes=64)
 
         idx = held("idx", [P, S // LIST], U16)
         idx2 = held("idx2", [P, S // LIST], U16)
@@ -86,28 +87,28 @@ def tile_list_gated_bilinear_decoder_kernel(
 
         nc.sync.dma_start(idx[:], offs)
         nc.sync.dma_start(idx2[:], offs2)
-        for a in range(KP):
-            nc.sync.dma_start(out=v_win[a][:], in_=words(tab_words[a]))
-        for a in range(KP):
-            load_a1(a)
+        nc.sync.dma_start(out=v_win[0][:], in_=words(tab_words[0]))
+        nc.sync.dma_start(out=v_win[1][:], in_=words(tab_words[1]))
+        load_a1(0)
+        load_a1(1)
         nc.sync.dma_start(out=a2_w[:].bitcast(I32), in_=a2_words.rearrange("a p e -> p a e").bitcast(I32))
-        for a in range(CP):
-            nc.sync.dma_start(out=v2_win[a][:], in_=words(tab2_words[a]))
-            if a < 2:
-                for Q in (2 * a, 2 * a + 1):
-                    nc.sync.dma_start(
-                        out=bd_sc[32 * Q : 32 * Q + 4, :, :].bitcast(I32),
-                        in_=bd_scales[:, 4 * Q : 4 * Q + 4, :].rearrange("a r e -> r a e").bitcast(I32),
-                    )
+        nc.sync.dma_start(out=v2_win[0][:], in_=words(tab2_words[0]))
+        nc.sync.dma_start(out=v2_win[1][:], in_=words(tab2_words[1]))
+        nc.sync.dma_start(out=bd_sc[0 : 4, :, :].bitcast(I32), in_=bd_scales[:, 0 : 4, :].rearrange("a r e -> r a e").bitcast(I32))
+        nc.sync.dma_start(out=bd_sc[32 : 36, :, :].bitcast(I32), in_=bd_scales[:, 4 : 8, :].rearrange("a r e -> r a e").bitcast(I32))
+        nc.sync.dma_start(out=v2_win[2][:], in_=words(tab2_words[2]))
+        nc.sync.dma_start(out=bd_sc[64 : 68, :, :].bitcast(I32), in_=bd_scales[:, 8 : 12, :].rearrange("a r e -> r a e").bitcast(I32))
+        nc.sync.dma_start(out=bd_sc[96 : 100, :, :].bitcast(I32), in_=bd_scales[:, 12 : 16, :].rearrange("a r e -> r a e").bitcast(I32))
         nc.sync.dma_start(out=bd_w[:], in_=bd_words.rearrange("a p e i -> p a (e i)").bitcast(I32))
-        for t in range(PACK - 1):
-            nc.sync.dma_start(out=g_win[t][:], in_=gate_rows[:, t, :])
+        load_w(0)
+        nc.sync.dma_start(out=g_win[0][:], in_=gate_rows[:, 0, :])
+        nc.sync.dma_start(out=g_win[1][:], in_=gate_rows[:, 1, :])
+        nc.sync.dma_start(out=g_win[2][:], in_=gate_rows[:, 2, :])
+        nc.sync.dma_start(out=g_win[3][:], in_=gate_rows[:, 3, :])
+        load_w(1)
+        load_w(2)
         with nc.allow_non_contiguous_dma(reason="one bias value for each partition"):
             nc.sync.dma_start(out=bias[:], in_=by.rearrange("(c p) -> p c", p=P))
-        load_w(0)
-        nc.sync.dma_start(out=g_win[PACK - 1][:], in_=gate_rows[:, PACK - 1, :])
-        for c in range(1, W_CHUNKS):
-            load_w(c)
 
         for Q in range(4):
             nc.scalar.dma_start(
@@ -143,11 +144,8 @@ def tile_list_gated_bilinear_decoder_kernel(
             u, first = divmod(j * P, S // len(parts))
             return parts[u][:, first : first + P].bitcast(FP8X4)
 
-        def rounded_tile(width):
-            return ring.tile([P, width, PACK], BF16, name="rounded", bufs=W_CHUNKS, align_bytes=64)
-
-        def quantize_rows(name, raw, grouped):
-            width = grouped.shape[1]
+        def quantize_rows(name, raw, width):
+            grouped = ring.tile([P, width, PACK], BF16, name="rounded", align_bytes=64)
             nc.scalar.activation(
                 grouped[:].rearrange("p (c i) t -> p c t i", i=2),
                 raw[:].rearrange("p t (c i) -> p c t i", i=2),
@@ -160,42 +158,55 @@ def tile_list_gated_bilinear_decoder_kernel(
             )
             return codes, scales
 
-        nc.vector.tensor_copy(v2_sc[:], v2_scale_win[:].indirect(idx2[:]))
         v = [gather_words("v%d" % a, v_win[a], idx, 2 if a == KP - 1 else 1) for a in range(KP)]
+        nc.vector.tensor_copy(v2_sc[:], v2_scale_win[:].indirect(idx2[:]))
 
         def dealt(bank):
             return bank[:].rearrange("p (m t) -> p t m", t=PACK)
 
-        a1_mx = [quantize_rows("a1_%d" % a, a1_raw[a], held("a1_bf%d" % a, [P, H, PACK], BF16)) for a in range(KP)]
+        a1_mx = [quantize_rows("a1_%d" % a, a1_raw[a], H) for a in range(KP)]
 
-        pq_sb = []
+        q_sb = []
         for j in range(TILES):
             cols = slice(j * P, (j + 1) * P)
-            q_acc = psum.tile([P, H], F32, name="acc", bufs=6)
+            acc = psum.tile([P, H], F32, name="bank", bufs=6)
             for a, plane in enumerate((v_sc, v_sc_low)):
                 nc.tensor.matmul_mx(
-                    out=q_acc[:], lhsT=token_tile(v[a], j), lhsT_scale=plane[:, cols],
+                    out=acc[:], lhsT=token_tile(v[a], j), lhsT_scale=plane[:, cols],
                     rhs=a2_w[:, a, :].bitcast(FP4X4), rhs_scale=a2_sc[:, a, :],
                     start=(a == 0), stop=(a == KP - 1),
                 )
-            q = ring.tile([P, PACK, P], F32, name="q", bufs=3)
-            nc.scalar.activation(q[:], dealt(q_acc), COPY)
-            p_acc = psum.tile([P, H], F32, name="acc", bufs=6)
+            q = held("q%d" % j, [P, PACK, P], F32)
+            nc.scalar.activation(q[:], dealt(acc), COPY)
+            q_sb.append(q)
+
+        p_halves = [held("p%d" % a, [P, TILES // KP, PACK, P], F32, tag="a1_raw%d" % a) for a in range(KP)]
+        p_sb = []
+        for j in range(TILES):
+            cols = slice(j * P, (j + 1) * P)
+            acc = psum.tile([P, H], F32, name="bank", bufs=6)
             for a, (codes, scales) in enumerate(a1_mx):
                 nc.tensor.matmul_mx(
-                    out=p_acc[:], lhsT=token_tile(v[a], j), lhsT_scale=v_sc[4 * a :, cols],
+                    out=acc[:], lhsT=token_tile(v[a], j), lhsT_scale=v_sc[4 * a :, cols],
                     rhs=codes[:].bitcast(FP8X4), rhs_scale=scales[:],
                     start=(a == 0), stop=(a == KP - 1),
                 )
-            pq = held("pq%d" % j, [P, PACK, P], F32)
-            nc.vector.tensor_tensor(pq[:], dealt(p_acc), q[:], MULT)
-            pq_sb.append(pq)
+            u, jj = divmod(j, TILES // KP)
+            nc.scalar.activation(p_halves[u][:, jj], dealt(acc), COPY)
+            p_sb.append(p_halves[u][:, jj])
 
         v2 = [gather_words("v2_%d" % a, v2_win[a], idx2, 2 if a == CP - 1 else 1) for a in range(CP)]
+
+        pq_all = held("pq_all", [P, TILES, PACK, P], F32, tag="v2_win%d" % (CP - 1))
+        pq_sb = []
+        for j in range(TILES):
+            nc.vector.tensor_tensor(pq_all[:, j], p_sb[j], q_sb[j][:], MULT)
+            pq_sb.append(pq_all[:, j])
+
         d_sb = []
         for j in range(TILES):
             cols = slice(j * P, (j + 1) * P)
-            acc = psum.tile([P, H], F32, name="acc", bufs=6)
+            acc = psum.tile([P, H], F32, name="bank", bufs=6)
             for a in range(CP):
                 nc.tensor.matmul_mx(
                     out=acc[:], lhsT=token_tile(v2[a], j), lhsT_scale=v2_sc[4 * (a + 1) :, cols],
@@ -206,19 +217,28 @@ def tile_list_gated_bilinear_decoder_kernel(
             nc.scalar.activation(d[:], dealt(acc), COPY)
             d_sb.append(d)
 
-        w_mx = [quantize_rows("w%d" % c, w_raw[c], rounded_tile(W_CHUNK)) for c in range(W_CHUNKS)]
+        w_mx = [quantize_rows("w%d" % c, w_raw[c], W_CHUNK) for c in range(W_CHUNKS)]
+
+        def turned_sum(j):
+            if j < RING:
+                total = psum.tile([P, PACK, P], F32, name="bank", bufs=6)
+            else:
+                total = psum.tile([P, PACK, P], F32, name="late_sum")
+            for t in range(PACK):
+                for term, first in ((pq_sb[j], True), (d_sb[j], False)):
+                    nc.tensor.matmul(
+                        total[:, t, :], lhsT=term[:, t, :], rhs=ident[:],
+                        is_transpose=True, start=first, stop=not first,
+                    )
+            return total
+
+        sums = [turned_sum(j) for j in range(TILES)]
 
         def gated_tiles(first_tile, count, gate):
-            h = rounded_tile(count * P)
+            h = held("h%d" % first_tile, [P, count * P, PACK], BF16)
             for jj in range(count):
                 j = first_tile + jj
-                total = psum.tile([P, PACK, P], F32, name="acc", bufs=6)
-                for t in range(PACK):
-                    for term, first in ((pq_sb[j], True), (d_sb[j], False)):
-                        nc.tensor.matmul(
-                            total[:, t, :], lhsT=term[:, t, :], rhs=ident[:],
-                            is_transpose=True, start=first, stop=not first,
-                        )
+                total = sums[j]
                 in_gate = (j * P) % GROUP
                 nc.vector.tensor_tensor(
                     h[:, jj * P : (jj + 1) * P, :].rearrange("p (c i) t -> p c t i", i=2),
@@ -226,8 +246,8 @@ def tile_list_gated_bilinear_decoder_kernel(
                     gate[:, :, in_gate : in_gate + P].rearrange("p t (c i) -> p c t i", i=2),
                     MULT,
                 )
-            h_codes = ring.tile([P, count * P], U32, name="h_codes", align_bytes=64)
-            h_scales = ring.tile([P, count * P], U8, name="h_scales", align_bytes=64)
+            h_codes = held("h_codes%d" % first_tile, [P, count * P], U32)
+            h_scales = held("h_scales%d" % first_tile, [P, count * P], U8)
             nc.vector.quantize_mx(
                 out=h_codes[:].bitcast(FP8X4), scales=h_scales[:], in_=h[:].rearrange("p s t -> p (s t)")
             )
@@ -237,7 +257,7 @@ def tile_list_gated_bilinear_decoder_kernel(
             h_codes, h_scales = h_mx
             tokens = slice(first_tile * P, (first_tile + count) * P)
             for b in range(N // P // per_bank):
-                y = psum.tile([P, per_bank, count * P], F32, name="y")
+                y = psum.tile([P, per_bank, count * P], F32, name="bank", bufs=6)
                 staged = ring.tile([P, per_bank, count * P], F32, name="staged", bufs=6)
                 n_tiles = range(b * per_bank, (b + 1) * per_bank)
                 for e, n_tile in enumerate(n_tiles):
@@ -259,11 +279,12 @@ def tile_list_gated_bilinear_decoder_kernel(
 
         per_group = GROUP // P
         for grp in range(GROUPS):
-            gate = ring.tile([P, PACK, GROUP], F32, name="gate", bufs=GATE_BUFS)
+            gate = held("gate%d" % grp, [P, PACK, GROUP], F32, tag="gate%d" % min(grp, GATE_BUFS - 1))
             for t in range(PACK):
                 nc.vector.tensor_copy(gate[:, t, :], g_win[t][:].indirect(entries(idx, grp * GROUP, GROUP)))
             if grp < GROUPS - 1:
                 project(grp * per_group, per_group, gated_tiles(grp * per_group, per_group, gate), 2, False)
             else:
-                for j in range(grp * per_group, TILES):
-                    project(j, 1, gated_tiles(j, 1, gate), 3, j == TILES - 1)
+                last = [(j, gated_tiles(j, 1, gate)) for j in range(grp * per_group, TILES)]
+                for j, h_mx in last:
+                    project(j, 1, h_mx, 3, True)

@@ -24,15 +24,13 @@ PACK = 4
 K_PASS = P * PACK
 KP = K // K_PASS
 CP = C // K_PASS
-HALF = S // 2
 TILES = S // P
-GROUP = 256
-GROUPS = S // GROUP
 W_CHUNK = 256
 W_CHUNKS = N // W_CHUNK
 LIST = 16
-GATE_BUFS = 3
-RING = 6
+RUN = 4
+GROUPS = ((0, 4), (4, 2), (6, 2))
+MOVED = 100
 
 
 def tile_list_gated_bilinear_decoder_kernel(
@@ -42,8 +40,7 @@ def tile_list_gated_bilinear_decoder_kernel(
     nc = tc.nc
     with ExitStack() as ctx:
         keep = ctx.enter_context(tc.tile_pool(name="keep", bufs=1))
-        ring = ctx.enter_context(tc.tile_pool(name="ring", bufs=2))
-        psum = ctx.enter_context(tc.psum_pool(name="psum", bufs=2))
+        psum = ctx.enter_context(tc.psum_pool(name="psum", bufs=8))
 
         def held(name, shape, dtype, tag=""):
             return keep.tile(shape, dtype, name=name, tag=tag or name, align_bytes=64)
@@ -56,7 +53,6 @@ def tile_list_gated_bilinear_decoder_kernel(
         bd_sc = held("bd_sc", [P, CP, H], U8)
         v_sc = held("v_sc", [P, S], U8)
         v_sc_low = held("v_sc_low", [P, S], U8)
-        v2_sc = held("v2_sc", [P, S], U8)
         v_win = [held("v_win%d" % a, [P, T], I32) for a in range(KP)]
         v2_win = [held("v2_win%d" % a, [P, T], I32) for a in range(CP)]
         g_win = [held("g_win%d" % t, [P, T], F32) for t in range(PACK)]
@@ -67,66 +63,59 @@ def tile_list_gated_bilinear_decoder_kernel(
         bias = held("bias", [P, N // P], F32)
         ident = held("ident", [P, P], F32)
 
-        nc.gpsimd.memset(v_scale_win[:].bitcast(I32), 0)
-        for plane in (v2_scale_win[:], v_sc_low[:], a2_sc[:], bd_sc[:]):
+        nc.gpsimd.memset(v2_scale_win[:].bitcast(I32), 0)
+        for plane in (v_scale_win[:], a2_sc[:], v_sc_low[:], bd_sc[:]):
             nc.vector.memset(plane.bitcast(I32), 0)
-        make_identity(nc, ident[:])
 
         def words(src):
             return src.rearrange("p t i -> p (t i)").bitcast(I32)
 
-        def load_w(c):
-            cols = slice(c * W_CHUNK, (c + 1) * W_CHUNK)
-            nc.sync.dma_start(out=w_raw[c][:], in_=w[:, cols].rearrange("(p j) n -> p j n", j=PACK))
+        def load_rows(dst, src):
+            nc.sync.dma_start(out=dst[:], in_=src.rearrange("(p j) n -> p j n", j=PACK))
 
-        def load_a1(a):
-            rows = slice(a * K_PASS, (a + 1) * K_PASS)
-            nc.sync.dma_start(out=a1_raw[a][:], in_=a1[rows, :].rearrange("(p j) r -> p j r", j=PACK))
+        def load_planes(queue, plane, src):
+            for Q in range(4):
+                queue.dma_start(
+                    out=plane[32 * Q : 32 * Q + 4, :, :].bitcast(I32),
+                    in_=src[:, 4 * Q : 4 * Q + 4, :].rearrange("a r e -> r a e").bitcast(I32),
+                )
 
         gate_rows = gT.rearrange("(p t) s -> p t s", t=PACK)
 
         nc.sync.dma_start(idx[:], offs)
-        nc.sync.dma_start(idx2[:], offs2)
-        nc.sync.dma_start(out=v_win[0][:], in_=words(tab_words[0]))
-        nc.sync.dma_start(out=v_win[1][:], in_=words(tab_words[1]))
-        load_a1(0)
-        load_a1(1)
-        nc.sync.dma_start(out=a2_w[:].bitcast(I32), in_=a2_words.rearrange("a p e -> p a e").bitcast(I32))
-        nc.sync.dma_start(out=v2_win[0][:], in_=words(tab2_words[0]))
-        nc.sync.dma_start(out=v2_win[1][:], in_=words(tab2_words[1]))
-        nc.sync.dma_start(out=bd_sc[0 : 4, :, :].bitcast(I32), in_=bd_scales[:, 0 : 4, :].rearrange("a r e -> r a e").bitcast(I32))
-        nc.sync.dma_start(out=bd_sc[32 : 36, :, :].bitcast(I32), in_=bd_scales[:, 4 : 8, :].rearrange("a r e -> r a e").bitcast(I32))
-        nc.sync.dma_start(out=v2_win[2][:], in_=words(tab2_words[2]))
-        nc.sync.dma_start(out=bd_sc[64 : 68, :, :].bitcast(I32), in_=bd_scales[:, 8 : 12, :].rearrange("a r e -> r a e").bitcast(I32))
-        nc.sync.dma_start(out=bd_sc[96 : 100, :, :].bitcast(I32), in_=bd_scales[:, 12 : 16, :].rearrange("a r e -> r a e").bitcast(I32))
-        nc.sync.dma_start(out=bd_w[:], in_=bd_words.rearrange("a p e i -> p a (e i)").bitcast(I32))
-        load_w(0)
-        nc.sync.dma_start(out=g_win[0][:], in_=gate_rows[:, 0, :])
-        nc.sync.dma_start(out=g_win[1][:], in_=gate_rows[:, 1, :])
-        nc.sync.dma_start(out=g_win[2][:], in_=gate_rows[:, 2, :])
-        nc.sync.dma_start(out=g_win[3][:], in_=gate_rows[:, 3, :])
-        load_w(1)
-        load_w(2)
-        with nc.allow_non_contiguous_dma(reason="one bias value for each partition"):
-            nc.sync.dma_start(out=bias[:], in_=by.rearrange("(c p) -> p c", p=P))
-
         for Q in range(4):
             nc.scalar.dma_start(
                 out=v_scale_win[32 * Q : 32 * Q + 4 * KP, :].bitcast(I32),
                 in_=tab_scales[:, 4 * Q : 4 * Q + 4, :].bitcast(I32),
             )
+        nc.vector.tensor_copy(v_sc[:], v_scale_win[:].indirect(idx[:]))
+        for a in range(KP):
+            load_rows(a1_raw[a], a1[a * K_PASS : (a + 1) * K_PASS, :])
+            if a == 1:
+                nc.sync.dma_start(out=a2_w[:].bitcast(I32), in_=a2_words.rearrange("a p e -> p a e").bitcast(I32))
+            nc.sync.dma_start(out=v_win[a][:], in_=words(tab_words[a]))
+            if a == 0:
+                nc.sync.dma_start(idx2[:], offs2)
+        load_planes(nc.sync, a2_sc, a2_scales)
+        nc.sync.dma_start(out=v_sc_low[0:MOVED, :].bitcast(I32), in_=v_sc[4 : 4 + MOVED, :].bitcast(I32))
+        for a in range(CP):
+            nc.sync.dma_start(out=v2_win[a][:], in_=words(tab2_words[a]))
+            if a == 0:
+                load_planes(nc.sync, bd_sc, bd_scales)
+        nc.sync.dma_start(out=bd_w[:], in_=bd_words.rearrange("a p e i -> p a (e i)").bitcast(I32))
+        for t in range(PACK):
+            nc.sync.dma_start(out=g_win[t][:], in_=gate_rows[:, t, :])
+        for c in range(W_CHUNKS):
+            load_rows(w_raw[c], w[:, c * W_CHUNK : (c + 1) * W_CHUNK])
+        with nc.allow_non_contiguous_dma(reason="one bias value for each partition"):
+            nc.sync.dma_start(out=bias[:], in_=by.rearrange("(c p) -> p c", p=P))
+
         for Q in range(4):
-            nc.scalar.dma_start(
+            nc.gpsimd.dma_start(
                 out=v2_scale_win[32 * Q + 4 : 32 * Q + 4 + 4 * CP, :].bitcast(I32),
                 in_=tab2_scales[:, 4 * Q : 4 * Q + 4, :].bitcast(I32),
             )
-        nc.vector.tensor_copy(v_sc[:], v_scale_win[:].indirect(idx[:]))
-        nc.scalar.dma_start(out=v_sc_low[0:112, :].bitcast(I32), in_=v_sc[4:116, :].bitcast(I32))
-        for Q in range(4):
-            nc.scalar.dma_start(
-                out=a2_sc[32 * Q : 32 * Q + 4, :, :].bitcast(I32),
-                in_=a2_scales[:, 4 * Q : 4 * Q + 4, :].rearrange("a r e -> r a e").bitcast(I32),
-            )
+        make_identity(nc, ident[:])
 
         def entries(lst, first, count):
             return lst[:, first // LIST : (first + count) // LIST]
@@ -145,10 +134,10 @@ def tile_list_gated_bilinear_decoder_kernel(
             return parts[u][:, first : first + P].bitcast(FP8X4)
 
         def quantize_rows(name, raw, width):
-            grouped = ring.tile([P, width, PACK], BF16, name="rounded", align_bytes=64)
+            grouped = held(name + "_rounded", [P, width, PACK], BF16)
             nc.scalar.activation(
-                grouped[:].rearrange("p (c i) t -> p c t i", i=2),
-                raw[:].rearrange("p t (c i) -> p c t i", i=2),
+                grouped[:].rearrange("p (c i) t -> p c t i", i=RUN),
+                raw[:].rearrange("p t (c i) -> p c t i", i=RUN),
                 COPY,
             )
             codes = held(name + "_codes", [P, width], U32)
@@ -158,92 +147,93 @@ def tile_list_gated_bilinear_decoder_kernel(
             )
             return codes, scales
 
-        v = [gather_words("v%d" % a, v_win[a], idx, 2 if a == KP - 1 else 1) for a in range(KP)]
+        v, a1_mx = [], []
+        for a in range(KP):
+            a1_mx.append(quantize_rows("a1_%d" % a, a1_raw[a], H))
+            v.append(gather_words("v%d" % a, v_win[a], idx, 2 if a == KP - 1 else 1))
+        v2_sc = held("v2_sc", [P, S], U8, tag="a1_%d_rounded" % (KP - 1))
         nc.vector.tensor_copy(v2_sc[:], v2_scale_win[:].indirect(idx2[:]))
+        v2 = [gather_words("v2_%d" % a, v2_win[a], idx2, 2 if a == CP - 1 else 1) for a in range(CP)]
 
-        def dealt(bank):
-            return bank[:].rearrange("p (m t) -> p t m", t=PACK)
+        def bank(shape):
+            return psum.tile(shape, F32, name="bank")
 
-        a1_mx = [quantize_rows("a1_%d" % a, a1_raw[a], H) for a in range(KP)]
+        def dealt(acc):
+            return acc[:].rearrange("p (m t) -> p t m", t=PACK)
 
-        q_sb = []
+        per_half = TILES // 2
+        pq_halves = [held("pq%d" % u, [P, per_half, PACK, P], F32, tag="v_win%d" % u) for u in range(2)]
+        d_halves = [held("d%d" % u, [P, per_half, PACK, P], F32, tag="a1_raw%d" % u) for u in range(2)]
+        v_planes = (v_sc, v_sc_low)
         for j in range(TILES):
             cols = slice(j * P, (j + 1) * P)
-            acc = psum.tile([P, H], F32, name="bank", bufs=6)
-            for a, plane in enumerate((v_sc, v_sc_low)):
+            q_acc = bank([P, H])
+            for a in range(KP):
                 nc.tensor.matmul_mx(
-                    out=acc[:], lhsT=token_tile(v[a], j), lhsT_scale=plane[:, cols],
+                    out=q_acc[:], lhsT=token_tile(v[a], j), lhsT_scale=v_planes[a][:, cols],
                     rhs=a2_w[:, a, :].bitcast(FP4X4), rhs_scale=a2_sc[:, a, :],
                     start=(a == 0), stop=(a == KP - 1),
                 )
             q = held("q%d" % j, [P, PACK, P], F32)
-            nc.scalar.activation(q[:], dealt(acc), COPY)
-            q_sb.append(q)
-
-        p_halves = [held("p%d" % a, [P, TILES // KP, PACK, P], F32, tag="a1_raw%d" % a) for a in range(KP)]
-        p_sb = []
-        for j in range(TILES):
-            cols = slice(j * P, (j + 1) * P)
-            acc = psum.tile([P, H], F32, name="bank", bufs=6)
+            nc.scalar.activation(q[:], dealt(q_acc), COPY)
+            p_acc = bank([P, H])
             for a, (codes, scales) in enumerate(a1_mx):
                 nc.tensor.matmul_mx(
-                    out=acc[:], lhsT=token_tile(v[a], j), lhsT_scale=v_sc[4 * a :, cols],
+                    out=p_acc[:], lhsT=token_tile(v[a], j), lhsT_scale=v_planes[a][:, cols],
                     rhs=codes[:].bitcast(FP8X4), rhs_scale=scales[:],
                     start=(a == 0), stop=(a == KP - 1),
                 )
-            u, jj = divmod(j, TILES // KP)
-            nc.scalar.activation(p_halves[u][:, jj], dealt(acc), COPY)
-            p_sb.append(p_halves[u][:, jj])
+            pq = pq_halves[j // per_half][:, j % per_half]
+            nc.scalar.activation(pq, dealt(p_acc), COPY)
+            nc.gpsimd.tensor_tensor(pq, pq, q[:], MULT)
 
-        v2 = [gather_words("v2_%d" % a, v2_win[a], idx2, 2 if a == CP - 1 else 1) for a in range(CP)]
-
-        pq_all = held("pq_all", [P, TILES, PACK, P], F32, tag="v2_win%d" % (CP - 1))
-        pq_sb = []
-        for j in range(TILES):
-            nc.vector.tensor_tensor(pq_all[:, j], p_sb[j], q_sb[j][:], MULT)
-            pq_sb.append(pq_all[:, j])
-
-        d_sb = []
-        for j in range(TILES):
+        def document_term(j):
             cols = slice(j * P, (j + 1) * P)
-            acc = psum.tile([P, H], F32, name="bank", bufs=6)
+            acc = bank([P, H])
             for a in range(CP):
                 nc.tensor.matmul_mx(
                     out=acc[:], lhsT=token_tile(v2[a], j), lhsT_scale=v2_sc[4 * (a + 1) :, cols],
                     rhs=bd_w[:, a, :].bitcast(FP8X4), rhs_scale=bd_sc[:, a, :],
                     start=(a == 0), stop=(a == CP - 1),
                 )
-            d = held("d%d" % j, [P, PACK, P], F32)
-            nc.scalar.activation(d[:], dealt(acc), COPY)
-            d_sb.append(d)
-
-        w_mx = [quantize_rows("w%d" % c, w_raw[c], W_CHUNK) for c in range(W_CHUNKS)]
+            nc.scalar.activation(d_halves[j // per_half][:, j % per_half], dealt(acc), COPY)
 
         def turned_sum(j):
-            if j < RING:
-                total = psum.tile([P, PACK, P], F32, name="bank", bufs=6)
-            else:
-                total = psum.tile([P, PACK, P], F32, name="late_sum")
+            total = bank([P, PACK, P])
             for t in range(PACK):
-                for term, first in ((pq_sb[j], True), (d_sb[j], False)):
+                for halves, first in ((d_halves, True), (pq_halves, False)):
                     nc.tensor.matmul(
-                        total[:, t, :], lhsT=term[:, t, :], rhs=ident[:],
+                        total[:, t, :], lhsT=halves[j // per_half][:, j % per_half, t, :], rhs=ident[:],
                         is_transpose=True, start=first, stop=not first,
                     )
             return total
 
-        sums = [turned_sum(j) for j in range(TILES)]
+        sums = []
+        document_term(0)
+        for j in range(TILES):
+            if j + 1 < TILES:
+                document_term(j + 1)
+            sums.append(turned_sum(j))
 
-        def gated_tiles(first_tile, count, gate):
+        gate = held("gate", [P, PACK, S], F32)
+        for t in range(PACK - 1):
+            nc.vector.tensor_copy(gate[:, t, :], g_win[t][:].indirect(idx[:]))
+
+        w_mx = [quantize_rows("w%d" % c, w_raw[c], W_CHUNK) for c in range(W_CHUNKS)]
+        staged = [held("staged%d" % c, [P, W_CHUNK // P, S], F32, tag="v2_win%d" % c) for c in range(W_CHUNKS)]
+
+        def gated_tiles(first_tile, count):
+            tokens = slice(first_tile * P, (first_tile + count) * P)
+            nc.vector.tensor_copy(
+                gate[:, PACK - 1, tokens], g_win[PACK - 1][:].indirect(entries(idx, tokens.start, count * P))
+            )
             h = held("h%d" % first_tile, [P, count * P, PACK], BF16)
             for jj in range(count):
                 j = first_tile + jj
-                total = sums[j]
-                in_gate = (j * P) % GROUP
                 nc.vector.tensor_tensor(
-                    h[:, jj * P : (jj + 1) * P, :].rearrange("p (c i) t -> p c t i", i=2),
-                    total[:].rearrange("p t (c i) -> p c t i", i=2),
-                    gate[:, :, in_gate : in_gate + P].rearrange("p t (c i) -> p c t i", i=2),
+                    h[:, jj * P : (jj + 1) * P, :].rearrange("p (c i) t -> p c t i", i=RUN),
+                    sums[j][:].rearrange("p t (c i) -> p c t i", i=RUN),
+                    gate[:, :, j * P : (j + 1) * P].rearrange("p t (c i) -> p c t i", i=RUN),
                     MULT,
                 )
             h_codes = held("h_codes%d" % first_tile, [P, count * P], U32)
@@ -253,38 +243,34 @@ def tile_list_gated_bilinear_decoder_kernel(
             )
             return h_codes, h_scales
 
-        def project(first_tile, count, h_mx, per_bank, share_with_vector):
+        def project(first_tile, count, h_mx, share_with_vector):
             h_codes, h_scales = h_mx
-            tokens = slice(first_tile * P, (first_tile + count) * P)
-            for b in range(N // P // per_bank):
-                y = psum.tile([P, per_bank, count * P], F32, name="bank", bufs=6)
-                staged = ring.tile([P, per_bank, count * P], F32, name="staged", bufs=6)
-                n_tiles = range(b * per_bank, (b + 1) * per_bank)
-                for e, n_tile in enumerate(n_tiles):
-                    codes, scales = w_mx[n_tile * P // W_CHUNK]
-                    in_chunk = (n_tile * P) % W_CHUNK
-                    chans = slice(in_chunk, in_chunk + P)
-                    nc.tensor.matmul_mx(
-                        out=y[:, e, :], lhsT=codes[:, chans].bitcast(FP8X4), lhsT_scale=scales[:, chans],
-                        rhs=h_codes[:].bitcast(FP8X4), rhs_scale=h_scales[:], start=True, stop=True,
-                    )
-                if share_with_vector and b % 2 == 1:
-                    spread = bias[:, n_tiles.start : n_tiles.stop].unsqueeze(2).to_broadcast([P, per_bank, count * P])
-                    nc.vector.tensor_tensor(staged[:], y[:], spread, ADD)
-                else:
-                    for e, n_tile in enumerate(n_tiles):
-                        nc.scalar.activation(staged[:, e, :], y[:, e, :], IDENTITY, bias=bias[:, n_tile : n_tile + 1])
-                rows = slice(n_tiles.start * P, n_tiles.stop * P)
-                nc.sync.dma_start(out=out[rows, tokens].rearrange("(e p) s -> p e s", p=P), in_=staged[:])
+            width = count * P
+            tokens = slice(first_tile * P, first_tile * P + width)
+            per_bank = min(W_CHUNK // P, K_PASS // width)
+            for c, (codes, scales) in enumerate(w_mx):
+                for first in range(0, W_CHUNK // P, per_bank):
+                    y = bank([P, per_bank, width])
+                    for e in range(per_bank):
+                        chans = slice((first + e) * P, (first + e + 1) * P)
+                        nc.tensor.matmul_mx(
+                            out=y[:, e, :], lhsT=codes[:, chans].bitcast(FP8X4), lhsT_scale=scales[:, chans],
+                            rhs=h_codes[:].bitcast(FP8X4), rhs_scale=h_scales[:], start=True, stop=True,
+                        )
+                    n_first = c * W_CHUNK // P + first
+                    if share_with_vector and c >= 1:
+                        spread = bias[:, n_first : n_first + per_bank].unsqueeze(2).to_broadcast([P, per_bank, width])
+                        nc.vector.tensor_tensor(staged[c][:, first : first + per_bank, tokens], y[:], spread, ADD)
+                    else:
+                        for e in range(per_bank):
+                            nc.scalar.activation(
+                                staged[c][:, first + e, tokens], y[:, e, :], IDENTITY,
+                                bias=bias[:, n_first + e : n_first + e + 1],
+                            )
+                rows = slice(c * W_CHUNK, (c + 1) * W_CHUNK)
+                nc.sync.dma_start(
+                    out=out[rows, tokens].rearrange("(e p) s -> p e s", p=P), in_=staged[c][:, :, tokens]
+                )
 
-        per_group = GROUP // P
-        for grp in range(GROUPS):
-            gate = held("gate%d" % grp, [P, PACK, GROUP], F32, tag="gate%d" % min(grp, GATE_BUFS - 1))
-            for t in range(PACK):
-                nc.vector.tensor_copy(gate[:, t, :], g_win[t][:].indirect(entries(idx, grp * GROUP, GROUP)))
-            if grp < GROUPS - 1:
-                project(grp * per_group, per_group, gated_tiles(grp * per_group, per_group, gate), 2, False)
-            else:
-                last = [(j, gated_tiles(j, 1, gate)) for j in range(grp * per_group, TILES)]
-                for j, h_mx in last:
-                    project(j, 1, h_mx, 3, True)
+        for first_tile, count in GROUPS:
+            project(first_tile, count, gated_tiles(first_tile, count), first_tile + count == TILES)

@@ -29,8 +29,9 @@ W_CHUNK = 256
 W_CHUNKS = N // W_CHUNK
 LIST = 16
 RUN = 4
-GROUPS = ((0, 4), (4, 2), (6, 2))
+GROUPS = ((0, 2), (2, 2), (4, 2), (6, 2))
 MOVED = 100
+PAIR = 2
 
 
 def tile_list_gated_bilinear_decoder_kernel(
@@ -60,6 +61,7 @@ def tile_list_gated_bilinear_decoder_kernel(
         w_raw = [held("w_raw%d" % c, [P, PACK, W_CHUNK], F32) for c in range(W_CHUNKS)]
         a2_w = held("a2_w", [P, KP, 2 * H], U8)
         bd_w = held("bd_w", [P, CP, H], I32)
+        bias_rows = held("bias_rows", [P, P], F32)
         bias = held("bias", [P, N // P], F32)
         ident = held("ident", [P, P], F32)
 
@@ -67,54 +69,55 @@ def tile_list_gated_bilinear_decoder_kernel(
         for plane in (v_scale_win[:], a2_sc[:], v_sc_low[:], bd_sc[:]):
             nc.vector.memset(plane.bitcast(I32), 0)
 
-        def words(src):
-            return src.rearrange("p t i -> p (t i)").bitcast(I32)
-
         def load_rows(dst, src):
             nc.sync.dma_start(out=dst[:], in_=src.rearrange("(p j) n -> p j n", j=PACK))
 
-        def load_planes(queue, plane, src):
+        def load_planes(plane, src):
             for Q in range(4):
-                queue.dma_start(
+                nc.sync.dma_start(
                     out=plane[32 * Q : 32 * Q + 4, :, :].bitcast(I32),
                     in_=src[:, 4 * Q : 4 * Q + 4, :].rearrange("a r e -> r a e").bitcast(I32),
                 )
 
         gate_rows = gT.rearrange("(p t) s -> p t s", t=PACK)
 
+        def load_words(dst, src):
+            nc.sync.dma_start(out=dst[:], in_=src.rearrange("p t i -> p (t i)").bitcast(I32))
+
         nc.sync.dma_start(idx[:], offs)
+        load_words(v_win[0], tab_words[0])
         for Q in range(4):
-            nc.scalar.dma_start(
+            nc.sync.dma_start(
                 out=v_scale_win[32 * Q : 32 * Q + 4 * KP, :].bitcast(I32),
                 in_=tab_scales[:, 4 * Q : 4 * Q + 4, :].bitcast(I32),
             )
+        load_rows(a1_raw[0], a1[0:K_PASS, :])
+        nc.sync.dma_start(idx2[:], offs2)
+        load_rows(a1_raw[1], a1[K_PASS:K, :])
+        nc.sync.dma_start(out=a2_w[:].bitcast(I32), in_=a2_words.rearrange("a p e -> p a e").bitcast(I32))
+        load_planes(a2_sc, a2_scales)
+        load_words(v_win[1], tab_words[1])
         nc.vector.tensor_copy(v_sc[:], v_scale_win[:].indirect(idx[:]))
-        for a in range(KP):
-            load_rows(a1_raw[a], a1[a * K_PASS : (a + 1) * K_PASS, :])
-            if a == 1:
-                nc.sync.dma_start(out=a2_w[:].bitcast(I32), in_=a2_words.rearrange("a p e -> p a e").bitcast(I32))
-            nc.sync.dma_start(out=v_win[a][:], in_=words(tab_words[a]))
-            if a == 0:
-                nc.sync.dma_start(idx2[:], offs2)
-        load_planes(nc.sync, a2_sc, a2_scales)
         nc.sync.dma_start(out=v_sc_low[0:MOVED, :].bitcast(I32), in_=v_sc[4 : 4 + MOVED, :].bitcast(I32))
-        for a in range(CP):
-            nc.sync.dma_start(out=v2_win[a][:], in_=words(tab2_words[a]))
-            if a == 0:
-                load_planes(nc.sync, bd_sc, bd_scales)
+        load_words(v2_win[0], tab2_words[0])
+        load_planes(bd_sc, bd_scales)
+        load_words(v2_win[1], tab2_words[1])
         nc.sync.dma_start(out=bd_w[:], in_=bd_words.rearrange("a p e i -> p a (e i)").bitcast(I32))
-        for t in range(PACK):
+        load_words(v2_win[2], tab2_words[2])
+        for t in range(PACK - 1):
             nc.sync.dma_start(out=g_win[t][:], in_=gate_rows[:, t, :])
         for c in range(W_CHUNKS):
             load_rows(w_raw[c], w[:, c * W_CHUNK : (c + 1) * W_CHUNK])
-        with nc.allow_non_contiguous_dma(reason="one bias value for each partition"):
-            nc.sync.dma_start(out=bias[:], in_=by.rearrange("(c p) -> p c", p=P))
+            if c == 0:
+                nc.sync.dma_start(out=g_win[PACK - 1][:], in_=gate_rows[:, PACK - 1, :])
 
         for Q in range(4):
             nc.gpsimd.dma_start(
                 out=v2_scale_win[32 * Q + 4 : 32 * Q + 4 + 4 * CP, :].bitcast(I32),
                 in_=tab2_scales[:, 4 * Q : 4 * Q + 4, :].bitcast(I32),
             )
+        nc.gpsimd.memset(bias_rows[:], 0.0)
+        nc.gpsimd.dma_start(out=bias_rows[0 : N // P, :], in_=by.rearrange("(c p) -> c p", p=P))
         make_identity(nc, ident[:])
 
         def entries(lst, first, count):
@@ -135,11 +138,9 @@ def tile_list_gated_bilinear_decoder_kernel(
 
         def quantize_rows(name, raw, width):
             grouped = held(name + "_rounded", [P, width, PACK], BF16)
-            nc.scalar.activation(
-                grouped[:].rearrange("p (c i) t -> p c t i", i=RUN),
-                raw[:].rearrange("p t (c i) -> p c t i", i=RUN),
-                COPY,
-            )
+            dst = grouped[:].rearrange("p (c i) t -> p c t i", i=RUN)
+            src = raw[:].rearrange("p t (c i) -> p c t i", i=RUN)
+            nc.scalar.activation(dst, src, COPY)
             codes = held(name + "_codes", [P, width], U32)
             scales = held(name + "_scales", [P, width], U8)
             nc.vector.quantize_mx(
@@ -147,11 +148,9 @@ def tile_list_gated_bilinear_decoder_kernel(
             )
             return codes, scales
 
-        v, a1_mx = [], []
-        for a in range(KP):
-            a1_mx.append(quantize_rows("a1_%d" % a, a1_raw[a], H))
-            v.append(gather_words("v%d" % a, v_win[a], idx, 2 if a == KP - 1 else 1))
-        v2_sc = held("v2_sc", [P, S], U8, tag="a1_%d_rounded" % (KP - 1))
+        v = [gather_words("v%d" % a, v_win[a], idx, 1 + 3 * a) for a in range(KP)]
+        a1_mx = [quantize_rows("a1_%d" % a, a1_raw[a], H) for a in range(KP)]
+        v2_sc = held("v2_sc", [P, S], U8, tag="a1_0_rounded")
         nc.vector.tensor_copy(v2_sc[:], v2_scale_win[:].indirect(idx2[:]))
         v2 = [gather_words("v2_%d" % a, v2_win[a], idx2, 2 if a == CP - 1 else 1) for a in range(CP)]
 
@@ -165,27 +164,37 @@ def tile_list_gated_bilinear_decoder_kernel(
         pq_halves = [held("pq%d" % u, [P, per_half, PACK, P], F32, tag="v_win%d" % u) for u in range(2)]
         d_halves = [held("d%d" % u, [P, per_half, PACK, P], F32, tag="a1_raw%d" % u) for u in range(2)]
         v_planes = (v_sc, v_sc_low)
+        a2_mx = [(a2_w[:, a, :].bitcast(FP4X4), a2_sc[:, a, :]) for a in range(KP)]
+        a1_ops = [(codes[:].bitcast(FP8X4), scales[:]) for codes, scales in a1_mx]
+
+        def token_pass(acc, weight, j, a):
+            codes, scales = weight[a]
+            nc.tensor.matmul_mx(
+                out=acc[:], lhsT=token_tile(v[a], j), lhsT_scale=v_planes[a][:, j * P : (j + 1) * P],
+                rhs=codes, rhs_scale=scales, start=(a == 0), stop=(a == KP - 1),
+            )
+
+        def opened(weight, j):
+            acc = bank([P, H])
+            token_pass(acc, weight, j, 0)
+            return acc
+
+        p_open = [opened(a1_ops, j) for j in range(per_half)]
+        q_open = [opened(a2_mx, j) for j in range(per_half)]
         for j in range(TILES):
-            cols = slice(j * P, (j + 1) * P)
-            q_acc = bank([P, H])
-            for a in range(KP):
-                nc.tensor.matmul_mx(
-                    out=q_acc[:], lhsT=token_tile(v[a], j), lhsT_scale=v_planes[a][:, cols],
-                    rhs=a2_w[:, a, :].bitcast(FP4X4), rhs_scale=a2_sc[:, a, :],
-                    start=(a == 0), stop=(a == KP - 1),
-                )
-            q = held("q%d" % j, [P, PACK, P], F32)
-            nc.scalar.activation(q[:], dealt(q_acc), COPY)
-            p_acc = bank([P, H])
-            for a, (codes, scales) in enumerate(a1_mx):
-                nc.tensor.matmul_mx(
-                    out=p_acc[:], lhsT=token_tile(v[a], j), lhsT_scale=v_planes[a][:, cols],
-                    rhs=codes[:].bitcast(FP8X4), rhs_scale=scales[:],
-                    start=(a == 0), stop=(a == KP - 1),
-                )
+            acc = p_open[j] if j < per_half else opened(a1_ops, j)
+            token_pass(acc, a1_ops, j, 1)
             pq = pq_halves[j // per_half][:, j % per_half]
-            nc.scalar.activation(pq, dealt(p_acc), COPY)
+            nc.scalar.activation(pq, dealt(acc), COPY)
+            acc = q_open[j] if j < per_half else opened(a2_mx, j)
+            token_pass(acc, a2_mx, j, 1)
+            q = held("q%d" % j, [P, PACK, P], F32)
+            nc.scalar.activation(q[:], dealt(acc), COPY)
             nc.gpsimd.tensor_tensor(pq, pq, q[:], MULT)
+
+        turned_bias = bank([P, P])
+        nc.tensor.transpose(turned_bias[:], bias_rows[:], ident[:])
+        nc.scalar.activation(bias[:], turned_bias[:, 0 : N // P], COPY)
 
         def document_term(j):
             cols = slice(j * P, (j + 1) * P)
@@ -208,19 +217,15 @@ def tile_list_gated_bilinear_decoder_kernel(
                     )
             return total
 
-        sums = []
-        document_term(0)
         for j in range(TILES):
-            if j + 1 < TILES:
-                document_term(j + 1)
-            sums.append(turned_sum(j))
+            document_term(j)
+        sums = [turned_sum(j) for j in range(TILES - PAIR)]
 
         gate = held("gate", [P, PACK, S], F32)
         for t in range(PACK - 1):
             nc.vector.tensor_copy(gate[:, t, :], g_win[t][:].indirect(idx[:]))
 
         w_mx = [quantize_rows("w%d" % c, w_raw[c], W_CHUNK) for c in range(W_CHUNKS)]
-        staged = [held("staged%d" % c, [P, W_CHUNK // P, S], F32, tag="v2_win%d" % c) for c in range(W_CHUNKS)]
 
         def gated_tiles(first_tile, count):
             tokens = slice(first_tile * P, (first_tile + count) * P)
@@ -243,34 +248,35 @@ def tile_list_gated_bilinear_decoder_kernel(
             )
             return h_codes, h_scales
 
+        spent = ["q%d" % j for j in range(TILES)] + ["v_scale_win", "v2_scale_win", "a1_1_rounded", "v2_win0"]
+
         def project(first_tile, count, h_mx, share_with_vector):
             h_codes, h_scales = h_mx
             width = count * P
             tokens = slice(first_tile * P, first_tile * P + width)
-            per_bank = min(W_CHUNK // P, K_PASS // width)
+            per_bank = W_CHUNK // P
             for c, (codes, scales) in enumerate(w_mx):
-                for first in range(0, W_CHUNK // P, per_bank):
-                    y = bank([P, per_bank, width])
+                y = bank([P, per_bank, width])
+                staged = held("staged%d_%d" % (first_tile, c), [P, per_bank, width], F32, tag=spent[first_tile // count * W_CHUNKS + c])
+                for e in range(per_bank):
+                    chans = slice(e * P, (e + 1) * P)
+                    nc.tensor.matmul_mx(
+                        out=y[:, e, :], lhsT=codes[:, chans].bitcast(FP8X4), lhsT_scale=scales[:, chans],
+                        rhs=h_codes[:].bitcast(FP8X4), rhs_scale=h_scales[:], start=True, stop=True,
+                    )
+                n_first = c * per_bank
+                if share_with_vector and c >= 1:
+                    spread = bias[:, n_first : n_first + per_bank].unsqueeze(2).to_broadcast([P, per_bank, width])
+                    nc.vector.tensor_tensor(staged[:], y[:], spread, ADD)
+                else:
                     for e in range(per_bank):
-                        chans = slice((first + e) * P, (first + e + 1) * P)
-                        nc.tensor.matmul_mx(
-                            out=y[:, e, :], lhsT=codes[:, chans].bitcast(FP8X4), lhsT_scale=scales[:, chans],
-                            rhs=h_codes[:].bitcast(FP8X4), rhs_scale=h_scales[:], start=True, stop=True,
+                        nc.scalar.activation(
+                            staged[:, e, :], y[:, e, :], IDENTITY, bias=bias[:, n_first + e : n_first + e + 1]
                         )
-                    n_first = c * W_CHUNK // P + first
-                    if share_with_vector and c >= 1:
-                        spread = bias[:, n_first : n_first + per_bank].unsqueeze(2).to_broadcast([P, per_bank, width])
-                        nc.vector.tensor_tensor(staged[c][:, first : first + per_bank, tokens], y[:], spread, ADD)
-                    else:
-                        for e in range(per_bank):
-                            nc.scalar.activation(
-                                staged[c][:, first + e, tokens], y[:, e, :], IDENTITY,
-                                bias=bias[:, n_first + e : n_first + e + 1],
-                            )
                 rows = slice(c * W_CHUNK, (c + 1) * W_CHUNK)
-                nc.sync.dma_start(
-                    out=out[rows, tokens].rearrange("(e p) s -> p e s", p=P), in_=staged[c][:, :, tokens]
-                )
+                nc.sync.dma_start(out=out[rows, tokens].rearrange("(e p) s -> p e s", p=P), in_=staged[:])
 
         for first_tile, count in GROUPS:
             project(first_tile, count, gated_tiles(first_tile, count), first_tile + count == TILES)
+            if first_tile == 0:
+                sums.extend([turned_sum(j) for j in range(TILES - PAIR, TILES)])

@@ -29,7 +29,8 @@ W_CHUNK = 256
 W_CHUNKS = N // W_CHUNK
 LIST = 16
 RUN = 4
-GROUPS = ((0, 2), (2, 2), (4, 2), (6, 2))
+GROUP = 256
+GROUPS = S // GROUP
 MOVED = 100
 PAIR = 2
 
@@ -58,7 +59,8 @@ def tile_list_gated_bilinear_decoder_kernel(
         v2_win = [held("v2_win%d" % a, [P, T], I32) for a in range(CP)]
         g_win = [held("g_win%d" % t, [P, T], F32) for t in range(PACK)]
         a1_raw = [held("a1_raw%d" % a, [P, PACK, H], F32) for a in range(KP)]
-        w_raw = [held("w_raw%d" % c, [P, PACK, W_CHUNK], F32) for c in range(W_CHUNKS)]
+        w_first = held("w_first", [P, PACK, W_CHUNK], F32)
+        w_rest = held("w_rest", [P, PACK, N - W_CHUNK], F32)
         a2_w = held("a2_w", [P, KP, 2 * H], U8)
         bd_w = held("bd_w", [P, CP, H], I32)
         bias_rows = held("bias_rows", [P, P], F32)
@@ -104,12 +106,11 @@ def tile_list_gated_bilinear_decoder_kernel(
         load_words(v2_win[1], tab2_words[1])
         nc.sync.dma_start(out=bd_w[:], in_=bd_words.rearrange("a p e i -> p a (e i)").bitcast(I32))
         load_words(v2_win[2], tab2_words[2])
-        for t in range(PACK - 1):
+        for t in range(PACK):
             nc.sync.dma_start(out=g_win[t][:], in_=gate_rows[:, t, :])
-        for c in range(W_CHUNKS):
-            load_rows(w_raw[c], w[:, c * W_CHUNK : (c + 1) * W_CHUNK])
-            if c == 0:
-                nc.sync.dma_start(out=g_win[PACK - 1][:], in_=gate_rows[:, PACK - 1, :])
+        load_rows(w_first, w[:, 0:W_CHUNK])
+        load_rows(w_rest, w[:, W_CHUNK:N])
+        w_raw = [w_first[:]] + [w_rest[:, :, c * W_CHUNK : (c + 1) * W_CHUNK] for c in range(W_CHUNKS - 1)]
 
         for Q in range(4):
             nc.gpsimd.dma_start(
@@ -139,7 +140,7 @@ def tile_list_gated_bilinear_decoder_kernel(
         def quantize_rows(name, raw, width):
             grouped = held(name + "_rounded", [P, width, PACK], BF16)
             dst = grouped[:].rearrange("p (c i) t -> p c t i", i=RUN)
-            src = raw[:].rearrange("p t (c i) -> p c t i", i=RUN)
+            src = raw.rearrange("p t (c i) -> p c t i", i=RUN)
             nc.scalar.activation(dst, src, COPY)
             codes = held(name + "_codes", [P, width], U32)
             scales = held(name + "_scales", [P, width], U8)
@@ -149,7 +150,7 @@ def tile_list_gated_bilinear_decoder_kernel(
             return codes, scales
 
         v = [gather_words("v%d" % a, v_win[a], idx, 1 + 3 * a) for a in range(KP)]
-        a1_mx = [quantize_rows("a1_%d" % a, a1_raw[a], H) for a in range(KP)]
+        a1_mx = [quantize_rows("a1_%d" % a, a1_raw[a][:], H) for a in range(KP)]
         v2_sc = held("v2_sc", [P, S], U8, tag="a1_0_rounded")
         nc.vector.tensor_copy(v2_sc[:], v2_scale_win[:].indirect(idx2[:]))
         v2 = [gather_words("v2_%d" % a, v2_win[a], idx2, 2 if a == CP - 1 else 1) for a in range(CP)]
@@ -217,15 +218,18 @@ def tile_list_gated_bilinear_decoder_kernel(
                     )
             return total
 
-        for j in range(TILES):
-            document_term(j)
-        sums = [turned_sum(j) for j in range(TILES - PAIR)]
+        sums = []
+        for first in range(0, TILES, PAIR):
+            for j in range(first, first + PAIR):
+                document_term(j)
+            for j in range(max(first - PAIR, 0), first):
+                sums.append(turned_sum(j))
+        for j in range(TILES - PAIR, TILES):
+            sums.append(turned_sum(j))
 
         gate = held("gate", [P, PACK, S], F32)
         for t in range(PACK - 1):
             nc.vector.tensor_copy(gate[:, t, :], g_win[t][:].indirect(idx[:]))
-
-        w_mx = [quantize_rows("w%d" % c, w_raw[c], W_CHUNK) for c in range(W_CHUNKS)]
 
         def gated_tiles(first_tile, count):
             tokens = slice(first_tile * P, (first_tile + count) * P)
@@ -250,33 +254,37 @@ def tile_list_gated_bilinear_decoder_kernel(
 
         spent = ["q%d" % j for j in range(TILES)] + ["v_scale_win", "v2_scale_win", "a1_1_rounded", "v2_win0"]
 
-        def project(first_tile, count, h_mx, share_with_vector):
-            h_codes, h_scales = h_mx
-            width = count * P
-            tokens = slice(first_tile * P, first_tile * P + width)
+        def project(grp, c):
+            h_codes, h_scales = h_mx[grp]
+            codes, scales = w_mx[c]
+            tokens = slice(grp * GROUP, (grp + 1) * GROUP)
             per_bank = W_CHUNK // P
-            for c, (codes, scales) in enumerate(w_mx):
-                y = bank([P, per_bank, width])
-                staged = held("staged%d_%d" % (first_tile, c), [P, per_bank, width], F32, tag=spent[first_tile // count * W_CHUNKS + c])
+            y = bank([P, per_bank, GROUP])
+            staged = held("staged%d_%d" % (grp, c), [P, per_bank, GROUP], F32, tag=spent[grp * W_CHUNKS + c])
+            for e in range(per_bank):
+                chans = slice(e * P, (e + 1) * P)
+                nc.tensor.matmul_mx(
+                    out=y[:, e, :], lhsT=codes[:, chans].bitcast(FP8X4), lhsT_scale=scales[:, chans],
+                    rhs=h_codes[:].bitcast(FP8X4), rhs_scale=h_scales[:], start=True, stop=True,
+                )
+            n_first = c * per_bank
+            if grp == GROUPS - 1:
+                spread = bias[:, n_first : n_first + per_bank].unsqueeze(2).to_broadcast([P, per_bank, GROUP])
+                nc.vector.tensor_tensor(staged[:], y[:], spread, ADD)
+            else:
                 for e in range(per_bank):
-                    chans = slice(e * P, (e + 1) * P)
-                    nc.tensor.matmul_mx(
-                        out=y[:, e, :], lhsT=codes[:, chans].bitcast(FP8X4), lhsT_scale=scales[:, chans],
-                        rhs=h_codes[:].bitcast(FP8X4), rhs_scale=h_scales[:], start=True, stop=True,
+                    nc.scalar.activation(
+                        staged[:, e, :], y[:, e, :], IDENTITY, bias=bias[:, n_first + e : n_first + e + 1]
                     )
-                n_first = c * per_bank
-                if share_with_vector and c >= 1:
-                    spread = bias[:, n_first : n_first + per_bank].unsqueeze(2).to_broadcast([P, per_bank, width])
-                    nc.vector.tensor_tensor(staged[:], y[:], spread, ADD)
-                else:
-                    for e in range(per_bank):
-                        nc.scalar.activation(
-                            staged[:, e, :], y[:, e, :], IDENTITY, bias=bias[:, n_first + e : n_first + e + 1]
-                        )
-                rows = slice(c * W_CHUNK, (c + 1) * W_CHUNK)
-                nc.sync.dma_start(out=out[rows, tokens].rearrange("(e p) s -> p e s", p=P), in_=staged[:])
+            rows = slice(c * W_CHUNK, (c + 1) * W_CHUNK)
+            nc.sync.dma_start(out=out[rows, tokens].rearrange("(e p) s -> p e s", p=P), in_=staged[:])
 
-        for first_tile, count in GROUPS:
-            project(first_tile, count, gated_tiles(first_tile, count), first_tile + count == TILES)
-            if first_tile == 0:
-                sums.extend([turned_sum(j) for j in range(TILES - PAIR, TILES)])
+        h_mx, w_mx = [], []
+        for step in range(GROUPS):
+            h_mx.append(gated_tiles(step * PAIR, PAIR))
+            for c in range(len(w_mx)):
+                project(step, c)
+            if step < W_CHUNKS:
+                w_mx.append(quantize_rows("w%d" % step, w_raw[step], W_CHUNK))
+                for grp in range(step + 1):
+                    project(grp, step)

@@ -70,13 +70,14 @@ def tile_list_gated_bilinear_decoder_kernel(
         nc.gpsimd.memset(v2_scale_win[:].bitcast(I32), 0)
         for plane in (v_scale_win[:], a2_sc[:], v_sc_low[:], bd_sc[:]):
             nc.vector.memset(plane.bitcast(I32), 0)
+        nc.vector.memset(bias_rows[:], 0.0)
 
         def load_rows(dst, src):
             nc.sync.dma_start(out=dst[:], in_=src.rearrange("(p j) n -> p j n", j=PACK))
 
         def load_planes(plane, src):
             for Q in range(4):
-                nc.sync.dma_start(
+                nc.gpsimd.dma_start(
                     out=plane[32 * Q : 32 * Q + 4, :, :].bitcast(I32),
                     in_=src[:, 4 * Q : 4 * Q + 4, :].rearrange("a r e -> r a e").bitcast(I32),
                 )
@@ -97,12 +98,10 @@ def tile_list_gated_bilinear_decoder_kernel(
         nc.sync.dma_start(idx2[:], offs2)
         load_rows(a1_raw[1], a1[K_PASS:K, :])
         nc.sync.dma_start(out=a2_w[:].bitcast(I32), in_=a2_words.rearrange("a p e -> p a e").bitcast(I32))
-        load_planes(a2_sc, a2_scales)
         load_words(v_win[1], tab_words[1])
         nc.vector.tensor_copy(v_sc[:], v_scale_win[:].indirect(idx[:]))
         nc.sync.dma_start(out=v_sc_low[0:MOVED, :].bitcast(I32), in_=v_sc[4 : 4 + MOVED, :].bitcast(I32))
         load_words(v2_win[0], tab2_words[0])
-        load_planes(bd_sc, bd_scales)
         load_words(v2_win[1], tab2_words[1])
         nc.sync.dma_start(out=bd_w[:], in_=bd_words.rearrange("a p e i -> p a (e i)").bitcast(I32))
         load_words(v2_win[2], tab2_words[2])
@@ -117,7 +116,8 @@ def tile_list_gated_bilinear_decoder_kernel(
                 out=v2_scale_win[32 * Q + 4 : 32 * Q + 4 + 4 * CP, :].bitcast(I32),
                 in_=tab2_scales[:, 4 * Q : 4 * Q + 4, :].bitcast(I32),
             )
-        nc.gpsimd.memset(bias_rows[:], 0.0)
+        load_planes(a2_sc, a2_scales)
+        load_planes(bd_sc, bd_scales)
         nc.gpsimd.dma_start(out=bias_rows[0 : N // P, :], in_=by.rearrange("(c p) -> c p", p=P))
         make_identity(nc, ident[:])
 

@@ -59,8 +59,7 @@ def tile_list_gated_bilinear_decoder_kernel(
         v2_win = [held("v2_win%d" % a, [P, T], I32) for a in range(CP)]
         g_win = [held("g_win%d" % t, [P, T], F32) for t in range(PACK)]
         a1_raw = [held("a1_raw%d" % a, [P, PACK, H], F32) for a in range(KP)]
-        w_first = held("w_first", [P, PACK, W_CHUNK], F32)
-        w_rest = held("w_rest", [P, PACK, N - W_CHUNK], F32)
+        w_raw = [held("w_raw%d" % c, [P, PACK, W_CHUNK], F32) for c in range(W_CHUNKS)]
         a2_w = held("a2_w", [P, KP, 2 * H], U8)
         bd_w = held("bd_w", [P, CP, H], I32)
         bias_rows = held("bias_rows", [P, P], F32)
@@ -107,9 +106,8 @@ def tile_list_gated_bilinear_decoder_kernel(
         load_words(v2_win[2], tab2_words[2])
         for t in range(PACK):
             nc.sync.dma_start(out=g_win[t][:], in_=gate_rows[:, t, :])
-        load_rows(w_first, w[:, 0:W_CHUNK])
-        load_rows(w_rest, w[:, W_CHUNK:N])
-        w_raw = [w_first[:]] + [w_rest[:, :, c * W_CHUNK : (c + 1) * W_CHUNK] for c in range(W_CHUNKS - 1)]
+        for c in range(W_CHUNKS):
+            load_rows(w_raw[c], w[:, c * W_CHUNK : (c + 1) * W_CHUNK])
 
         for Q in range(4):
             nc.gpsimd.dma_start(
@@ -285,6 +283,6 @@ def tile_list_gated_bilinear_decoder_kernel(
             for c in range(len(w_mx)):
                 project(step, c)
             if step < W_CHUNKS:
-                w_mx.append(quantize_rows("w%d" % step, w_raw[step], W_CHUNK))
+                w_mx.append(quantize_rows("w%d" % step, w_raw[step][:], W_CHUNK))
                 for grp in range(step + 1):
                     project(grp, step)

@@ -42,7 +42,7 @@ def tile_list_gated_bilinear_decoder_kernel(
     nc = tc.nc
     with ExitStack() as ctx:
         keep = ctx.enter_context(tc.tile_pool(name="keep", bufs=1))
-        psum = ctx.enter_context(tc.psum_pool(name="psum", bufs=8))
+        psum = ctx.enter_context(tc.psum_pool(name="psum", bufs=1))
 
         def held(name, shape, dtype, tag=""):
             return keep.tile(shape, dtype, name=name, tag=tag or name, align_bytes=64)
@@ -66,10 +66,10 @@ def tile_list_gated_bilinear_decoder_kernel(
         bias = held("bias", [P, N // P], F32)
         ident = held("ident", [P, P], F32)
 
+        nc.gpsimd.memset(bias_rows[:], 0.0)
         nc.gpsimd.memset(v2_scale_win[:].bitcast(I32), 0)
         for plane in (v_scale_win[:], a2_sc[:], v_sc_low[:], bd_sc[:]):
             nc.vector.memset(plane.bitcast(I32), 0)
-        nc.vector.memset(bias_rows[:], 0.0)
 
         def load_rows(dst, src):
             nc.sync.dma_start(out=dst[:], in_=src.rearrange("(p j) n -> p j n", j=PACK))
@@ -109,15 +109,15 @@ def tile_list_gated_bilinear_decoder_kernel(
         for c in range(W_CHUNKS):
             load_rows(w_raw[c], w[:, c * W_CHUNK : (c + 1) * W_CHUNK])
 
+        nc.gpsimd.dma_start(out=bias_rows[0 : N // P, :], in_=by.rearrange("(c p) -> c p", p=P))
         for Q in range(4):
             nc.gpsimd.dma_start(
                 out=v2_scale_win[32 * Q + 4 : 32 * Q + 4 + 4 * CP, :].bitcast(I32),
                 in_=tab2_scales[:, 4 * Q : 4 * Q + 4, :].bitcast(I32),
             )
+        make_identity(nc, ident[:])
         load_planes(a2_sc, a2_scales)
         load_planes(bd_sc, bd_scales)
-        nc.gpsimd.dma_start(out=bias_rows[0 : N // P, :], in_=by.rearrange("(c p) -> c p", p=P))
-        make_identity(nc, ident[:])
 
         def entries(lst, first, count):
             return lst[:, first // LIST : (first + count) // LIST]
@@ -135,11 +135,14 @@ def tile_list_gated_bilinear_decoder_kernel(
             u, first = divmod(j * P, S // len(parts))
             return parts[u][:, first : first + P].bitcast(FP8X4)
 
-        def quantize_rows(name, raw, width):
+        def quantize_rows(name, raw, width, engine_copy=None):
             grouped = held(name + "_rounded", [P, width, PACK], BF16)
             dst = grouped[:].rearrange("p (c i) t -> p c t i", i=RUN)
             src = raw.rearrange("p t (c i) -> p c t i", i=RUN)
-            nc.scalar.activation(dst, src, COPY)
+            if engine_copy:
+                engine_copy(dst, src)
+            else:
+                nc.scalar.activation(dst, src, COPY)
             codes = held(name + "_codes", [P, width], U32)
             scales = held(name + "_scales", [P, width], U8)
             nc.vector.quantize_mx(
@@ -147,14 +150,15 @@ def tile_list_gated_bilinear_decoder_kernel(
             )
             return codes, scales
 
-        v = [gather_words("v%d" % a, v_win[a], idx, 1 + 3 * a) for a in range(KP)]
-        a1_mx = [quantize_rows("a1_%d" % a, a1_raw[a][:], H) for a in range(KP)]
-        v2_sc = held("v2_sc", [P, S], U8, tag="a1_0_rounded")
+        v = [gather_words("v0", v_win[0], idx, 1)]
+        v2_sc = held("v2_sc", [P, S], U8, tag="v_scale_win")
         nc.vector.tensor_copy(v2_sc[:], v2_scale_win[:].indirect(idx2[:]))
+        a1_mx = [quantize_rows("a1_%d" % a, a1_raw[a][:], H) for a in range(KP)]
+        v.append(gather_words("v1", v_win[1], idx, 4))
         v2 = [gather_words("v2_%d" % a, v2_win[a], idx2, 2 if a == CP - 1 else 1) for a in range(CP)]
 
-        def bank(shape):
-            return psum.tile(shape, F32, name="bank")
+        def bank(shape, b):
+            return psum.tile(shape, F32, name="bank%d" % b)
 
         def dealt(acc):
             return acc[:].rearrange("p (m t) -> p t m", t=PACK)
@@ -173,31 +177,32 @@ def tile_list_gated_bilinear_decoder_kernel(
                 rhs=codes, rhs_scale=scales, start=(a == 0), stop=(a == KP - 1),
             )
 
-        def opened(weight, j):
-            acc = bank([P, H])
+        def opened(weight, j, b):
+            acc = bank([P, H], b)
             token_pass(acc, weight, j, 0)
             return acc
 
-        p_open = [opened(a1_ops, j) for j in range(per_half)]
-        q_open = [opened(a2_mx, j) for j in range(per_half)]
+        turned_bias = bank([P, P], TILES - 1)
+        nc.tensor.transpose(turned_bias[:], bias_rows[:], ident[:])
+        nc.scalar.activation(bias[:], turned_bias[:, 0 : N // P], COPY)
+
+        p_open = [opened(a1_ops, j, 2 * j) for j in range(per_half)]
+        q_open = [opened(a2_mx, j, 2 * j + 1) for j in range(per_half)]
         for j in range(TILES):
-            acc = p_open[j] if j < per_half else opened(a1_ops, j)
+            acc = p_open[j] if j < per_half else opened(a1_ops, j, 2 * (j - per_half))
             token_pass(acc, a1_ops, j, 1)
             pq = pq_halves[j // per_half][:, j % per_half]
             nc.scalar.activation(pq, dealt(acc), COPY)
-            acc = q_open[j] if j < per_half else opened(a2_mx, j)
+            acc = q_open[j] if j < per_half else opened(a2_mx, j, 2 * (j - per_half) + 1)
             token_pass(acc, a2_mx, j, 1)
             q = held("q%d" % j, [P, PACK, P], F32)
             nc.scalar.activation(q[:], dealt(acc), COPY)
             nc.gpsimd.tensor_tensor(pq, pq, q[:], MULT)
 
-        turned_bias = bank([P, P])
-        nc.tensor.transpose(turned_bias[:], bias_rows[:], ident[:])
-        nc.scalar.activation(bias[:], turned_bias[:, 0 : N // P], COPY)
 
         def document_term(j):
             cols = slice(j * P, (j + 1) * P)
-            acc = bank([P, H])
+            acc = bank([P, H], j)
             for a in range(CP):
                 nc.tensor.matmul_mx(
                     out=acc[:], lhsT=token_tile(v2[a], j), lhsT_scale=v2_sc[4 * (a + 1) :, cols],
@@ -207,7 +212,7 @@ def tile_list_gated_bilinear_decoder_kernel(
             nc.scalar.activation(d_halves[j // per_half][:, j % per_half], dealt(acc), COPY)
 
         def turned_sum(j):
-            total = bank([P, PACK, P])
+            total = bank([P, PACK, P], j)
             for t in range(PACK):
                 for halves, first in ((d_halves, True), (pq_halves, False)):
                     nc.tensor.matmul(
@@ -216,14 +221,9 @@ def tile_list_gated_bilinear_decoder_kernel(
                     )
             return total
 
-        sums = []
-        for first in range(0, TILES, PAIR):
-            for j in range(first, first + PAIR):
-                document_term(j)
-            for j in range(max(first - PAIR, 0), first):
-                sums.append(turned_sum(j))
-        for j in range(TILES - PAIR, TILES):
-            sums.append(turned_sum(j))
+        for j in range(TILES):
+            document_term(j)
+        sums = [turned_sum(j) for j in range(TILES)]
 
         gate = held("gate", [P, PACK, S], F32)
         for t in range(PACK - 1):
@@ -250,14 +250,15 @@ def tile_list_gated_bilinear_decoder_kernel(
             )
             return h_codes, h_scales
 
-        spent = ["q%d" % j for j in range(TILES)] + ["v_scale_win", "v2_scale_win", "a1_1_rounded", "v2_win0"]
+        spent = ["q%d" % j for j in range(TILES)] + ["a1_0_rounded", "v2_scale_win", "a1_1_rounded", "v2_win0"]
 
         def project(grp, c):
             h_codes, h_scales = h_mx[grp]
             codes, scales = w_mx[c]
             tokens = slice(grp * GROUP, (grp + 1) * GROUP)
             per_bank = W_CHUNK // P
-            y = bank([P, per_bank, GROUP])
+            b = free.pop(0)
+            y = bank([P, per_bank, GROUP], b)
             staged = held("staged%d_%d" % (grp, c), [P, per_bank, GROUP], F32, tag=spent[grp * W_CHUNKS + c])
             for e in range(per_bank):
                 chans = slice(e * P, (e + 1) * P)
@@ -266,7 +267,7 @@ def tile_list_gated_bilinear_decoder_kernel(
                     rhs=h_codes[:].bitcast(FP8X4), rhs_scale=h_scales[:], start=True, stop=True,
                 )
             n_first = c * per_bank
-            if grp == GROUPS - 1:
+            if grp == GROUPS - 1 and c != 1:
                 spread = bias[:, n_first : n_first + per_bank].unsqueeze(2).to_broadcast([P, per_bank, GROUP])
                 nc.vector.tensor_tensor(staged[:], y[:], spread, ADD)
             else:
@@ -276,13 +277,28 @@ def tile_list_gated_bilinear_decoder_kernel(
                     )
             rows = slice(c * W_CHUNK, (c + 1) * W_CHUNK)
             nc.sync.dma_start(out=out[rows, tokens].rearrange("(e p) s -> p e s", p=P), in_=staged[:])
+            free.append(b)
 
-        h_mx, w_mx = [], []
-        for step in range(GROUPS):
-            h_mx.append(gated_tiles(step * PAIR, PAIR))
+        h_mx, w_mx, free = [], [], []
+
+
+        def next_group():
+            grp = len(h_mx)
+            h_mx.append(gated_tiles(grp * PAIR, PAIR))
+            free[0:0] = range(grp * PAIR, (grp + 1) * PAIR)
             for c in range(len(w_mx)):
-                project(step, c)
-            if step < W_CHUNKS:
-                w_mx.append(quantize_rows("w%d" % step, w_raw[step][:], W_CHUNK))
-                for grp in range(step + 1):
-                    project(grp, step)
+                project(grp, c)
+
+        def next_chunk(engine_copy):
+            c = len(w_mx)
+            w_mx.append(quantize_rows("w%d" % c, w_raw[c][:], W_CHUNK, engine_copy))
+            for grp in range(len(h_mx)):
+                project(grp, c)
+
+        next_group()
+        next_chunk(None)
+        next_chunk(None)
+        next_group()
+        next_chunk(nc.vector.tensor_copy)
+        next_group()
+        next_group()

@@ -66,8 +66,8 @@ def tile_list_gated_bilinear_decoder_kernel(
         bias = held("bias", [P, N // P], F32)
         ident = held("ident", [P, P], F32)
 
-        nc.gpsimd.memset(bias_rows[:], 0.0)
         nc.gpsimd.memset(v2_scale_win[:].bitcast(I32), 0)
+        nc.vector.memset(bias_rows[:], 0.0)
         for plane in (v_scale_win[:], a2_sc[:], v_sc_low[:], bd_sc[:]):
             nc.vector.memset(plane.bitcast(I32), 0)
 
@@ -109,15 +109,15 @@ def tile_list_gated_bilinear_decoder_kernel(
         for c in range(W_CHUNKS):
             load_rows(w_raw[c], w[:, c * W_CHUNK : (c + 1) * W_CHUNK])
 
-        nc.gpsimd.dma_start(out=bias_rows[0 : N // P, :], in_=by.rearrange("(c p) -> c p", p=P))
         for Q in range(4):
             nc.gpsimd.dma_start(
                 out=v2_scale_win[32 * Q + 4 : 32 * Q + 4 + 4 * CP, :].bitcast(I32),
                 in_=tab2_scales[:, 4 * Q : 4 * Q + 4, :].bitcast(I32),
             )
-        make_identity(nc, ident[:])
         load_planes(a2_sc, a2_scales)
         load_planes(bd_sc, bd_scales)
+        nc.gpsimd.dma_start(out=bias_rows[0 : N // P, :], in_=by.rearrange("(c p) -> c p", p=P))
+        make_identity(nc, ident[:])
 
         def entries(lst, first, count):
             return lst[:, first // LIST : (first + count) // LIST]
@@ -182,10 +182,6 @@ def tile_list_gated_bilinear_decoder_kernel(
             token_pass(acc, weight, j, 0)
             return acc
 
-        turned_bias = bank([P, P], TILES - 1)
-        nc.tensor.transpose(turned_bias[:], bias_rows[:], ident[:])
-        nc.scalar.activation(bias[:], turned_bias[:, 0 : N // P], COPY)
-
         p_open = [opened(a1_ops, j, 2 * j) for j in range(per_half)]
         q_open = [opened(a2_mx, j, 2 * j + 1) for j in range(per_half)]
         for j in range(TILES):
@@ -199,6 +195,10 @@ def tile_list_gated_bilinear_decoder_kernel(
             nc.scalar.activation(q[:], dealt(acc), COPY)
             nc.gpsimd.tensor_tensor(pq, pq, q[:], MULT)
 
+
+        turned_bias = bank([P, P], TILES - 1)
+        nc.tensor.transpose(turned_bias[:], bias_rows[:], ident[:])
+        nc.scalar.activation(bias[:], turned_bias[:, 0 : N // P], COPY)
 
         def document_term(j):
             cols = slice(j * P, (j + 1) * P)

@@ -52,7 +52,7 @@ def tile_list_gated_bilinear_decoder_kernel(
         v_scale_win = held("v_scale_win", [P, T], U8)
         v2_scale_win = held("v2_scale_win", [P, T], U8)
         a2_sc = held("a2_sc", [P, KP, H], U8)
-        bd_sc = held("bd_sc", [P, CP, H], U8)
+        bd_sc = held("bd_sc", [P, H], U8)
         v_sc = held("v_sc", [P, S], U8)
         v_sc_low = held("v_sc_low", [P, S], U8)
         v_win = [held("v_win%d" % a, [P, T], I32) for a in range(KP)]
@@ -115,7 +115,11 @@ def tile_list_gated_bilinear_decoder_kernel(
                 in_=tab2_scales[:, 4 * Q : 4 * Q + 4, :].bitcast(I32),
             )
         load_planes(a2_sc, a2_scales)
-        load_planes(bd_sc, bd_scales)
+        for Q in range(4):
+            nc.gpsimd.dma_start(
+                out=bd_sc[32 * Q + 4 : 32 * Q + 4 + 4 * CP, :].bitcast(I32),
+                in_=bd_scales[:, 4 * Q : 4 * Q + 4, :].bitcast(I32),
+            )
         nc.gpsimd.dma_start(out=bias_rows[0 : N // P, :], in_=by.rearrange("(c p) -> c p", p=P))
         make_identity(nc, ident[:])
 
@@ -206,7 +210,7 @@ def tile_list_gated_bilinear_decoder_kernel(
             for a in range(CP):
                 nc.tensor.matmul_mx(
                     out=acc[:], lhsT=token_tile(v2[a], j), lhsT_scale=v2_sc[4 * (a + 1) :, cols],
-                    rhs=bd_w[:, a, :].bitcast(FP8X4), rhs_scale=bd_sc[:, a, :],
+                    rhs=bd_w[:, a, :].bitcast(FP8X4), rhs_scale=bd_sc[4 * (a + 1) :, :],
                     start=(a == 0), stop=(a == CP - 1),
                 )
             nc.scalar.activation(d_halves[j // per_half][:, j % per_half], dealt(acc), COPY)

@@ -200,13 +200,9 @@ def tile_list_gated_bilinear_decoder_kernel(
             nc.gpsimd.tensor_tensor(pq, pq, q[:], MULT)
 
 
-        turned_bias = bank([P, P], TILES - 1)
-        nc.tensor.transpose(turned_bias[:], bias_rows[:], ident[:])
-        nc.scalar.activation(bias[:], turned_bias[:, 0 : N // P], COPY)
-
         def document_term(j):
             cols = slice(j * P, (j + 1) * P)
-            acc = bank([P, H], j)
+            acc = bank([P, H], j % per_half)
             for a in range(CP):
                 nc.tensor.matmul_mx(
                     out=acc[:], lhsT=token_tile(v2[a], j), lhsT_scale=v2_sc[4 * (a + 1) :, cols],
@@ -216,7 +212,7 @@ def tile_list_gated_bilinear_decoder_kernel(
             nc.scalar.activation(d_halves[j // per_half][:, j % per_half], dealt(acc), COPY)
 
         def turned_sum(j):
-            total = bank([P, PACK, P], j)
+            total = bank([P, PACK, P], (j + per_half) % TILES)
             for t in range(PACK):
                 for halves, first in ((d_halves, True), (pq_halves, False)):
                     nc.tensor.matmul(
@@ -227,17 +223,22 @@ def tile_list_gated_bilinear_decoder_kernel(
 
         for j in range(TILES):
             document_term(j)
+        turned_bias = bank([P, P], 0)
+        nc.tensor.transpose(turned_bias[:], bias_rows[:], ident[:])
+        nc.scalar.activation(bias[:], turned_bias[:, 0 : N // P], COPY)
         sums = [turned_sum(j) for j in range(TILES)]
 
         gate = held("gate", [P, PACK, S], F32)
         for t in range(PACK - 1):
             nc.vector.tensor_copy(gate[:, t, :], g_win[t][:].indirect(idx[:]))
 
-        def gated_tiles(first_tile, count):
-            tokens = slice(first_tile * P, (first_tile + count) * P)
+        def last_gates(grp):
             nc.vector.tensor_copy(
-                gate[:, PACK - 1, tokens], g_win[PACK - 1][:].indirect(entries(idx, tokens.start, count * P))
+                gate[:, PACK - 1, grp * GROUP : (grp + 1) * GROUP],
+                g_win[PACK - 1][:].indirect(entries(idx, grp * GROUP, GROUP)),
             )
+
+        def gated_tiles(first_tile, count):
             h = held("h%d" % first_tile, [P, count * P, PACK], BF16)
             for jj in range(count):
                 j = first_tile + jj
@@ -289,7 +290,7 @@ def tile_list_gated_bilinear_decoder_kernel(
         def next_group():
             grp = len(h_mx)
             h_mx.append(gated_tiles(grp * PAIR, PAIR))
-            free[0:0] = range(grp * PAIR, (grp + 1) * PAIR)
+            free[0:0] = [(j + per_half) % TILES for j in range(grp * PAIR, (grp + 1) * PAIR)]
             for c in range(len(w_mx)):
                 project(grp, c)
 
@@ -299,10 +300,14 @@ def tile_list_gated_bilinear_decoder_kernel(
             for grp in range(len(h_mx)):
                 project(grp, c)
 
+        last_gates(0)
+        next_group()
+        last_gates(1)
+        next_chunk(None)
         next_group()
         next_chunk(None)
-        next_chunk(None)
-        next_group()
+        last_gates(2)
         next_chunk(nc.vector.tensor_copy)
         next_group()
+        last_gates(3)
         next_group()

@@ -61,7 +61,8 @@ def tile_list_gated_bilinear_decoder_kernel(
         a1_raw = [held("a1_raw%d" % a, [P, PACK, H], F32) for a in range(KP)]
         w_raw = [held("w_raw%d" % c, [P, PACK, W_CHUNK], F32) for c in range(W_CHUNKS)]
         a2_w = held("a2_w", [P, KP, 2 * H], U8)
-        bd_w = held("bd_w", [P, CP, H], I32)
+        bd_w = held("bd_w", [P, CP - 1, H], I32)
+        bd_last = held("bd_last", [P, H], I32)
         bias_rows = held("bias_rows", [P, P], F32)
         bias = held("bias", [P, N // P], F32)
         ident = held("ident", [P, P], F32)
@@ -102,10 +103,12 @@ def tile_list_gated_bilinear_decoder_kernel(
         nc.sync.dma_start(out=v_sc_low[0:MOVED, :].bitcast(I32), in_=v_sc[4 : 4 + MOVED, :].bitcast(I32))
         load_words(v2_win[0], tab2_words[0])
         load_words(v2_win[1], tab2_words[1])
-        nc.sync.dma_start(out=bd_w[:], in_=bd_words.rearrange("a p e i -> p a (e i)").bitcast(I32))
+        nc.sync.dma_start(out=bd_w[:], in_=bd_words[0 : CP - 1].rearrange("a p e i -> p a (e i)").bitcast(I32))
         load_words(v2_win[2], tab2_words[2])
         for t in range(PACK):
             nc.sync.dma_start(out=g_win[t][:], in_=gate_rows[:, t, :])
+            if t == 0:
+                load_words(bd_last, bd_words[CP - 1])
         for c in range(W_CHUNKS):
             load_rows(w_raw[c], w[:, c * W_CHUNK : (c + 1) * W_CHUNK])
 
@@ -206,7 +209,7 @@ def tile_list_gated_bilinear_decoder_kernel(
             for a in range(CP):
                 nc.tensor.matmul_mx(
                     out=acc[:], lhsT=token_tile(v2[a], j), lhsT_scale=v2_sc[4 * (a + 1) :, cols],
-                    rhs=bd_w[:, a, :].bitcast(FP8X4), rhs_scale=bd_sc[4 * (a + 1) :, :],
+                    rhs=(bd_w[:, a, :] if a < CP - 1 else bd_last[:]).bitcast(FP8X4), rhs_scale=bd_sc[4 * (a + 1) :, :],
                     start=(a == 0), stop=(a == CP - 1),
                 )
             nc.scalar.activation(d_halves[j // per_half][:, j % per_half], dealt(acc), COPY)
@@ -307,7 +310,7 @@ def tile_list_gated_bilinear_decoder_kernel(
         next_group()
         next_chunk(None)
         last_gates(2)
-        next_chunk(nc.vector.tensor_copy)
         next_group()
+        next_chunk(None)
         last_gates(3)
         next_group()

@@ -31,7 +31,6 @@ LIST = 16
 RUN = 4
 GROUP = 256
 GROUPS = S // GROUP
-MOVED = 100
 PAIR = 2
 
 
@@ -100,7 +99,10 @@ def tile_list_gated_bilinear_decoder_kernel(
         nc.sync.dma_start(out=a2_w[:].bitcast(I32), in_=a2_words.rearrange("a p e -> p a e").bitcast(I32))
         load_words(v_win[1], tab_words[1])
         nc.vector.tensor_copy(v_sc[:], v_scale_win[:].indirect(idx[:]))
-        nc.sync.dma_start(out=v_sc_low[0:MOVED, :].bitcast(I32), in_=v_sc[4 : 4 + MOVED, :].bitcast(I32))
+        for Q in range(4):
+            nc.sync.dma_start(
+                out=v_sc_low[32 * Q : 32 * Q + 4, :].bitcast(I32), in_=v_sc[32 * Q + 4 : 32 * Q + 8, :].bitcast(I32)
+            )
         load_words(v2_win[0], tab2_words[0])
         load_words(v2_win[1], tab2_words[1])
         nc.sync.dma_start(out=bd_w[:], in_=bd_words[0 : CP - 1].rearrange("a p e i -> p a (e i)").bitcast(I32))

@@ -22,16 +22,22 @@ ADD = mybir.AluOpType.add
 P = 128
 PACK = 4
 K_PASS = P * PACK
-KP = K // K_PASS
-CP = C // K_PASS
+TOKEN_PASSES = K // K_PASS
+DOC_PASSES = C // K_PASS
 TILES = S // P
-W_CHUNK = 256
-W_CHUNKS = N // W_CHUNK
+HALF = TILES // 2
+QUADRANTS = 4
+ROWS = 4
 LIST = 16
 RUN = 4
+CHUNK = 256
+CHUNKS = N // CHUNK
+BLOCKS = CHUNK // P
 GROUP = 256
 GROUPS = S // GROUP
-PAIR = 2
+PAIR = GROUP // P
+TOKEN_PIECES = 4
+DOC_PIECES = 2
 
 
 def tile_list_gated_bilinear_decoder_kernel(
@@ -40,103 +46,103 @@ def tile_list_gated_bilinear_decoder_kernel(
 ):
     nc = tc.nc
     with ExitStack() as ctx:
-        keep = ctx.enter_context(tc.tile_pool(name="keep", bufs=1))
+        sbuf = ctx.enter_context(tc.tile_pool(name="sbuf", bufs=1))
         psum = ctx.enter_context(tc.psum_pool(name="psum", bufs=1))
 
         def held(name, shape, dtype, tag=""):
-            return keep.tile(shape, dtype, name=name, tag=tag or name, align_bytes=64)
+            return sbuf.tile(shape, dtype, name=name, tag=tag or name, align_bytes=64)
+
+        def bank(b, shape):
+            return psum.tile(shape, F32, name="bank%d" % b)
 
         idx = held("idx", [P, S // LIST], U16)
         idx2 = held("idx2", [P, S // LIST], U16)
-        v_scale_win = held("v_scale_win", [P, T], U8)
-        v2_scale_win = held("v2_scale_win", [P, T], U8)
-        a2_sc = held("a2_sc", [P, KP, H], U8)
-        bd_sc = held("bd_sc", [P, H], U8)
-        v_sc = held("v_sc", [P, S], U8)
-        v_sc_low = held("v_sc_low", [P, S], U8)
-        v_win = [held("v_win%d" % a, [P, T], I32) for a in range(KP)]
-        v2_win = [held("v2_win%d" % a, [P, T], I32) for a in range(CP)]
-        g_win = [held("g_win%d" % t, [P, T], F32) for t in range(PACK)]
-        a1_raw = [held("a1_raw%d" % a, [P, PACK, H], F32) for a in range(KP)]
-        w_raw = [held("w_raw%d" % c, [P, PACK, W_CHUNK], F32) for c in range(W_CHUNKS)]
-        a2_w = held("a2_w", [P, KP, 2 * H], U8)
-        bd_w = held("bd_w", [P, CP - 1, H], I32)
+        tok_scale_win = held("tok_scale_win", [P, T], U8)
+        doc_scale_win = held("doc_scale_win", [P, T], U8)
+        tok_win = [held("tok_win%d" % a, [P, T], I32) for a in range(TOKEN_PASSES)]
+        doc_win = [held("doc_win%d" % a, [P, T], I32) for a in range(DOC_PASSES)]
+        gate_win = [held("gate_win%d" % t, [P, T], F32) for t in range(PACK)]
+        a1_raw = [held("a1_raw%d" % a, [P, PACK, H], F32) for a in range(TOKEN_PASSES)]
+        w_raw = [held("w_raw%d" % c, [P, PACK, CHUNK], F32) for c in range(CHUNKS)]
+        a2_codes = held("a2_codes", [P, TOKEN_PASSES, 2 * H], U8)
+        a2_planes = held("a2_planes", [P, TOKEN_PASSES, H], U8)
+        bd_codes = held("bd_codes", [P, DOC_PASSES - 1, H], I32)
         bd_last = held("bd_last", [P, H], I32)
+        bd_planes = held("bd_planes", [P, DOC_PASSES, H], U8)
+        tok_planes = held("tok_planes", [P, S], U8)
+        tok_plane_low = held("tok_plane_low", [P, S], U8)
         bias_rows = held("bias_rows", [P, P], F32)
         bias = held("bias", [P, N // P], F32)
         ident = held("ident", [P, P], F32)
 
-        nc.gpsimd.memset(v2_scale_win[:].bitcast(I32), 0)
-        nc.vector.memset(bias_rows[:], 0.0)
-        for plane in (v_scale_win[:], a2_sc[:], v_sc_low[:], bd_sc[:]):
+        nc.gpsimd.memset(doc_scale_win[:].bitcast(I32), 0)
+        for plane in (tok_scale_win[:], a2_planes[:], tok_plane_low[:], bd_planes[:]):
             nc.vector.memset(plane.bitcast(I32), 0)
-
-        def load_rows(dst, src):
-            nc.sync.dma_start(out=dst[:], in_=src.rearrange("(p j) n -> p j n", j=PACK))
-
-        def load_planes(plane, src):
-            for Q in range(4):
-                nc.gpsimd.dma_start(
-                    out=plane[32 * Q : 32 * Q + 4, :, :].bitcast(I32),
-                    in_=src[:, 4 * Q : 4 * Q + 4, :].rearrange("a r e -> r a e").bitcast(I32),
-                )
-
-        gate_rows = gT.rearrange("(p t) s -> p t s", t=PACK)
+        nc.vector.memset(bias_rows[:], 0.0)
 
         def load_words(dst, src):
             nc.sync.dma_start(out=dst[:], in_=src.rearrange("p t i -> p (t i)").bitcast(I32))
 
+        def load_rows(dst, src):
+            nc.sync.dma_start(out=dst[:], in_=src.rearrange("(p j) n -> p j n", j=PACK))
+
+        def load_packed_scales(queue, win, src, first_row):
+            rows = ROWS * src.shape[0]
+            for Q in range(QUADRANTS):
+                queue.dma_start(
+                    out=win[32 * Q + first_row : 32 * Q + first_row + rows, :].bitcast(I32),
+                    in_=src[:, ROWS * Q : ROWS * (Q + 1), :].bitcast(I32),
+                )
+
+        def load_weight_scales(planes, src):
+            for Q in range(QUADRANTS):
+                nc.sync.dma_start(
+                    out=planes[32 * Q : 32 * Q + ROWS, :, :].bitcast(I32),
+                    in_=src[:, ROWS * Q : ROWS * (Q + 1), :].rearrange("a r e -> r a e").bitcast(I32),
+                )
+
+        gate_rows = gT.rearrange("(p t) s -> p t s", t=PACK)
+
+        load_packed_scales(nc.gpsimd, doc_scale_win, tab2_scales, ROWS)
+        make_identity(nc, ident[:])
+
         nc.sync.dma_start(idx[:], offs)
-        load_words(v_win[0], tab_words[0])
-        for Q in range(4):
-            nc.sync.dma_start(
-                out=v_scale_win[32 * Q : 32 * Q + 4 * KP, :].bitcast(I32),
-                in_=tab_scales[:, 4 * Q : 4 * Q + 4, :].bitcast(I32),
-            )
+        load_words(tok_win[0], tab_words[0])
+        load_packed_scales(nc.sync, tok_scale_win, tab_scales, 0)
         load_rows(a1_raw[0], a1[0:K_PASS, :])
         nc.sync.dma_start(idx2[:], offs2)
         load_rows(a1_raw[1], a1[K_PASS:K, :])
-        nc.sync.dma_start(out=a2_w[:].bitcast(I32), in_=a2_words.rearrange("a p e -> p a e").bitcast(I32))
-        load_words(v_win[1], tab_words[1])
-        nc.vector.tensor_copy(v_sc[:], v_scale_win[:].indirect(idx[:]))
-        for Q in range(4):
+        load_weight_scales(a2_planes, a2_scales)
+        nc.sync.dma_start(out=a2_codes[:].bitcast(I32), in_=a2_words.rearrange("a p e -> p a e").bitcast(I32))
+        load_words(tok_win[1], tab_words[1])
+        nc.vector.tensor_copy(tok_planes[:], tok_scale_win[:].indirect(idx[:]))
+        for Q in range(QUADRANTS):
             nc.sync.dma_start(
-                out=v_sc_low[32 * Q : 32 * Q + 4, :].bitcast(I32), in_=v_sc[32 * Q + 4 : 32 * Q + 8, :].bitcast(I32)
+                out=tok_plane_low[32 * Q : 32 * Q + ROWS, :].bitcast(I32),
+                in_=tok_planes[32 * Q + ROWS : 32 * Q + 2 * ROWS, :].bitcast(I32),
             )
-        load_words(v2_win[0], tab2_words[0])
-        load_words(v2_win[1], tab2_words[1])
-        nc.sync.dma_start(out=bd_w[:], in_=bd_words[0 : CP - 1].rearrange("a p e i -> p a (e i)").bitcast(I32))
-        load_words(v2_win[2], tab2_words[2])
+        load_words(doc_win[0], tab2_words[0])
+        load_words(doc_win[1], tab2_words[1])
+        load_weight_scales(bd_planes, bd_scales)
+        nc.sync.dma_start(
+            out=bd_codes[:], in_=bd_words[0 : DOC_PASSES - 1].rearrange("a p e i -> p a (e i)").bitcast(I32)
+        )
+        load_words(doc_win[2], tab2_words[2])
+        nc.sync.dma_start(out=bias_rows[0 : N // P, :], in_=by.rearrange("(c p) -> c p", p=P))
         for t in range(PACK):
-            nc.sync.dma_start(out=g_win[t][:], in_=gate_rows[:, t, :])
+            nc.sync.dma_start(out=gate_win[t][:], in_=gate_rows[:, t, :])
             if t == 0:
-                load_words(bd_last, bd_words[CP - 1])
-        for c in range(W_CHUNKS):
-            load_rows(w_raw[c], w[:, c * W_CHUNK : (c + 1) * W_CHUNK])
-
-        for Q in range(4):
-            nc.gpsimd.dma_start(
-                out=v2_scale_win[32 * Q + 4 : 32 * Q + 4 + 4 * CP, :].bitcast(I32),
-                in_=tab2_scales[:, 4 * Q : 4 * Q + 4, :].bitcast(I32),
-            )
-        load_planes(a2_sc, a2_scales)
-        for Q in range(4):
-            nc.gpsimd.dma_start(
-                out=bd_sc[32 * Q + 4 : 32 * Q + 4 + 4 * CP, :].bitcast(I32),
-                in_=bd_scales[:, 4 * Q : 4 * Q + 4, :].bitcast(I32),
-            )
-        nc.gpsimd.dma_start(out=bias_rows[0 : N // P, :], in_=by.rearrange("(c p) -> c p", p=P))
-        make_identity(nc, ident[:])
-
-        def entries(lst, first, count):
-            return lst[:, first // LIST : (first + count) // LIST]
+                load_words(bd_last, bd_words[DOC_PASSES - 1])
+        for c in range(CHUNKS):
+            load_rows(w_raw[c], w[:, c * CHUNK : (c + 1) * CHUNK])
 
         def gather_words(name, win, lst, pieces):
             count = S // pieces
             parts = []
             for u in range(pieces):
                 picked = held("%s_%d" % (name, u), [P, count], U32)
-                nc.vector.tensor_copy(picked[:], win[:].bitcast(U32).indirect(entries(lst, u * count, count)))
+                entries = lst[:, u * count // LIST : (u + 1) * count // LIST]
+                nc.vector.tensor_copy(picked[:], win[:].bitcast(U32).indirect(entries))
                 parts.append(picked)
             return parts
 
@@ -144,14 +150,16 @@ def tile_list_gated_bilinear_decoder_kernel(
             u, first = divmod(j * P, S // len(parts))
             return parts[u][:, first : first + P].bitcast(FP8X4)
 
-        def quantize_rows(name, raw, width, engine_copy=None):
+        def rounded_rows(name, raw, width):
             grouped = held(name + "_rounded", [P, width, PACK], BF16)
-            dst = grouped[:].rearrange("p (c i) t -> p c t i", i=RUN)
-            src = raw.rearrange("p t (c i) -> p c t i", i=RUN)
-            if engine_copy:
-                engine_copy(dst, src)
-            else:
-                nc.scalar.activation(dst, src, COPY)
+            nc.scalar.activation(
+                grouped[:].rearrange("p (c i) t -> p c t i", i=RUN),
+                raw[:].rearrange("p t (c i) -> p c t i", i=RUN),
+                COPY,
+            )
+            return grouped
+
+        def quantized(name, grouped, width):
             codes = held(name + "_codes", [P, width], U32)
             scales = held(name + "_scales", [P, width], U8)
             nc.vector.quantize_mx(
@@ -159,160 +167,148 @@ def tile_list_gated_bilinear_decoder_kernel(
             )
             return codes, scales
 
-        v = [gather_words("v0", v_win[0], idx, 1)]
-        v2_sc = held("v2_sc", [P, S], U8, tag="v_scale_win")
-        nc.vector.tensor_copy(v2_sc[:], v2_scale_win[:].indirect(idx2[:]))
-        a1_mx = [quantize_rows("a1_%d" % a, a1_raw[a][:], H) for a in range(KP)]
-        v.append(gather_words("v1", v_win[1], idx, 4))
-        v2 = [gather_words("v2_%d" % a, v2_win[a], idx2, 2 if a == CP - 1 else 1) for a in range(CP)]
-
-        def bank(shape, b):
-            return psum.tile(shape, F32, name="bank%d" % b)
+        tok = [gather_words("tok0", tok_win[0], idx, 1)]
+        doc_planes = held("doc_planes", [P, S], U8, tag="tok_scale_win")
+        nc.vector.tensor_copy(doc_planes[:], doc_scale_win[:].indirect(idx2[:]))
+        a1_mx = [quantized("a1_%d" % a, rounded_rows("a1_%d" % a, a1_raw[a], H), H) for a in range(TOKEN_PASSES)]
+        tok.append(gather_words("tok1", tok_win[1], idx, TOKEN_PIECES))
+        doc = [
+            gather_words("doc%d" % a, doc_win[a], idx2, DOC_PIECES if a == DOC_PASSES - 1 else 1)
+            for a in range(DOC_PASSES)
+        ]
 
         def dealt(acc):
             return acc[:].rearrange("p (m t) -> p t m", t=PACK)
 
-        per_half = TILES // 2
-        pq_halves = [held("pq%d" % u, [P, per_half, PACK, P], F32, tag="v_win%d" % u) for u in range(2)]
-        d_halves = [held("d%d" % u, [P, per_half, PACK, P], F32, tag="a1_raw%d" % u) for u in range(2)]
-        v_planes = (v_sc, v_sc_low)
-        a2_mx = [(a2_w[:, a, :].bitcast(FP4X4), a2_sc[:, a, :]) for a in range(KP)]
+        pq_halves = [held("pq%d" % u, [P, HALF, PACK, P], F32, tag="tok_win%d" % u) for u in range(2)]
+        d_halves = [held("d%d" % u, [P, HALF, PACK, P], F32, tag="a1_raw%d" % u) for u in range(2)]
+        planes_of_pass = (tok_planes, tok_plane_low)
         a1_ops = [(codes[:].bitcast(FP8X4), scales[:]) for codes, scales in a1_mx]
+        a2_ops = [(a2_codes[:, a, :].bitcast(FP4X4), a2_planes[:, a, :]) for a in range(TOKEN_PASSES)]
 
         def token_pass(acc, weight, j, a):
             codes, scales = weight[a]
             nc.tensor.matmul_mx(
-                out=acc[:], lhsT=token_tile(v[a], j), lhsT_scale=v_planes[a][:, j * P : (j + 1) * P],
-                rhs=codes, rhs_scale=scales, start=(a == 0), stop=(a == KP - 1),
+                out=acc[:], lhsT=token_tile(tok[a], j), lhsT_scale=planes_of_pass[a][:, j * P : (j + 1) * P],
+                rhs=codes, rhs_scale=scales, start=(a == 0), stop=(a == TOKEN_PASSES - 1),
             )
 
         def opened(weight, j, b):
-            acc = bank([P, H], b)
+            acc = bank(b, [P, H])
             token_pass(acc, weight, j, 0)
             return acc
 
-        p_open = [opened(a1_ops, j, 2 * j) for j in range(per_half)]
-        q_open = [opened(a2_mx, j, 2 * j + 1) for j in range(per_half)]
+        p_open = [opened(a1_ops, j, 2 * j) for j in range(HALF)]
+        q_open = [opened(a2_ops, j, 2 * j + 1) for j in range(HALF)]
         for j in range(TILES):
-            acc = p_open[j] if j < per_half else opened(a1_ops, j, 2 * (j - per_half))
+            acc = p_open[j] if j < HALF else opened(a1_ops, j, 2 * (j - HALF))
             token_pass(acc, a1_ops, j, 1)
-            pq = pq_halves[j // per_half][:, j % per_half]
+            pq = pq_halves[j // HALF][:, j % HALF]
             nc.scalar.activation(pq, dealt(acc), COPY)
-            acc = q_open[j] if j < per_half else opened(a2_mx, j, 2 * (j - per_half) + 1)
-            token_pass(acc, a2_mx, j, 1)
+            acc = q_open[j] if j < HALF else opened(a2_ops, j, 2 * (j - HALF) + 1)
+            token_pass(acc, a2_ops, j, 1)
             q = held("q%d" % j, [P, PACK, P], F32)
             nc.scalar.activation(q[:], dealt(acc), COPY)
             nc.gpsimd.tensor_tensor(pq, pq, q[:], MULT)
 
+        def doc_pass(acc, j, a):
+            codes = bd_codes[:, a, :] if a < DOC_PASSES - 1 else bd_last[:]
+            nc.tensor.matmul_mx(
+                out=acc[:], lhsT=token_tile(doc[a], j), lhsT_scale=doc_planes[ROWS * (a + 1) :, j * P : (j + 1) * P],
+                rhs=codes.bitcast(FP8X4), rhs_scale=bd_planes[:, a, :],
+                start=(a == 0), stop=(a == DOC_PASSES - 1),
+            )
 
-        def document_term(j):
-            cols = slice(j * P, (j + 1) * P)
-            acc = bank([P, H], j % per_half)
-            for a in range(CP):
-                nc.tensor.matmul_mx(
-                    out=acc[:], lhsT=token_tile(v2[a], j), lhsT_scale=v2_sc[4 * (a + 1) :, cols],
-                    rhs=(bd_w[:, a, :] if a < CP - 1 else bd_last[:]).bitcast(FP8X4), rhs_scale=bd_sc[4 * (a + 1) :, :],
-                    start=(a == 0), stop=(a == CP - 1),
-                )
-            nc.scalar.activation(d_halves[j // per_half][:, j % per_half], dealt(acc), COPY)
+        d_open = [bank(j, [P, H]) for j in range(TILES)]
+        for j in range(TILES):
+            for a in range(DOC_PASSES - 1):
+                doc_pass(d_open[j], j, a)
+        for j in range(TILES):
+            doc_pass(d_open[j], j, DOC_PASSES - 1)
+            nc.scalar.activation(d_halves[j // HALF][:, j % HALF], dealt(d_open[j]), COPY)
 
         def turned_sum(j):
-            total = bank([P, PACK, P], (j + per_half) % TILES)
+            total = bank(j, [P, PACK, P])
             for t in range(PACK):
                 for halves, first in ((d_halves, True), (pq_halves, False)):
                     nc.tensor.matmul(
-                        total[:, t, :], lhsT=halves[j // per_half][:, j % per_half, t, :], rhs=ident[:],
+                        total[:, t, :], lhsT=halves[j // HALF][:, j % HALF, t, :], rhs=ident[:],
                         is_transpose=True, start=first, stop=not first,
                     )
             return total
 
-        for j in range(TILES):
-            document_term(j)
-        turned_bias = bank([P, P], 0)
-        nc.tensor.transpose(turned_bias[:], bias_rows[:], ident[:])
-        nc.scalar.activation(bias[:], turned_bias[:, 0 : N // P], COPY)
         sums = [turned_sum(j) for j in range(TILES)]
 
         gate = held("gate", [P, PACK, S], F32)
-        for t in range(PACK - 1):
-            nc.vector.tensor_copy(gate[:, t, :], g_win[t][:].indirect(idx[:]))
+        for t in range(PACK):
+            nc.vector.tensor_copy(gate[:, t, :], gate_win[t][:].indirect(idx[:]))
+        w_rounded = [rounded_rows("w%d" % c, w_raw[c], CHUNK) for c in range(CHUNKS)]
 
-        def last_gates(grp):
-            nc.vector.tensor_copy(
-                gate[:, PACK - 1, grp * GROUP : (grp + 1) * GROUP],
-                g_win[PACK - 1][:].indirect(entries(idx, grp * GROUP, GROUP)),
+        def gated(h, grp, jj):
+            j = grp * PAIR + jj
+            nc.vector.tensor_tensor(
+                h[:, jj * P : (jj + 1) * P, :].rearrange("p (c i) t -> p c t i", i=RUN),
+                sums[j][:].rearrange("p t (c i) -> p c t i", i=RUN),
+                gate[:, :, j * P : (j + 1) * P].rearrange("p t (c i) -> p c t i", i=RUN),
+                MULT,
             )
 
-        def gated_tiles(first_tile, count):
-            h = held("h%d" % first_tile, [P, count * P, PACK], BF16)
-            for jj in range(count):
-                j = first_tile + jj
-                nc.vector.tensor_tensor(
-                    h[:, jj * P : (jj + 1) * P, :].rearrange("p (c i) t -> p c t i", i=RUN),
-                    sums[j][:].rearrange("p t (c i) -> p c t i", i=RUN),
-                    gate[:, :, j * P : (j + 1) * P].rearrange("p t (c i) -> p c t i", i=RUN),
-                    MULT,
-                )
-            h_codes = held("h_codes%d" % first_tile, [P, count * P], U32)
-            h_scales = held("h_scales%d" % first_tile, [P, count * P], U8)
-            nc.vector.quantize_mx(
-                out=h_codes[:].bitcast(FP8X4), scales=h_scales[:], in_=h[:].rearrange("p s t -> p (s t)")
-            )
-            return h_codes, h_scales
+        def gated_group(grp, tag=""):
+            h = held("h%d" % grp, [P, GROUP, PACK], BF16, tag=tag)
+            for jj in range(PAIR):
+                gated(h, grp, jj)
+            return h
 
-        spent = ["q%d" % j for j in range(TILES)] + ["a1_0_rounded", "v2_scale_win", "a1_1_rounded", "v2_win0"]
+        spent = ["q%d" % j for j in range(TILES)] + ["a1_0_rounded", "a1_1_rounded", "doc_win0", "doc_win1"]
 
-        def project(grp, c):
+        def project(grp, c, b, on_vector=False):
             h_codes, h_scales = h_mx[grp]
             codes, scales = w_mx[c]
-            tokens = slice(grp * GROUP, (grp + 1) * GROUP)
-            per_bank = W_CHUNK // P
-            b = free.pop(0)
-            y = bank([P, per_bank, GROUP], b)
-            staged = held("staged%d_%d" % (grp, c), [P, per_bank, GROUP], F32, tag=spent[grp * W_CHUNKS + c])
-            for e in range(per_bank):
+            y = bank(b, [P, BLOCKS, GROUP])
+            staged = held("staged%d_%d" % (grp, c), [P, BLOCKS, GROUP], F32, tag=spent[grp * CHUNKS + c])
+            for e in range(BLOCKS):
                 chans = slice(e * P, (e + 1) * P)
                 nc.tensor.matmul_mx(
                     out=y[:, e, :], lhsT=codes[:, chans].bitcast(FP8X4), lhsT_scale=scales[:, chans],
                     rhs=h_codes[:].bitcast(FP8X4), rhs_scale=h_scales[:], start=True, stop=True,
                 )
-            n_first = c * per_bank
-            if grp == GROUPS - 1 and c != 1:
-                spread = bias[:, n_first : n_first + per_bank].unsqueeze(2).to_broadcast([P, per_bank, GROUP])
+            first = c * BLOCKS
+            if on_vector:
+                spread = bias[:, first : first + BLOCKS].unsqueeze(2).to_broadcast([P, BLOCKS, GROUP])
                 nc.vector.tensor_tensor(staged[:], y[:], spread, ADD)
             else:
-                for e in range(per_bank):
+                for e in range(BLOCKS):
                     nc.scalar.activation(
-                        staged[:, e, :], y[:, e, :], IDENTITY, bias=bias[:, n_first + e : n_first + e + 1]
+                        staged[:, e, :], y[:, e, :], IDENTITY, bias=bias[:, first + e : first + e + 1]
                     )
-            rows = slice(c * W_CHUNK, (c + 1) * W_CHUNK)
-            nc.sync.dma_start(out=out[rows, tokens].rearrange("(e p) s -> p e s", p=P), in_=staged[:])
-            free.append(b)
+            nc.sync.dma_start(
+                out=out[c * CHUNK : (c + 1) * CHUNK, grp * GROUP : (grp + 1) * GROUP].rearrange(
+                    "(e p) s -> p e s", p=P
+                ),
+                in_=staged[:],
+            )
 
-        h_mx, w_mx, free = [], [], []
-
-
-        def next_group():
-            grp = len(h_mx)
-            h_mx.append(gated_tiles(grp * PAIR, PAIR))
-            free[0:0] = [(j + per_half) % TILES for j in range(grp * PAIR, (grp + 1) * PAIR)]
-            for c in range(len(w_mx)):
-                project(grp, c)
-
-        def next_chunk(engine_copy):
-            c = len(w_mx)
-            w_mx.append(quantize_rows("w%d" % c, w_raw[c][:], W_CHUNK, engine_copy))
-            for grp in range(len(h_mx)):
-                project(grp, c)
-
-        last_gates(0)
-        next_group()
-        last_gates(1)
-        next_chunk(None)
-        next_group()
-        next_chunk(None)
-        last_gates(2)
-        next_group()
-        next_chunk(None)
-        last_gates(3)
-        next_group()
+        h_mx, w_mx = [], []
+        h_mx.append(quantized("h0", gated_group(0), GROUP))
+        turned_bias = bank(0, [P, P])
+        nc.tensor.transpose(turned_bias[:], bias_rows[:], ident[:])
+        nc.scalar.activation(bias[:], turned_bias[:, 0 : N // P], COPY)
+        for c in range(2):
+            w_mx.append(quantized("w%d" % c, w_rounded[c], CHUNK))
+            project(0, c, 1 - c)
+        h = gated_group(1, tag="w_raw1")
+        w_mx.append(quantized("w2", w_rounded[2], CHUNK))
+        h_mx.append(quantized("h1", h, GROUP))
+        project(0, 2, 2)
+        for c, b in enumerate((3, 1, 0)):
+            project(1, c, b)
+        h = gated_group(2, tag="w_raw2")
+        h_last = held("h3", [P, GROUP, PACK], BF16)
+        gated(h_last, 3, 0)
+        h_mx.append(quantized("h2", h, GROUP))
+        gated(h_last, 3, 1)
+        for c, b in enumerate((4, 5, 2)):
+            project(2, c, b)
+        h_mx.append(quantized("h3", h_last, GROUP))
+        for c, b in enumerate((6, 7, 3)):
+            project(3, c, b, on_vector=(c != 2))

@@ -28,6 +28,7 @@ TILES = S // P
 HALF = TILES // 2
 QUADRANTS = 4
 ROWS = 4
+BLOCK_ROWS = 16
 LIST = 16
 RUN = 4
 CHUNK = 256
@@ -36,7 +37,7 @@ BLOCKS = CHUNK // P
 GROUP = 256
 GROUPS = S // GROUP
 PAIR = GROUP // P
-TOKEN_PIECES = 4
+TOKEN_PIECES = 2
 DOC_PIECES = 2
 
 
@@ -66,17 +67,19 @@ def tile_list_gated_bilinear_decoder_kernel(
         w_raw = [held("w_raw%d" % c, [P, PACK, CHUNK], F32) for c in range(CHUNKS)]
         a2_codes = held("a2_codes", [P, TOKEN_PASSES, 2 * H], U8)
         a2_planes = held("a2_planes", [P, TOKEN_PASSES, H], U8)
-        bd_codes = held("bd_codes", [P, DOC_PASSES - 1, H], I32)
-        bd_last = held("bd_last", [P, H], I32)
-        bd_planes = held("bd_planes", [P, DOC_PASSES, H], U8)
-        tok_planes = held("tok_planes", [P, S], U8)
-        tok_plane_low = held("tok_plane_low", [P, S], U8)
+        bd_codes = [held("bd_codes%d" % a, [P, H], I32) for a in range(DOC_PASSES)]
+        bd_planes = held("bd_planes", [P, H], U8)
+        tok_scale_rows = held("tok_scale_rows", [P, S], U8)
+        planes_of_pass = [held("tok_plane%d" % a, [P, S], U8) for a in range(TOKEN_PASSES)]
         bias_rows = held("bias_rows", [P, P], F32)
         bias = held("bias", [P, N // P], F32)
         ident = held("ident", [P, P], F32)
 
         nc.gpsimd.memset(doc_scale_win[:].bitcast(I32), 0)
-        for plane in (tok_scale_win[:], a2_planes[:], tok_plane_low[:], bd_planes[:]):
+        for plane in (
+            tok_scale_win[32:64, :], tok_scale_win[64:P, :], a2_planes[:],
+            planes_of_pass[0][:], planes_of_pass[1][:], bd_planes[:],
+        ):
             nc.vector.memset(plane.bitcast(I32), 0)
         nc.vector.memset(bias_rows[:], 0.0)
 
@@ -86,53 +89,54 @@ def tile_list_gated_bilinear_decoder_kernel(
         def load_rows(dst, src):
             nc.sync.dma_start(out=dst[:], in_=src.rearrange("(p j) n -> p j n", j=PACK))
 
-        def load_packed_scales(queue, win, src, first_row):
-            rows = ROWS * src.shape[0]
+        def load_packed_scales(queue, win, src):
             for Q in range(QUADRANTS):
                 queue.dma_start(
-                    out=win[32 * Q + first_row : 32 * Q + first_row + rows, :].bitcast(I32),
+                    out=win[32 * Q + ROWS : 32 * Q + ROWS * (1 + DOC_PASSES), :].bitcast(I32),
                     in_=src[:, ROWS * Q : ROWS * (Q + 1), :].bitcast(I32),
                 )
 
-        def load_weight_scales(planes, src):
-            for Q in range(QUADRANTS):
+        def move_plane(a):
+            for r in range(ROWS):
                 nc.sync.dma_start(
-                    out=planes[32 * Q : 32 * Q + ROWS, :, :].bitcast(I32),
-                    in_=src[:, ROWS * Q : ROWS * (Q + 1), :].rearrange("a r e -> r a e").bitcast(I32),
+                    out=planes_of_pass[a][r:P:32, :].bitcast(I32),
+                    in_=tok_scale_rows[BLOCK_ROWS * a + r : BLOCK_ROWS * (a + 1) : ROWS, :].bitcast(I32),
                 )
 
         gate_rows = gT.rearrange("(p t) s -> p t s", t=PACK)
 
-        load_packed_scales(nc.gpsimd, doc_scale_win, tab2_scales, ROWS)
+        load_packed_scales(nc.gpsimd, doc_scale_win, tab2_scales)
+        for Q in range(QUADRANTS):
+            nc.gpsimd.dma_start(
+                out=a2_planes[32 * Q : 32 * Q + ROWS, :, :].bitcast(I32),
+                in_=a2_scales[:, ROWS * Q : ROWS * (Q + 1), :].rearrange("a r e -> r a e").bitcast(I32),
+            )
         make_identity(nc, ident[:])
 
         nc.sync.dma_start(idx[:], offs)
-        load_words(tok_win[0], tab_words[0])
-        load_packed_scales(nc.sync, tok_scale_win, tab_scales, 0)
-        load_rows(a1_raw[0], a1[0:K_PASS, :])
+        nc.sync.dma_start(
+            out=tok_scale_win[0:32, :].bitcast(I32), in_=tab_scales.rearrange("a q t -> (a q) t").bitcast(I32)
+        )
         nc.sync.dma_start(idx2[:], offs2)
-        load_rows(a1_raw[1], a1[K_PASS:K, :])
-        load_weight_scales(a2_planes, a2_scales)
-        nc.sync.dma_start(out=a2_codes[:].bitcast(I32), in_=a2_words.rearrange("a p e -> p a e").bitcast(I32))
+        load_words(tok_win[0], tab_words[0])
+        load_rows(a1_raw[0], a1[0:K_PASS, :])
         load_words(tok_win[1], tab_words[1])
-        nc.vector.tensor_copy(tok_planes[:], tok_scale_win[:].indirect(idx[:]))
-        for Q in range(QUADRANTS):
-            nc.sync.dma_start(
-                out=tok_plane_low[32 * Q : 32 * Q + ROWS, :].bitcast(I32),
-                in_=tok_planes[32 * Q + ROWS : 32 * Q + 2 * ROWS, :].bitcast(I32),
-            )
+        nc.vector.tensor_copy(tok_scale_rows[:], tok_scale_win[:].indirect(idx[:]))
+        move_plane(0)
+        load_rows(a1_raw[1], a1[K_PASS:K, :])
+        move_plane(1)
+        nc.sync.dma_start(out=a2_codes[:].bitcast(I32), in_=a2_words.rearrange("a p e -> p a e").bitcast(I32))
         load_words(doc_win[0], tab2_words[0])
         load_words(doc_win[1], tab2_words[1])
-        load_weight_scales(bd_planes, bd_scales)
-        nc.sync.dma_start(
-            out=bd_codes[:], in_=bd_words[0 : DOC_PASSES - 1].rearrange("a p e i -> p a (e i)").bitcast(I32)
-        )
+        load_packed_scales(nc.sync, bd_planes, bd_scales)
+        load_words(bd_codes[0], bd_words[0])
         load_words(doc_win[2], tab2_words[2])
+        load_words(bd_codes[1], bd_words[1])
         nc.sync.dma_start(out=bias_rows[0 : N // P, :], in_=by.rearrange("(c p) -> c p", p=P))
         for t in range(PACK):
             nc.sync.dma_start(out=gate_win[t][:], in_=gate_rows[:, t, :])
             if t == 0:
-                load_words(bd_last, bd_words[DOC_PASSES - 1])
+                load_words(bd_codes[2], bd_words[2])
         for c in range(CHUNKS):
             load_rows(w_raw[c], w[:, c * CHUNK : (c + 1) * CHUNK])
 
@@ -150,13 +154,19 @@ def tile_list_gated_bilinear_decoder_kernel(
             u, first = divmod(j * P, S // len(parts))
             return parts[u][:, first : first + P].bitcast(FP8X4)
 
-        def rounded_rows(name, raw, width):
+        def rounded_rows(name, raw, width, on_vector=0):
             grouped = held(name + "_rounded", [P, width, PACK], BF16)
+            cut = width - on_vector
             nc.scalar.activation(
-                grouped[:].rearrange("p (c i) t -> p c t i", i=RUN),
-                raw[:].rearrange("p t (c i) -> p c t i", i=RUN),
+                grouped[:, 0:cut, :].rearrange("p (c i) t -> p c t i", i=RUN),
+                raw[:, :, 0:cut].rearrange("p t (c i) -> p c t i", i=RUN),
                 COPY,
             )
+            if on_vector:
+                nc.vector.tensor_copy(
+                    grouped[:, cut:width, :].rearrange("p (c i) t -> p c t i", i=RUN),
+                    raw[:, :, cut:width].rearrange("p t (c i) -> p c t i", i=RUN),
+                )
             return grouped
 
         def quantized(name, grouped, width):
@@ -168,10 +178,11 @@ def tile_list_gated_bilinear_decoder_kernel(
             return codes, scales
 
         tok = [gather_words("tok0", tok_win[0], idx, 1)]
-        doc_planes = held("doc_planes", [P, S], U8, tag="tok_scale_win")
+        doc_planes = held("doc_planes", [P, S], U8, tag="tok_win0")
         nc.vector.tensor_copy(doc_planes[:], doc_scale_win[:].indirect(idx2[:]))
-        a1_mx = [quantized("a1_%d" % a, rounded_rows("a1_%d" % a, a1_raw[a], H), H) for a in range(TOKEN_PASSES)]
+        a1_mx = [quantized("a1_0", rounded_rows("a1_0", a1_raw[0], H), H)]
         tok.append(gather_words("tok1", tok_win[1], idx, TOKEN_PIECES))
+        a1_mx.append(quantized("a1_1", rounded_rows("a1_1", a1_raw[1], H, on_vector=H // 2), H))
         doc = [
             gather_words("doc%d" % a, doc_win[a], idx2, DOC_PIECES if a == DOC_PASSES - 1 else 1)
             for a in range(DOC_PASSES)
@@ -180,9 +191,8 @@ def tile_list_gated_bilinear_decoder_kernel(
         def dealt(acc):
             return acc[:].rearrange("p (m t) -> p t m", t=PACK)
 
-        pq_halves = [held("pq%d" % u, [P, HALF, PACK, P], F32, tag="tok_win%d" % u) for u in range(2)]
+        pq_halves = [held("pq%d" % u, [P, HALF, PACK, P], F32, tag=("tok_win1", "doc_win0")[u]) for u in range(2)]
         d_halves = [held("d%d" % u, [P, HALF, PACK, P], F32, tag="a1_raw%d" % u) for u in range(2)]
-        planes_of_pass = (tok_planes, tok_plane_low)
         a1_ops = [(codes[:].bitcast(FP8X4), scales[:]) for codes, scales in a1_mx]
         a2_ops = [(a2_codes[:, a, :].bitcast(FP4X4), a2_planes[:, a, :]) for a in range(TOKEN_PASSES)]
 
@@ -198,28 +208,34 @@ def tile_list_gated_bilinear_decoder_kernel(
             token_pass(acc, weight, j, 0)
             return acc
 
-        p_open = [opened(a1_ops, j, 2 * j) for j in range(HALF)]
-        q_open = [opened(a2_ops, j, 2 * j + 1) for j in range(HALF)]
-        for j in range(TILES):
-            acc = p_open[j] if j < HALF else opened(a1_ops, j, 2 * (j - HALF))
-            token_pass(acc, a1_ops, j, 1)
-            pq = pq_halves[j // HALF][:, j % HALF]
-            nc.scalar.activation(pq, dealt(acc), COPY)
-            acc = q_open[j] if j < HALF else opened(a2_ops, j, 2 * (j - HALF) + 1)
-            token_pass(acc, a2_ops, j, 1)
-            q = held("q%d" % j, [P, PACK, P], F32)
-            nc.scalar.activation(q[:], dealt(acc), COPY)
-            nc.gpsimd.tensor_tensor(pq, pq, q[:], MULT)
+        def closed(acc, weight, j, dst):
+            token_pass(acc, weight, j, 1)
+            nc.scalar.activation(dst, dealt(acc), COPY)
+
+        pq = [pq_halves[j // HALF][:, j % HALF] for j in range(TILES)]
+        q = [held("q%d" % j, [P, PACK, P], F32) for j in range(TILES)]
+        p_open = [opened(a1_ops, j, j) for j in range(HALF)]
+        q_open = [opened(a2_ops, j, HALF + j) for j in range(HALF)]
+        for j in range(HALF):
+            closed(q_open[j], a2_ops, j, q[j][:])
+        for j in range(HALF):
+            closed(p_open[j], a1_ops, j, pq[j])
+            nc.gpsimd.tensor_tensor(pq[j], pq[j], q[j][:], MULT)
+        freed = [(HALF + n) % TILES for n in range(TILES)]
+        for j in range(HALF, TILES):
+            first = 2 * (j - HALF)
+            closed(opened(a2_ops, j, freed[first]), a2_ops, j, q[j][:])
+            closed(opened(a1_ops, j, freed[first + 1]), a1_ops, j, pq[j])
+            nc.gpsimd.tensor_tensor(pq[j], pq[j], q[j][:], MULT)
 
         def doc_pass(acc, j, a):
-            codes = bd_codes[:, a, :] if a < DOC_PASSES - 1 else bd_last[:]
             nc.tensor.matmul_mx(
                 out=acc[:], lhsT=token_tile(doc[a], j), lhsT_scale=doc_planes[ROWS * (a + 1) :, j * P : (j + 1) * P],
-                rhs=codes.bitcast(FP8X4), rhs_scale=bd_planes[:, a, :],
+                rhs=bd_codes[a][:].bitcast(FP8X4), rhs_scale=bd_planes[ROWS * (a + 1) :, :],
                 start=(a == 0), stop=(a == DOC_PASSES - 1),
             )
 
-        d_open = [bank(j, [P, H]) for j in range(TILES)]
+        d_open = [bank(freed[j], [P, H]) for j in range(TILES)]
         for j in range(TILES):
             for a in range(DOC_PASSES - 1):
                 doc_pass(d_open[j], j, a)
@@ -228,7 +244,7 @@ def tile_list_gated_bilinear_decoder_kernel(
             nc.scalar.activation(d_halves[j // HALF][:, j % HALF], dealt(d_open[j]), COPY)
 
         def turned_sum(j):
-            total = bank(j, [P, PACK, P])
+            total = bank(freed[j], [P, PACK, P])
             for t in range(PACK):
                 for halves, first in ((d_halves, True), (pq_halves, False)):
                     nc.tensor.matmul(
@@ -240,9 +256,14 @@ def tile_list_gated_bilinear_decoder_kernel(
         sums = [turned_sum(j) for j in range(TILES)]
 
         gate = held("gate", [P, PACK, S], F32)
-        for t in range(PACK):
+        for t in range(PACK - 1):
             nc.vector.tensor_copy(gate[:, t, :], gate_win[t][:].indirect(idx[:]))
-        w_rounded = [rounded_rows("w%d" % c, w_raw[c], CHUNK) for c in range(CHUNKS)]
+
+        def last_gates(grp):
+            nc.vector.tensor_copy(
+                gate[:, PACK - 1, grp * GROUP : (grp + 1) * GROUP],
+                gate_win[PACK - 1][:].indirect(idx[:, grp * GROUP // LIST : (grp + 1) * GROUP // LIST]),
+            )
 
         def gated(h, grp, jj):
             j = grp * PAIR + jj
@@ -259,9 +280,11 @@ def tile_list_gated_bilinear_decoder_kernel(
                 gated(h, grp, jj)
             return h
 
-        spent = ["q%d" % j for j in range(TILES)] + ["a1_0_rounded", "a1_1_rounded", "doc_win0", "doc_win1"]
+        spent = ["q%d" % j for j in range(TILES)] + ["a1_0_rounded", "a1_1_rounded", "doc_win2", "doc_win1"]
 
-        def project(grp, c, b, on_vector=False):
+        def project(grp, c):
+            b = free.pop(0)
+            on_vector = grp == GROUPS - 1 and c != 1
             h_codes, h_scales = h_mx[grp]
             codes, scales = w_mx[c]
             y = bank(b, [P, BLOCKS, GROUP])
@@ -287,28 +310,35 @@ def tile_list_gated_bilinear_decoder_kernel(
                 ),
                 in_=staged[:],
             )
+            free.append(b)
 
-        h_mx, w_mx = [], []
-        h_mx.append(quantized("h0", gated_group(0), GROUP))
-        turned_bias = bank(0, [P, P])
-        nc.tensor.transpose(turned_bias[:], bias_rows[:], ident[:])
-        nc.scalar.activation(bias[:], turned_bias[:, 0 : N // P], COPY)
-        for c in range(2):
-            w_mx.append(quantized("w%d" % c, w_rounded[c], CHUNK))
-            project(0, c, 1 - c)
-        h = gated_group(1, tag="w_raw1")
-        w_mx.append(quantized("w2", w_rounded[2], CHUNK))
-        h_mx.append(quantized("h1", h, GROUP))
-        project(0, 2, 2)
-        for c, b in enumerate((3, 1, 0)):
-            project(1, c, b)
-        h = gated_group(2, tag="w_raw2")
-        h_last = held("h3", [P, GROUP, PACK], BF16)
-        gated(h_last, 3, 0)
-        h_mx.append(quantized("h2", h, GROUP))
-        gated(h_last, 3, 1)
-        for c, b in enumerate((4, 5, 2)):
-            project(2, c, b)
-        h_mx.append(quantized("h3", h_last, GROUP))
-        for c, b in enumerate((6, 7, 3)):
-            project(3, c, b, on_vector=(c != 2))
+        h_mx, w_mx, free = [], [], []
+
+        def next_group():
+            grp = len(h_mx)
+            h_mx.append(quantized("h%d" % grp, gated_group(grp), GROUP))
+            free[0:0] = freed[grp * PAIR : (grp + 1) * PAIR]
+            if grp == 0:
+                turned_bias = bank(free[1], [P, P])
+                nc.tensor.transpose(turned_bias[:], bias_rows[:], ident[:])
+                nc.scalar.activation(bias[:], turned_bias[:, 0 : N // P], COPY)
+            for c in range(len(w_mx)):
+                project(grp, c)
+
+        def next_chunk():
+            c = len(w_mx)
+            w_mx.append(quantized("w%d" % c, rounded_rows("w%d" % c, w_raw[c], CHUNK), CHUNK))
+            for grp in range(len(h_mx)):
+                project(grp, c)
+
+        last_gates(0)
+        next_group()
+        last_gates(1)
+        next_chunk()
+        next_group()
+        next_chunk()
+        last_gates(2)
+        next_group()
+        next_chunk()
+        last_gates(3)
+        next_group()

@@ -29,6 +29,7 @@ HALF = TILES // 2
 QUADRANTS = 4
 ROWS = 4
 BLOCK_ROWS = 16
+LAST_QUADRANT = 96
 LIST = 16
 RUN = 4
 CHUNK = 256
@@ -66,22 +67,22 @@ def tile_list_gated_bilinear_decoder_kernel(
         a1_raw = [held("a1_raw%d" % a, [P, PACK, H], F32) for a in range(TOKEN_PASSES)]
         w_raw = [held("w_raw%d" % c, [P, PACK, CHUNK], F32) for c in range(CHUNKS)]
         a2_codes = held("a2_codes", [P, TOKEN_PASSES, 2 * H], U8)
-        a2_planes = held("a2_planes", [P, TOKEN_PASSES, H], U8)
         bd_codes = [held("bd_codes%d" % a, [P, H], I32) for a in range(DOC_PASSES)]
-        bd_planes = held("bd_planes", [P, H], U8)
         tok_scale_rows = held("tok_scale_rows", [P, S], U8)
-        planes_of_pass = [held("tok_plane%d" % a, [P, S], U8) for a in range(TOKEN_PASSES)]
+        planes = held("planes", [P, TOKEN_PASSES * (S + H) + H], U8)
+        planes_of_pass = [planes[:, a * S : (a + 1) * S] for a in range(TOKEN_PASSES)]
+        a2_planes = planes[:, TOKEN_PASSES * S : TOKEN_PASSES * (S + H)].rearrange("p (a e) -> p a e", e=H)
+        bd_planes = planes[:, TOKEN_PASSES * (S + H) :]
         bias_rows = held("bias_rows", [P, P], F32)
         bias = held("bias", [P, N // P], F32)
         ident = held("ident", [P, P], F32)
 
         nc.gpsimd.memset(doc_scale_win[:].bitcast(I32), 0)
-        for plane in (
-            tok_scale_win[32:64, :], tok_scale_win[64:P, :], a2_planes[:],
-            planes_of_pass[0][:], planes_of_pass[1][:], bd_planes[:],
-        ):
-            nc.vector.memset(plane.bitcast(I32), 0)
-        nc.vector.memset(bias_rows[:], 0.0)
+        nc.gpsimd.memset(bias_rows[:], 0.0)
+        for dead in (tok_scale_win[0:LAST_QUADRANT, :], planes[:]):
+            words = dead.bitcast(I32)
+            nc.vector.memset(words[:, 1:], 0)
+            nc.vector.memset(words[:, 0:1], 0)
 
         def load_words(dst, src):
             nc.sync.dma_start(out=dst[:], in_=src.rearrange("p t i -> p (t i)").bitcast(I32))
@@ -97,10 +98,11 @@ def tile_list_gated_bilinear_decoder_kernel(
                 )
 
         def move_plane(a):
+            first = LAST_QUADRANT + BLOCK_ROWS * a
             for r in range(ROWS):
                 nc.sync.dma_start(
                     out=planes_of_pass[a][r:P:32, :].bitcast(I32),
-                    in_=tok_scale_rows[BLOCK_ROWS * a + r : BLOCK_ROWS * (a + 1) : ROWS, :].bitcast(I32),
+                    in_=tok_scale_rows[first + r : first + BLOCK_ROWS : ROWS, :].bitcast(I32),
                 )
 
         gate_rows = gT.rearrange("(p t) s -> p t s", t=PACK)
@@ -115,7 +117,7 @@ def tile_list_gated_bilinear_decoder_kernel(
 
         nc.sync.dma_start(idx[:], offs)
         nc.sync.dma_start(
-            out=tok_scale_win[0:32, :].bitcast(I32), in_=tab_scales.rearrange("a q t -> (a q) t").bitcast(I32)
+            out=tok_scale_win[LAST_QUADRANT:P, :].bitcast(I32), in_=tab_scales.rearrange("a q t -> (a q) t").bitcast(I32)
         )
         nc.sync.dma_start(idx2[:], offs2)
         load_words(tok_win[0], tab_words[0])

@@ -69,10 +69,10 @@ def tile_list_gated_bilinear_decoder_kernel(
         a2_codes = held("a2_codes", [P, TOKEN_PASSES, 2 * H], U8)
         bd_codes = [held("bd_codes%d" % a, [P, H], I32) for a in range(DOC_PASSES)]
         tok_scale_rows = held("tok_scale_rows", [P, S], U8)
-        planes = held("planes", [P, TOKEN_PASSES * (S + H) + H], U8)
+        planes = held("planes", [P, TOKEN_PASSES * (S + H) + DOC_PASSES * H], U8)
         planes_of_pass = [planes[:, a * S : (a + 1) * S] for a in range(TOKEN_PASSES)]
         a2_planes = planes[:, TOKEN_PASSES * S : TOKEN_PASSES * (S + H)].rearrange("p (a e) -> p a e", e=H)
-        bd_planes = planes[:, TOKEN_PASSES * (S + H) :]
+        bd_planes = planes[:, TOKEN_PASSES * (S + H) :].rearrange("p (a e) -> p a e", e=H)
         bias_rows = held("bias_rows", [P, P], F32)
         bias = held("bias", [P, N // P], F32)
         ident = held("ident", [P, P], F32)
@@ -90,13 +90,6 @@ def tile_list_gated_bilinear_decoder_kernel(
         def load_rows(dst, src):
             nc.sync.dma_start(out=dst[:], in_=src.rearrange("(p j) n -> p j n", j=PACK))
 
-        def load_packed_scales(queue, win, src):
-            for Q in range(QUADRANTS):
-                queue.dma_start(
-                    out=win[32 * Q + ROWS : 32 * Q + ROWS * (1 + DOC_PASSES), :].bitcast(I32),
-                    in_=src[:, ROWS * Q : ROWS * (Q + 1), :].bitcast(I32),
-                )
-
         def move_plane(a):
             first = LAST_QUADRANT + BLOCK_ROWS * a
             for r in range(ROWS):
@@ -107,7 +100,11 @@ def tile_list_gated_bilinear_decoder_kernel(
 
         gate_rows = gT.rearrange("(p t) s -> p t s", t=PACK)
 
-        load_packed_scales(nc.gpsimd, doc_scale_win, tab2_scales)
+        for Q in range(QUADRANTS):
+            nc.gpsimd.dma_start(
+                out=doc_scale_win[32 * Q + ROWS : 32 * Q + ROWS * (1 + DOC_PASSES), :].bitcast(I32),
+                in_=tab2_scales[:, ROWS * Q : ROWS * (Q + 1), :].bitcast(I32),
+            )
         for Q in range(QUADRANTS):
             nc.gpsimd.dma_start(
                 out=a2_planes[32 * Q : 32 * Q + ROWS, :, :].bitcast(I32),
@@ -125,20 +122,25 @@ def tile_list_gated_bilinear_decoder_kernel(
         load_words(tok_win[1], tab_words[1])
         nc.vector.tensor_copy(tok_scale_rows[:], tok_scale_win[:].indirect(idx[:]))
         move_plane(0)
-        load_rows(a1_raw[1], a1[K_PASS:K, :])
-        move_plane(1)
         nc.sync.dma_start(out=a2_codes[:].bitcast(I32), in_=a2_words.rearrange("a p e -> p a e").bitcast(I32))
+        load_rows(a1_raw[1], a1[K_PASS:K, :])
         load_words(doc_win[0], tab2_words[0])
+        move_plane(1)
         load_words(doc_win[1], tab2_words[1])
-        load_packed_scales(nc.sync, bd_planes, bd_scales)
         load_words(bd_codes[0], bd_words[0])
         load_words(doc_win[2], tab2_words[2])
+        for r in range(ROWS):
+            nc.sync.dma_start(
+                out=bd_planes[r:P:32, :, :].bitcast(I32),
+                in_=bd_scales[:, r:BLOCK_ROWS:ROWS, :].rearrange("a q e -> q a e").bitcast(I32),
+            )
         load_words(bd_codes[1], bd_words[1])
+        nc.sync.dma_start(out=gate_win[0][:], in_=gate_rows[:, 0, :])
+        load_words(bd_codes[2], bd_words[2])
+        nc.sync.dma_start(out=gate_win[1][:], in_=gate_rows[:, 1, :])
         nc.sync.dma_start(out=bias_rows[0 : N // P, :], in_=by.rearrange("(c p) -> c p", p=P))
-        for t in range(PACK):
+        for t in range(2, PACK):
             nc.sync.dma_start(out=gate_win[t][:], in_=gate_rows[:, t, :])
-            if t == 0:
-                load_words(bd_codes[2], bd_words[2])
         for c in range(CHUNKS):
             load_rows(w_raw[c], w[:, c * CHUNK : (c + 1) * CHUNK])
 
@@ -233,7 +235,7 @@ def tile_list_gated_bilinear_decoder_kernel(
         def doc_pass(acc, j, a):
             nc.tensor.matmul_mx(
                 out=acc[:], lhsT=token_tile(doc[a], j), lhsT_scale=doc_planes[ROWS * (a + 1) :, j * P : (j + 1) * P],
-                rhs=bd_codes[a][:].bitcast(FP8X4), rhs_scale=bd_planes[ROWS * (a + 1) :, :],
+                rhs=bd_codes[a][:].bitcast(FP8X4), rhs_scale=bd_planes[:, a, :],
                 start=(a == 0), stop=(a == DOC_PASSES - 1),
             )
 

@@ -38,7 +38,7 @@ BLOCKS = CHUNK // P
 GROUP = 256
 GROUPS = S // GROUP
 PAIR = GROUP // P
-TOKEN_PIECES = 2
+TOKEN_PIECES = 4
 DOC_PIECES = 2
 
 
@@ -69,17 +69,19 @@ def tile_list_gated_bilinear_decoder_kernel(
         a2_codes = held("a2_codes", [P, TOKEN_PASSES, 2 * H], U8)
         bd_codes = [held("bd_codes%d" % a, [P, H], I32) for a in range(DOC_PASSES)]
         tok_scale_rows = held("tok_scale_rows", [P, S], U8)
-        planes = held("planes", [P, TOKEN_PASSES * (S + H) + DOC_PASSES * H], U8)
-        planes_of_pass = [planes[:, a * S : (a + 1) * S] for a in range(TOKEN_PASSES)]
-        a2_planes = planes[:, TOKEN_PASSES * S : TOKEN_PASSES * (S + H)].rearrange("p (a e) -> p a e", e=H)
-        bd_planes = planes[:, TOKEN_PASSES * (S + H) :].rearrange("p (a e) -> p a e", e=H)
+        planes_of_pass = [held("tok_plane%d" % a, [P, S], U8) for a in range(TOKEN_PASSES)]
+        a2_planes = held("a2_planes", [P, TOKEN_PASSES, H], U8)
+        bd_planes = held("bd_planes", [P, DOC_PASSES, H], U8)
         bias_rows = held("bias_rows", [P, P], F32)
         bias = held("bias", [P, N // P], F32)
         ident = held("ident", [P, P], F32)
 
         nc.gpsimd.memset(doc_scale_win[:].bitcast(I32), 0)
         nc.gpsimd.memset(bias_rows[:], 0.0)
-        for dead in (tok_scale_win[0:LAST_QUADRANT, :], planes[:]):
+        for dead in (
+            a2_planes[:].rearrange("p a e -> p (a e)"), tok_scale_win[0:LAST_QUADRANT, :],
+            planes_of_pass[0][:], planes_of_pass[1][:], bd_planes[:].rearrange("p a e -> p (a e)"),
+        ):
             words = dead.bitcast(I32)
             nc.vector.memset(words[:, 1:], 0)
             nc.vector.memset(words[:, 0:1], 0)
@@ -89,6 +91,13 @@ def tile_list_gated_bilinear_decoder_kernel(
 
         def load_rows(dst, src):
             nc.sync.dma_start(out=dst[:], in_=src.rearrange("(p j) n -> p j n", j=PACK))
+
+        def load_weight_scales(queue, dst, src):
+            for r in range(ROWS):
+                queue.dma_start(
+                    out=dst[r:P:32, :, :].bitcast(I32),
+                    in_=src[:, r:BLOCK_ROWS:ROWS, :].rearrange("a q e -> q a e").bitcast(I32),
+                )
 
         def move_plane(a):
             first = LAST_QUADRANT + BLOCK_ROWS * a
@@ -105,11 +114,6 @@ def tile_list_gated_bilinear_decoder_kernel(
                 out=doc_scale_win[32 * Q + ROWS : 32 * Q + ROWS * (1 + DOC_PASSES), :].bitcast(I32),
                 in_=tab2_scales[:, ROWS * Q : ROWS * (Q + 1), :].bitcast(I32),
             )
-        for Q in range(QUADRANTS):
-            nc.gpsimd.dma_start(
-                out=a2_planes[32 * Q : 32 * Q + ROWS, :, :].bitcast(I32),
-                in_=a2_scales[:, ROWS * Q : ROWS * (Q + 1), :].rearrange("a r e -> r a e").bitcast(I32),
-            )
         make_identity(nc, ident[:])
 
         nc.sync.dma_start(idx[:], offs)
@@ -118,25 +122,22 @@ def tile_list_gated_bilinear_decoder_kernel(
         )
         nc.sync.dma_start(idx2[:], offs2)
         load_words(tok_win[0], tab_words[0])
+        load_weight_scales(nc.scalar, a2_planes, a2_scales)
         load_rows(a1_raw[0], a1[0:K_PASS, :])
-        load_words(tok_win[1], tab_words[1])
+        load_rows(a1_raw[1], a1[K_PASS:K, :])
+        nc.sync.dma_start(out=a2_codes[:].bitcast(I32), in_=a2_words.rearrange("a p e -> p a e").bitcast(I32))
         nc.vector.tensor_copy(tok_scale_rows[:], tok_scale_win[:].indirect(idx[:]))
         move_plane(0)
-        nc.sync.dma_start(out=a2_codes[:].bitcast(I32), in_=a2_words.rearrange("a p e -> p a e").bitcast(I32))
-        load_rows(a1_raw[1], a1[K_PASS:K, :])
-        load_words(doc_win[0], tab2_words[0])
+        load_words(tok_win[1], tab_words[1])
         move_plane(1)
+        load_words(doc_win[0], tab2_words[0])
         load_words(doc_win[1], tab2_words[1])
+        load_weight_scales(nc.sync, bd_planes, bd_scales)
         load_words(bd_codes[0], bd_words[0])
         load_words(doc_win[2], tab2_words[2])
-        for r in range(ROWS):
-            nc.sync.dma_start(
-                out=bd_planes[r:P:32, :, :].bitcast(I32),
-                in_=bd_scales[:, r:BLOCK_ROWS:ROWS, :].rearrange("a q e -> q a e").bitcast(I32),
-            )
         load_words(bd_codes[1], bd_words[1])
-        nc.sync.dma_start(out=gate_win[0][:], in_=gate_rows[:, 0, :])
         load_words(bd_codes[2], bd_words[2])
+        nc.sync.dma_start(out=gate_win[0][:], in_=gate_rows[:, 0, :])
         nc.sync.dma_start(out=gate_win[1][:], in_=gate_rows[:, 1, :])
         nc.sync.dma_start(out=bias_rows[0 : N // P, :], in_=by.rearrange("(c p) -> c p", p=P))
         for t in range(2, PACK):
@@ -158,19 +159,13 @@ def tile_list_gated_bilinear_decoder_kernel(
             u, first = divmod(j * P, S // len(parts))
             return parts[u][:, first : first + P].bitcast(FP8X4)
 
-        def rounded_rows(name, raw, width, on_vector=0):
+        def rounded_rows(name, raw, width):
             grouped = held(name + "_rounded", [P, width, PACK], BF16)
-            cut = width - on_vector
             nc.scalar.activation(
-                grouped[:, 0:cut, :].rearrange("p (c i) t -> p c t i", i=RUN),
-                raw[:, :, 0:cut].rearrange("p t (c i) -> p c t i", i=RUN),
+                grouped[:].rearrange("p (c i) t -> p c t i", i=RUN),
+                raw[:].rearrange("p t (c i) -> p c t i", i=RUN),
                 COPY,
             )
-            if on_vector:
-                nc.vector.tensor_copy(
-                    grouped[:, cut:width, :].rearrange("p (c i) t -> p c t i", i=RUN),
-                    raw[:, :, cut:width].rearrange("p t (c i) -> p c t i", i=RUN),
-                )
             return grouped
 
         def quantized(name, grouped, width):
@@ -184,9 +179,8 @@ def tile_list_gated_bilinear_decoder_kernel(
         tok = [gather_words("tok0", tok_win[0], idx, 1)]
         doc_planes = held("doc_planes", [P, S], U8, tag="tok_win0")
         nc.vector.tensor_copy(doc_planes[:], doc_scale_win[:].indirect(idx2[:]))
-        a1_mx = [quantized("a1_0", rounded_rows("a1_0", a1_raw[0], H), H)]
+        a1_mx = [quantized("a1_%d" % a, rounded_rows("a1_%d" % a, a1_raw[a], H), H) for a in range(TOKEN_PASSES)]
         tok.append(gather_words("tok1", tok_win[1], idx, TOKEN_PIECES))
-        a1_mx.append(quantized("a1_1", rounded_rows("a1_1", a1_raw[1], H, on_vector=H // 2), H))
         doc = [
             gather_words("doc%d" % a, doc_win[a], idx2, DOC_PIECES if a == DOC_PASSES - 1 else 1)
             for a in range(DOC_PASSES)
@@ -195,7 +189,7 @@ def tile_list_gated_bilinear_decoder_kernel(
         def dealt(acc):
             return acc[:].rearrange("p (m t) -> p t m", t=PACK)
 
-        pq_halves = [held("pq%d" % u, [P, HALF, PACK, P], F32, tag=("tok_win1", "doc_win0")[u]) for u in range(2)]
+        pq_halves = [held("pq%d" % u, [P, HALF, PACK, P], F32, tag=("tok_scale_win", "tok_win1")[u]) for u in range(2)]
         d_halves = [held("d%d" % u, [P, HALF, PACK, P], F32, tag="a1_raw%d" % u) for u in range(2)]
         a1_ops = [(codes[:].bitcast(FP8X4), scales[:]) for codes, scales in a1_mx]
         a2_ops = [(a2_codes[:, a, :].bitcast(FP4X4), a2_planes[:, a, :]) for a in range(TOKEN_PASSES)]
@@ -212,25 +206,18 @@ def tile_list_gated_bilinear_decoder_kernel(
             token_pass(acc, weight, j, 0)
             return acc
 
-        def closed(acc, weight, j, dst):
-            token_pass(acc, weight, j, 1)
-            nc.scalar.activation(dst, dealt(acc), COPY)
-
-        pq = [pq_halves[j // HALF][:, j % HALF] for j in range(TILES)]
-        q = [held("q%d" % j, [P, PACK, P], F32) for j in range(TILES)]
-        p_open = [opened(a1_ops, j, j) for j in range(HALF)]
-        q_open = [opened(a2_ops, j, HALF + j) for j in range(HALF)]
-        for j in range(HALF):
-            closed(q_open[j], a2_ops, j, q[j][:])
-        for j in range(HALF):
-            closed(p_open[j], a1_ops, j, pq[j])
-            nc.gpsimd.tensor_tensor(pq[j], pq[j], q[j][:], MULT)
-        freed = [(HALF + n) % TILES for n in range(TILES)]
-        for j in range(HALF, TILES):
-            first = 2 * (j - HALF)
-            closed(opened(a2_ops, j, freed[first]), a2_ops, j, q[j][:])
-            closed(opened(a1_ops, j, freed[first + 1]), a1_ops, j, pq[j])
-            nc.gpsimd.tensor_tensor(pq[j], pq[j], q[j][:], MULT)
+        p_open = [opened(a1_ops, j, 2 * j) for j in range(HALF)]
+        q_open = [opened(a2_ops, j, 2 * j + 1) for j in range(HALF)]
+        for j in range(TILES):
+            acc = p_open[j] if j < HALF else opened(a1_ops, j, 2 * (j - HALF))
+            token_pass(acc, a1_ops, j, 1)
+            pq = pq_halves[j // HALF][:, j % HALF]
+            nc.scalar.activation(pq, dealt(acc), COPY)
+            acc = q_open[j] if j < HALF else opened(a2_ops, j, 2 * (j - HALF) + 1)
+            token_pass(acc, a2_ops, j, 1)
+            q = held("q%d" % j, [P, PACK, P], F32)
+            nc.scalar.activation(q[:], dealt(acc), COPY)
+            nc.gpsimd.tensor_tensor(pq, pq, q[:], MULT)
 
         def doc_pass(acc, j, a):
             nc.tensor.matmul_mx(
@@ -239,7 +226,7 @@ def tile_list_gated_bilinear_decoder_kernel(
                 start=(a == 0), stop=(a == DOC_PASSES - 1),
             )
 
-        d_open = [bank(freed[j], [P, H]) for j in range(TILES)]
+        d_open = [bank(j, [P, H]) for j in range(TILES)]
         for j in range(TILES):
             for a in range(DOC_PASSES - 1):
                 doc_pass(d_open[j], j, a)
@@ -248,7 +235,7 @@ def tile_list_gated_bilinear_decoder_kernel(
             nc.scalar.activation(d_halves[j // HALF][:, j % HALF], dealt(d_open[j]), COPY)
 
         def turned_sum(j):
-            total = bank(freed[j], [P, PACK, P])
+            total = bank(j, [P, PACK, P])
             for t in range(PACK):
                 for halves, first in ((d_halves, True), (pq_halves, False)):
                     nc.tensor.matmul(
@@ -321,7 +308,7 @@ def tile_list_gated_bilinear_decoder_kernel(
         def next_group():
             grp = len(h_mx)
             h_mx.append(quantized("h%d" % grp, gated_group(grp), GROUP))
-            free[0:0] = freed[grp * PAIR : (grp + 1) * PAIR]
+            free[0:0] = range(grp * PAIR, (grp + 1) * PAIR)
             if grp == 0:
                 turned_bias = bank(free[1], [P, P])
                 nc.tensor.transpose(turned_bias[:], bias_rows[:], ident[:])

@@ -67,20 +67,21 @@ def tile_list_gated_bilinear_decoder_kernel(
         a1_raw = [held("a1_raw%d" % a, [P, PACK, H], F32) for a in range(TOKEN_PASSES)]
         w_raw = [held("w_raw%d" % c, [P, PACK, CHUNK], F32) for c in range(CHUNKS)]
         a2_codes = held("a2_codes", [P, TOKEN_PASSES, 2 * H], U8)
-        bd_codes = [held("bd_codes%d" % a, [P, H], I32) for a in range(DOC_PASSES)]
+        bd_first = held("bd_first", [P, DOC_PASSES - 1, H], I32)
+        bd_last = held("bd_last", [P, H], I32)
+        bd_codes = [bd_first[:, a, :] for a in range(DOC_PASSES - 1)] + [bd_last[:]]
         tok_scale_rows = held("tok_scale_rows", [P, S], U8)
         planes_of_pass = [held("tok_plane%d" % a, [P, S], U8) for a in range(TOKEN_PASSES)]
         a2_planes = held("a2_planes", [P, TOKEN_PASSES, H], U8)
-        bd_planes = held("bd_planes", [P, DOC_PASSES, H], U8)
+        bd_planes = held("bd_planes", [P, H], U8)
         bias_rows = held("bias_rows", [P, P], F32)
         bias = held("bias", [P, N // P], F32)
         ident = held("ident", [P, P], F32)
 
         nc.gpsimd.memset(doc_scale_win[:].bitcast(I32), 0)
-        nc.gpsimd.memset(bias_rows[:], 0.0)
         for dead in (
             a2_planes[:].rearrange("p a e -> p (a e)"), tok_scale_win[0:LAST_QUADRANT, :],
-            planes_of_pass[0][:], planes_of_pass[1][:], bd_planes[:].rearrange("p a e -> p (a e)"),
+            planes_of_pass[0][:], planes_of_pass[1][:], bd_planes[:],
         ):
             words = dead.bitcast(I32)
             nc.vector.memset(words[:, 1:], 0)
@@ -92,13 +93,6 @@ def tile_list_gated_bilinear_decoder_kernel(
         def load_rows(dst, src):
             nc.sync.dma_start(out=dst[:], in_=src.rearrange("(p j) n -> p j n", j=PACK))
 
-        def load_weight_scales(queue, dst, src):
-            for r in range(ROWS):
-                queue.dma_start(
-                    out=dst[r:P:32, :, :].bitcast(I32),
-                    in_=src[:, r:BLOCK_ROWS:ROWS, :].rearrange("a q e -> q a e").bitcast(I32),
-                )
-
         def move_plane(a):
             first = LAST_QUADRANT + BLOCK_ROWS * a
             for r in range(ROWS):
@@ -109,11 +103,13 @@ def tile_list_gated_bilinear_decoder_kernel(
 
         gate_rows = gT.rearrange("(p t) s -> p t s", t=PACK)
 
-        for Q in range(QUADRANTS):
-            nc.gpsimd.dma_start(
-                out=doc_scale_win[32 * Q + ROWS : 32 * Q + ROWS * (1 + DOC_PASSES), :].bitcast(I32),
-                in_=tab2_scales[:, ROWS * Q : ROWS * (Q + 1), :].bitcast(I32),
-            )
+        for dst, src in ((doc_scale_win, tab2_scales), (bd_planes, bd_scales)):
+            for Q in range(QUADRANTS):
+                nc.gpsimd.dma_start(
+                    out=dst[32 * Q + ROWS : 32 * Q + ROWS * (1 + DOC_PASSES), :].bitcast(I32),
+                    in_=src[:, ROWS * Q : ROWS * (Q + 1), :].bitcast(I32),
+                )
+        nc.gpsimd.memset(bias_rows[:], 0.0)
         make_identity(nc, ident[:])
 
         nc.sync.dma_start(idx[:], offs)
@@ -122,7 +118,11 @@ def tile_list_gated_bilinear_decoder_kernel(
         )
         nc.sync.dma_start(idx2[:], offs2)
         load_words(tok_win[0], tab_words[0])
-        load_weight_scales(nc.scalar, a2_planes, a2_scales)
+        for r in range(ROWS):
+            nc.scalar.dma_start(
+                out=a2_planes[r:P:32, :, :].bitcast(I32),
+                in_=a2_scales[:, r:BLOCK_ROWS:ROWS, :].rearrange("a q e -> q a e").bitcast(I32),
+            )
         load_rows(a1_raw[0], a1[0:K_PASS, :])
         load_rows(a1_raw[1], a1[K_PASS:K, :])
         nc.sync.dma_start(out=a2_codes[:].bitcast(I32), in_=a2_words.rearrange("a p e -> p a e").bitcast(I32))
@@ -132,12 +132,12 @@ def tile_list_gated_bilinear_decoder_kernel(
         move_plane(1)
         load_words(doc_win[0], tab2_words[0])
         load_words(doc_win[1], tab2_words[1])
-        load_weight_scales(nc.sync, bd_planes, bd_scales)
-        load_words(bd_codes[0], bd_words[0])
+        nc.sync.dma_start(
+            out=bd_first[:], in_=bd_words[0 : DOC_PASSES - 1].rearrange("a p e i -> p a (e i)").bitcast(I32)
+        )
         load_words(doc_win[2], tab2_words[2])
-        load_words(bd_codes[1], bd_words[1])
-        load_words(bd_codes[2], bd_words[2])
         nc.sync.dma_start(out=gate_win[0][:], in_=gate_rows[:, 0, :])
+        load_words(bd_last, bd_words[DOC_PASSES - 1])
         nc.sync.dma_start(out=gate_win[1][:], in_=gate_rows[:, 1, :])
         nc.sync.dma_start(out=bias_rows[0 : N // P, :], in_=by.rearrange("(c p) -> c p", p=P))
         for t in range(2, PACK):
@@ -182,7 +182,7 @@ def tile_list_gated_bilinear_decoder_kernel(
         a1_mx = [quantized("a1_%d" % a, rounded_rows("a1_%d" % a, a1_raw[a], H), H) for a in range(TOKEN_PASSES)]
         tok.append(gather_words("tok1", tok_win[1], idx, TOKEN_PIECES))
         doc = [
-            gather_words("doc%d" % a, doc_win[a], idx2, DOC_PIECES if a == DOC_PASSES - 1 else 1)
+            gather_words("doc%d" % a, doc_win[a], idx2, DOC_PIECES if a else 1)
             for a in range(DOC_PASSES)
         ]
 
@@ -222,7 +222,7 @@ def tile_list_gated_bilinear_decoder_kernel(
         def doc_pass(acc, j, a):
             nc.tensor.matmul_mx(
                 out=acc[:], lhsT=token_tile(doc[a], j), lhsT_scale=doc_planes[ROWS * (a + 1) :, j * P : (j + 1) * P],
-                rhs=bd_codes[a][:].bitcast(FP8X4), rhs_scale=bd_planes[:, a, :],
+                rhs=bd_codes[a].bitcast(FP8X4), rhs_scale=bd_planes[ROWS * (a + 1) :, :],
                 start=(a == 0), stop=(a == DOC_PASSES - 1),
             )
 

@@ -38,7 +38,7 @@ BLOCKS = CHUNK // P
 GROUP = 256
 GROUPS = S // GROUP
 PAIR = GROUP // P
-TOKEN_PIECES = 4
+TOKEN_PIECES = 1
 DOC_PIECES = 2
 
 
@@ -124,11 +124,11 @@ def tile_list_gated_bilinear_decoder_kernel(
                 in_=a2_scales[:, r:BLOCK_ROWS:ROWS, :].rearrange("a q e -> q a e").bitcast(I32),
             )
         load_rows(a1_raw[0], a1[0:K_PASS, :])
-        load_rows(a1_raw[1], a1[K_PASS:K, :])
         nc.sync.dma_start(out=a2_codes[:].bitcast(I32), in_=a2_words.rearrange("a p e -> p a e").bitcast(I32))
+        load_words(tok_win[1], tab_words[1])
         nc.vector.tensor_copy(tok_scale_rows[:], tok_scale_win[:].indirect(idx[:]))
         move_plane(0)
-        load_words(tok_win[1], tab_words[1])
+        load_rows(a1_raw[1], a1[K_PASS:K, :])
         move_plane(1)
         load_words(doc_win[0], tab2_words[0])
         load_words(doc_win[1], tab2_words[1])
@@ -145,11 +145,11 @@ def tile_list_gated_bilinear_decoder_kernel(
         for c in range(CHUNKS):
             load_rows(w_raw[c], w[:, c * CHUNK : (c + 1) * CHUNK])
 
-        def gather_words(name, win, lst, pieces):
+        def gather_words(name, win, lst, pieces, tag=""):
             count = S // pieces
             parts = []
             for u in range(pieces):
-                picked = held("%s_%d" % (name, u), [P, count], U32)
+                picked = held("%s_%d" % (name, u), [P, count], U32, tag=tag)
                 entries = lst[:, u * count // LIST : (u + 1) * count // LIST]
                 nc.vector.tensor_copy(picked[:], win[:].bitcast(U32).indirect(entries))
                 parts.append(picked)
@@ -159,13 +159,19 @@ def tile_list_gated_bilinear_decoder_kernel(
             u, first = divmod(j * P, S // len(parts))
             return parts[u][:, first : first + P].bitcast(FP8X4)
 
-        def rounded_rows(name, raw, width):
+        def rounded_rows(name, raw, width, on_vector=0):
             grouped = held(name + "_rounded", [P, width, PACK], BF16)
+            cut = width - on_vector
             nc.scalar.activation(
-                grouped[:].rearrange("p (c i) t -> p c t i", i=RUN),
-                raw[:].rearrange("p t (c i) -> p c t i", i=RUN),
+                grouped[:, 0:cut, :].rearrange("p (c i) t -> p c t i", i=RUN),
+                raw[:, :, 0:cut].rearrange("p t (c i) -> p c t i", i=RUN),
                 COPY,
             )
+            if on_vector:
+                nc.vector.tensor_copy(
+                    grouped[:, cut:width, :].rearrange("p (c i) t -> p c t i", i=RUN),
+                    raw[:, :, cut:width].rearrange("p t (c i) -> p c t i", i=RUN),
+                )
             return grouped
 
         def quantized(name, grouped, width):
@@ -179,8 +185,9 @@ def tile_list_gated_bilinear_decoder_kernel(
         tok = [gather_words("tok0", tok_win[0], idx, 1)]
         doc_planes = held("doc_planes", [P, S], U8, tag="tok_win0")
         nc.vector.tensor_copy(doc_planes[:], doc_scale_win[:].indirect(idx2[:]))
-        a1_mx = [quantized("a1_%d" % a, rounded_rows("a1_%d" % a, a1_raw[a], H), H) for a in range(TOKEN_PASSES)]
-        tok.append(gather_words("tok1", tok_win[1], idx, TOKEN_PIECES))
+        a1_mx = [quantized("a1_0", rounded_rows("a1_0", a1_raw[0], H), H)]
+        tok.append(gather_words("tok1", tok_win[1], idx, TOKEN_PIECES, tag="a1_raw0"))
+        a1_mx.append(quantized("a1_1", rounded_rows("a1_1", a1_raw[1], H, on_vector=H // 2), H))
         doc = [
             gather_words("doc%d" % a, doc_win[a], idx2, DOC_PIECES if a else 1)
             for a in range(DOC_PASSES)

@@ -124,11 +124,11 @@ def tile_list_gated_bilinear_decoder_kernel(
                 in_=a2_scales[:, r:BLOCK_ROWS:ROWS, :].rearrange("a q e -> q a e").bitcast(I32),
             )
         load_rows(a1_raw[0], a1[0:K_PASS, :])
-        nc.sync.dma_start(out=a2_codes[:].bitcast(I32), in_=a2_words.rearrange("a p e -> p a e").bitcast(I32))
         load_words(tok_win[1], tab_words[1])
         nc.vector.tensor_copy(tok_scale_rows[:], tok_scale_win[:].indirect(idx[:]))
         move_plane(0)
         load_rows(a1_raw[1], a1[K_PASS:K, :])
+        nc.sync.dma_start(out=a2_codes[:].bitcast(I32), in_=a2_words.rearrange("a p e -> p a e").bitcast(I32))
         move_plane(1)
         load_words(doc_win[0], tab2_words[0])
         load_words(doc_win[1], tab2_words[1])
@@ -159,19 +159,13 @@ def tile_list_gated_bilinear_decoder_kernel(
             u, first = divmod(j * P, S // len(parts))
             return parts[u][:, first : first + P].bitcast(FP8X4)
 
-        def rounded_rows(name, raw, width, on_vector=0):
+        def rounded_rows(name, raw, width):
             grouped = held(name + "_rounded", [P, width, PACK], BF16)
-            cut = width - on_vector
             nc.scalar.activation(
-                grouped[:, 0:cut, :].rearrange("p (c i) t -> p c t i", i=RUN),
-                raw[:, :, 0:cut].rearrange("p t (c i) -> p c t i", i=RUN),
+                grouped[:].rearrange("p (c i) t -> p c t i", i=RUN),
+                raw[:].rearrange("p t (c i) -> p c t i", i=RUN),
                 COPY,
             )
-            if on_vector:
-                nc.vector.tensor_copy(
-                    grouped[:, cut:width, :].rearrange("p (c i) t -> p c t i", i=RUN),
-                    raw[:, :, cut:width].rearrange("p t (c i) -> p c t i", i=RUN),
-                )
             return grouped
 
         def quantized(name, grouped, width):
@@ -183,11 +177,11 @@ def tile_list_gated_bilinear_decoder_kernel(
             return codes, scales
 
         tok = [gather_words("tok0", tok_win[0], idx, 1)]
-        doc_planes = held("doc_planes", [P, S], U8, tag="tok_win0")
+        doc_planes = held("doc_planes", [P, S], U8, tag="tok_win1")
         nc.vector.tensor_copy(doc_planes[:], doc_scale_win[:].indirect(idx2[:]))
         a1_mx = [quantized("a1_0", rounded_rows("a1_0", a1_raw[0], H), H)]
         tok.append(gather_words("tok1", tok_win[1], idx, TOKEN_PIECES, tag="a1_raw0"))
-        a1_mx.append(quantized("a1_1", rounded_rows("a1_1", a1_raw[1], H, on_vector=H // 2), H))
+        a1_mx.append(quantized("a1_1", rounded_rows("a1_1", a1_raw[1], H), H))
         doc = [
             gather_words("doc%d" % a, doc_win[a], idx2, DOC_PIECES if a else 1)
             for a in range(DOC_PASSES)
@@ -196,7 +190,7 @@ def tile_list_gated_bilinear_decoder_kernel(
         def dealt(acc):
             return acc[:].rearrange("p (m t) -> p t m", t=PACK)
 
-        pq_halves = [held("pq%d" % u, [P, HALF, PACK, P], F32, tag=("tok_scale_win", "tok_win1")[u]) for u in range(2)]
+        pq_halves = [held("pq%d" % u, [P, HALF, PACK, P], F32, tag=("tok_scale_win", "doc_win0")[u]) for u in range(2)]
         d_halves = [held("d%d" % u, [P, HALF, PACK, P], F32, tag="a1_raw%d" % u) for u in range(2)]
         a1_ops = [(codes[:].bitcast(FP8X4), scales[:]) for codes, scales in a1_mx]
         a2_ops = [(a2_codes[:, a, :].bitcast(FP4X4), a2_planes[:, a, :]) for a in range(TOKEN_PASSES)]
@@ -213,18 +207,25 @@ def tile_list_gated_bilinear_decoder_kernel(
             token_pass(acc, weight, j, 0)
             return acc
 
-        p_open = [opened(a1_ops, j, 2 * j) for j in range(HALF)]
-        q_open = [opened(a2_ops, j, 2 * j + 1) for j in range(HALF)]
-        for j in range(TILES):
-            acc = p_open[j] if j < HALF else opened(a1_ops, j, 2 * (j - HALF))
-            token_pass(acc, a1_ops, j, 1)
-            pq = pq_halves[j // HALF][:, j % HALF]
-            nc.scalar.activation(pq, dealt(acc), COPY)
-            acc = q_open[j] if j < HALF else opened(a2_ops, j, 2 * (j - HALF) + 1)
-            token_pass(acc, a2_ops, j, 1)
-            q = held("q%d" % j, [P, PACK, P], F32)
-            nc.scalar.activation(q[:], dealt(acc), COPY)
-            nc.gpsimd.tensor_tensor(pq, pq, q[:], MULT)
+        def closed(acc, weight, j, dst):
+            token_pass(acc, weight, j, 1)
+            nc.scalar.activation(dst, dealt(acc), COPY)
+
+        pq = [pq_halves[j // HALF][:, j % HALF] for j in range(TILES)]
+        q = [held("q%d" % j, [P, PACK, P], F32) for j in range(TILES)]
+        p_open = [opened(a1_ops, j, j) for j in range(HALF)]
+        q_open = [opened(a2_ops, j, HALF + j) for j in range(HALF)]
+        for j in range(HALF):
+            closed(q_open[j], a2_ops, j, q[j][:])
+        for j in range(HALF):
+            closed(p_open[j], a1_ops, j, pq[j])
+            nc.gpsimd.tensor_tensor(pq[j], pq[j], q[j][:], MULT)
+        freed = [(HALF + n) % TILES for n in range(TILES)]
+        for j in range(HALF, TILES):
+            first = 2 * (j - HALF)
+            closed(opened(a2_ops, j, freed[first]), a2_ops, j, q[j][:])
+            closed(opened(a1_ops, j, freed[first + 1]), a1_ops, j, pq[j])
+            nc.gpsimd.tensor_tensor(pq[j], pq[j], q[j][:], MULT)
 
         def doc_pass(acc, j, a):
             nc.tensor.matmul_mx(
@@ -233,7 +234,7 @@ def tile_list_gated_bilinear_decoder_kernel(
                 start=(a == 0), stop=(a == DOC_PASSES - 1),
             )
 
-        d_open = [bank(j, [P, H]) for j in range(TILES)]
+        d_open = [bank(freed[j], [P, H]) for j in range(TILES)]
         for j in range(TILES):
             for a in range(DOC_PASSES - 1):
                 doc_pass(d_open[j], j, a)
@@ -242,7 +243,7 @@ def tile_list_gated_bilinear_decoder_kernel(
             nc.scalar.activation(d_halves[j // HALF][:, j % HALF], dealt(d_open[j]), COPY)
 
         def turned_sum(j):
-            total = bank(j, [P, PACK, P])
+            total = bank(freed[j], [P, PACK, P])
             for t in range(PACK):
                 for halves, first in ((d_halves, True), (pq_halves, False)):
                     nc.tensor.matmul(
@@ -315,7 +316,7 @@ def tile_list_gated_bilinear_decoder_kernel(
         def next_group():
             grp = len(h_mx)
             h_mx.append(quantized("h%d" % grp, gated_group(grp), GROUP))
-            free[0:0] = range(grp * PAIR, (grp + 1) * PAIR)
+            free[0:0] = freed[grp * PAIR : (grp + 1) * PAIR]
             if grp == 0:
                 turned_bias = bank(free[1], [P, P])
                 nc.tensor.transpose(turned_bias[:], bias_rows[:], ident[:])

@@ -38,8 +38,6 @@ BLOCKS = CHUNK // P
 GROUP = 256
 GROUPS = S // GROUP
 PAIR = GROUP // P
-TOKEN_PIECES = 1
-DOC_PIECES = 2
 
 
 def tile_list_gated_bilinear_decoder_kernel(
@@ -71,7 +69,7 @@ def tile_list_gated_bilinear_decoder_kernel(
         bd_last = held("bd_last", [P, H], I32)
         bd_codes = [bd_first[:, a, :] for a in range(DOC_PASSES - 1)] + [bd_last[:]]
         tok_scale_rows = held("tok_scale_rows", [P, S], U8)
-        planes_of_pass = [held("tok_plane%d" % a, [P, S], U8) for a in range(TOKEN_PASSES)]
+        tok_planes = [held("tok_plane%d" % a, [P, S], U8) for a in range(TOKEN_PASSES)]
         a2_planes = held("a2_planes", [P, TOKEN_PASSES, H], U8)
         bd_planes = held("bd_planes", [P, H], U8)
         bias_rows = held("bias_rows", [P, P], F32)
@@ -81,7 +79,7 @@ def tile_list_gated_bilinear_decoder_kernel(
         nc.gpsimd.memset(doc_scale_win[:].bitcast(I32), 0)
         for dead in (
             a2_planes[:].rearrange("p a e -> p (a e)"), tok_scale_win[0:LAST_QUADRANT, :],
-            planes_of_pass[0][:], planes_of_pass[1][:], bd_planes[:],
+            tok_planes[0][:], tok_planes[1][:], bd_planes[:],
         ):
             words = dead.bitcast(I32)
             nc.vector.memset(words[:, 1:], 0)
@@ -97,7 +95,7 @@ def tile_list_gated_bilinear_decoder_kernel(
             first = LAST_QUADRANT + BLOCK_ROWS * a
             for r in range(ROWS):
                 nc.sync.dma_start(
-                    out=planes_of_pass[a][r:P:32, :].bitcast(I32),
+                    out=tok_planes[a][r:P:32, :].bitcast(I32),
                     in_=tok_scale_rows[first + r : first + BLOCK_ROWS : ROWS, :].bitcast(I32),
                 )
 
@@ -116,20 +114,20 @@ def tile_list_gated_bilinear_decoder_kernel(
         nc.sync.dma_start(
             out=tok_scale_win[LAST_QUADRANT:P, :].bitcast(I32), in_=tab_scales.rearrange("a q t -> (a q) t").bitcast(I32)
         )
-        nc.sync.dma_start(idx2[:], offs2)
         load_words(tok_win[0], tab_words[0])
         for r in range(ROWS):
-            nc.scalar.dma_start(
+            nc.sync.dma_start(
                 out=a2_planes[r:P:32, :, :].bitcast(I32),
                 in_=a2_scales[:, r:BLOCK_ROWS:ROWS, :].rearrange("a q e -> q a e").bitcast(I32),
             )
-        load_rows(a1_raw[0], a1[0:K_PASS, :])
         load_words(tok_win[1], tab_words[1])
+        nc.sync.dma_start(idx2[:], offs2)
+        nc.sync.dma_start(out=a2_codes[:].bitcast(I32), in_=a2_words.rearrange("a p e -> p a e").bitcast(I32))
         nc.vector.tensor_copy(tok_scale_rows[:], tok_scale_win[:].indirect(idx[:]))
         move_plane(0)
-        load_rows(a1_raw[1], a1[K_PASS:K, :])
-        nc.sync.dma_start(out=a2_codes[:].bitcast(I32), in_=a2_words.rearrange("a p e -> p a e").bitcast(I32))
+        load_rows(a1_raw[0], a1[0:K_PASS, :])
         move_plane(1)
+        load_rows(a1_raw[1], a1[K_PASS:K, :])
         load_words(doc_win[0], tab2_words[0])
         load_words(doc_win[1], tab2_words[1])
         nc.sync.dma_start(
@@ -138,18 +136,17 @@ def tile_list_gated_bilinear_decoder_kernel(
         load_words(doc_win[2], tab2_words[2])
         nc.sync.dma_start(out=gate_win[0][:], in_=gate_rows[:, 0, :])
         load_words(bd_last, bd_words[DOC_PASSES - 1])
-        nc.sync.dma_start(out=gate_win[1][:], in_=gate_rows[:, 1, :])
         nc.sync.dma_start(out=bias_rows[0 : N // P, :], in_=by.rearrange("(c p) -> c p", p=P))
-        for t in range(2, PACK):
+        for t in range(1, PACK):
             nc.sync.dma_start(out=gate_win[t][:], in_=gate_rows[:, t, :])
         for c in range(CHUNKS):
             load_rows(w_raw[c], w[:, c * CHUNK : (c + 1) * CHUNK])
 
-        def gather_words(name, win, lst, pieces, tag=""):
+        def gather_words(name, win, lst, pieces):
             count = S // pieces
             parts = []
             for u in range(pieces):
-                picked = held("%s_%d" % (name, u), [P, count], U32, tag=tag)
+                picked = held("%s_%d" % (name, u), [P, count], U32)
                 entries = lst[:, u * count // LIST : (u + 1) * count // LIST]
                 nc.vector.tensor_copy(picked[:], win[:].bitcast(U32).indirect(entries))
                 parts.append(picked)
@@ -159,13 +156,14 @@ def tile_list_gated_bilinear_decoder_kernel(
             u, first = divmod(j * P, S // len(parts))
             return parts[u][:, first : first + P].bitcast(FP8X4)
 
-        def rounded_rows(name, raw, width):
+        def rounded_rows(name, raw, width, on_vector=False):
             grouped = held(name + "_rounded", [P, width, PACK], BF16)
-            nc.scalar.activation(
-                grouped[:].rearrange("p (c i) t -> p c t i", i=RUN),
-                raw[:].rearrange("p t (c i) -> p c t i", i=RUN),
-                COPY,
-            )
+            dst = grouped[:].rearrange("p (c i) t -> p c t i", i=RUN)
+            src = raw[:].rearrange("p t (c i) -> p c t i", i=RUN)
+            if on_vector:
+                nc.vector.tensor_copy(dst, src)
+            else:
+                nc.scalar.activation(dst, src, COPY)
             return grouped
 
         def quantized(name, grouped, width):
@@ -176,56 +174,32 @@ def tile_list_gated_bilinear_decoder_kernel(
             )
             return codes, scales
 
-        tok = [gather_words("tok0", tok_win[0], idx, 1)]
-        doc_planes = held("doc_planes", [P, S], U8, tag="tok_win1")
+        tok = [gather_words("tok0", tok_win[0], idx, 1), gather_words("tok1", tok_win[1], idx, 2)]
+        doc_planes = held("doc_planes", [P, S], U8)
         nc.vector.tensor_copy(doc_planes[:], doc_scale_win[:].indirect(idx2[:]))
-        a1_mx = [quantized("a1_0", rounded_rows("a1_0", a1_raw[0], H), H)]
-        tok.append(gather_words("tok1", tok_win[1], idx, TOKEN_PIECES, tag="a1_raw0"))
-        a1_mx.append(quantized("a1_1", rounded_rows("a1_1", a1_raw[1], H), H))
-        doc = [
-            gather_words("doc%d" % a, doc_win[a], idx2, DOC_PIECES if a else 1)
-            for a in range(DOC_PASSES)
+        a1_mx = [
+            quantized("a1_%d" % a, rounded_rows("a1_%d" % a, a1_raw[a], H, on_vector=(a == 1)), H)
+            for a in range(TOKEN_PASSES)
         ]
+        doc = [gather_words("doc%d" % a, doc_win[a], idx2, 2 if a == DOC_PASSES - 1 else 1) for a in range(DOC_PASSES)]
 
         def dealt(acc):
             return acc[:].rearrange("p (m t) -> p t m", t=PACK)
 
-        pq_halves = [held("pq%d" % u, [P, HALF, PACK, P], F32, tag=("tok_scale_win", "doc_win0")[u]) for u in range(2)]
+        pq_halves = [held("pq%d" % u, [P, HALF, PACK, P], F32, tag="tok_win%d" % u) for u in range(2)]
         d_halves = [held("d%d" % u, [P, HALF, PACK, P], F32, tag="a1_raw%d" % u) for u in range(2)]
+        pq = [pq_halves[j // HALF][:, j % HALF] for j in range(TILES)]
+        d = [d_halves[j // HALF][:, j % HALF] for j in range(TILES)]
+        q = [held("q%d" % j, [P, PACK, P], F32) for j in range(TILES)]
         a1_ops = [(codes[:].bitcast(FP8X4), scales[:]) for codes, scales in a1_mx]
         a2_ops = [(a2_codes[:, a, :].bitcast(FP4X4), a2_planes[:, a, :]) for a in range(TOKEN_PASSES)]
 
         def token_pass(acc, weight, j, a):
             codes, scales = weight[a]
             nc.tensor.matmul_mx(
-                out=acc[:], lhsT=token_tile(tok[a], j), lhsT_scale=planes_of_pass[a][:, j * P : (j + 1) * P],
+                out=acc[:], lhsT=token_tile(tok[a], j), lhsT_scale=tok_planes[a][:, j * P : (j + 1) * P],
                 rhs=codes, rhs_scale=scales, start=(a == 0), stop=(a == TOKEN_PASSES - 1),
             )
-
-        def opened(weight, j, b):
-            acc = bank(b, [P, H])
-            token_pass(acc, weight, j, 0)
-            return acc
-
-        def closed(acc, weight, j, dst):
-            token_pass(acc, weight, j, 1)
-            nc.scalar.activation(dst, dealt(acc), COPY)
-
-        pq = [pq_halves[j // HALF][:, j % HALF] for j in range(TILES)]
-        q = [held("q%d" % j, [P, PACK, P], F32) for j in range(TILES)]
-        p_open = [opened(a1_ops, j, j) for j in range(HALF)]
-        q_open = [opened(a2_ops, j, HALF + j) for j in range(HALF)]
-        for j in range(HALF):
-            closed(q_open[j], a2_ops, j, q[j][:])
-        for j in range(HALF):
-            closed(p_open[j], a1_ops, j, pq[j])
-            nc.gpsimd.tensor_tensor(pq[j], pq[j], q[j][:], MULT)
-        freed = [(HALF + n) % TILES for n in range(TILES)]
-        for j in range(HALF, TILES):
-            first = 2 * (j - HALF)
-            closed(opened(a2_ops, j, freed[first]), a2_ops, j, q[j][:])
-            closed(opened(a1_ops, j, freed[first + 1]), a1_ops, j, pq[j])
-            nc.gpsimd.tensor_tensor(pq[j], pq[j], q[j][:], MULT)
 
         def doc_pass(acc, j, a):
             nc.tensor.matmul_mx(
@@ -234,25 +208,41 @@ def tile_list_gated_bilinear_decoder_kernel(
                 start=(a == 0), stop=(a == DOC_PASSES - 1),
             )
 
-        d_open = [bank(freed[j], [P, H]) for j in range(TILES)]
+        q_open = [bank(j, [P, H]) for j in range(TILES)]
+        for j in range(TILES):
+            token_pass(q_open[j], a2_ops, j, 0)
+        for j in range(TILES):
+            token_pass(q_open[j], a2_ops, j, 1)
+            nc.scalar.activation(q[j][:], dealt(q_open[j]), COPY)
+        for j in range(TILES):
+            acc = bank(j, [P, H])
+            for a in range(TOKEN_PASSES):
+                token_pass(acc, a1_ops, j, a)
+            nc.scalar.activation(pq[j], dealt(acc), COPY)
+            nc.gpsimd.tensor_tensor(pq[j], pq[j], q[j][:], MULT)
+        d_open = [bank(j, [P, H]) for j in range(TILES)]
         for j in range(TILES):
             for a in range(DOC_PASSES - 1):
                 doc_pass(d_open[j], j, a)
         for j in range(TILES):
             doc_pass(d_open[j], j, DOC_PASSES - 1)
-            nc.scalar.activation(d_halves[j // HALF][:, j % HALF], dealt(d_open[j]), COPY)
+            nc.scalar.activation(d[j], dealt(d_open[j]), COPY)
 
         def turned_sum(j):
-            total = bank(freed[j], [P, PACK, P])
+            total = bank(j, [P, PACK, P])
             for t in range(PACK):
-                for halves, first in ((d_halves, True), (pq_halves, False)):
+                for term, first in ((d[j], True), (pq[j], False)):
                     nc.tensor.matmul(
-                        total[:, t, :], lhsT=halves[j // HALF][:, j % HALF, t, :], rhs=ident[:],
+                        total[:, t, :], lhsT=term[:, t, :], rhs=ident[:],
                         is_transpose=True, start=first, stop=not first,
                     )
             return total
 
-        sums = [turned_sum(j) for j in range(TILES)]
+        sums = [turned_sum(j) for j in range(TILES - 1)]
+        turned_bias = bank(TILES - 1, [P, P])
+        nc.tensor.transpose(turned_bias[:], bias_rows[:], ident[:])
+        nc.scalar.activation(bias[:], turned_bias[:, 0 : N // P], COPY)
+        sums.append(turned_sum(TILES - 1))
 
         gate = held("gate", [P, PACK, S], F32)
         for t in range(PACK - 1):
@@ -264,19 +254,16 @@ def tile_list_gated_bilinear_decoder_kernel(
                 gate_win[PACK - 1][:].indirect(idx[:, grp * GROUP // LIST : (grp + 1) * GROUP // LIST]),
             )
 
-        def gated(h, grp, jj):
-            j = grp * PAIR + jj
-            nc.vector.tensor_tensor(
-                h[:, jj * P : (jj + 1) * P, :].rearrange("p (c i) t -> p c t i", i=RUN),
-                sums[j][:].rearrange("p t (c i) -> p c t i", i=RUN),
-                gate[:, :, j * P : (j + 1) * P].rearrange("p t (c i) -> p c t i", i=RUN),
-                MULT,
-            )
-
-        def gated_group(grp, tag=""):
-            h = held("h%d" % grp, [P, GROUP, PACK], BF16, tag=tag)
+        def gated_group(grp):
+            h = held("h%d" % grp, [P, GROUP, PACK], BF16)
             for jj in range(PAIR):
-                gated(h, grp, jj)
+                j = grp * PAIR + jj
+                nc.vector.tensor_tensor(
+                    h[:, jj * P : (jj + 1) * P, :].rearrange("p (c i) t -> p c t i", i=RUN),
+                    sums[j][:].rearrange("p t (c i) -> p c t i", i=RUN),
+                    gate[:, :, j * P : (j + 1) * P].rearrange("p t (c i) -> p c t i", i=RUN),
+                    MULT,
+                )
             return h
 
         spent = ["q%d" % j for j in range(TILES)] + ["a1_0_rounded", "a1_1_rounded", "doc_win2", "doc_win1"]
@@ -316,11 +303,7 @@ def tile_list_gated_bilinear_decoder_kernel(
         def next_group():
             grp = len(h_mx)
             h_mx.append(quantized("h%d" % grp, gated_group(grp), GROUP))
-            free[0:0] = freed[grp * PAIR : (grp + 1) * PAIR]
-            if grp == 0:
-                turned_bias = bank(free[1], [P, P])
-                nc.tensor.transpose(turned_bias[:], bias_rows[:], ident[:])
-                nc.scalar.activation(bias[:], turned_bias[:, 0 : N // P], COPY)
+            free[0:0] = list(range(grp * PAIR, (grp + 1) * PAIR))
             for c in range(len(w_mx)):
                 project(grp, c)
 

@@ -78,7 +78,7 @@ def tile_list_gated_bilinear_decoder_kernel(
 
         nc.gpsimd.memset(doc_scale_win[:].bitcast(I32), 0)
         for dead in (
-            a2_planes[:].rearrange("p a e -> p (a e)"), tok_scale_win[0:LAST_QUADRANT, :],
+            tok_scale_win[0:LAST_QUADRANT, :], a2_planes[:].rearrange("p a e -> p (a e)"),
             tok_planes[0][:], tok_planes[1][:], bd_planes[:],
         ):
             words = dead.bitcast(I32)
@@ -91,42 +91,45 @@ def tile_list_gated_bilinear_decoder_kernel(
         def load_rows(dst, src):
             nc.sync.dma_start(out=dst[:], in_=src.rearrange("(p j) n -> p j n", j=PACK))
 
-        def move_plane(a):
+        def move_plane(queue, a):
             first = LAST_QUADRANT + BLOCK_ROWS * a
             for r in range(ROWS):
-                nc.sync.dma_start(
+                queue.dma_start(
                     out=tok_planes[a][r:P:32, :].bitcast(I32),
                     in_=tok_scale_rows[first + r : first + BLOCK_ROWS : ROWS, :].bitcast(I32),
                 )
 
         gate_rows = gT.rearrange("(p t) s -> p t s", t=PACK)
 
-        for dst, src in ((doc_scale_win, tab2_scales), (bd_planes, bd_scales)):
+        def load_packed_planes(dst, src):
             for Q in range(QUADRANTS):
                 nc.gpsimd.dma_start(
                     out=dst[32 * Q + ROWS : 32 * Q + ROWS * (1 + DOC_PASSES), :].bitcast(I32),
                     in_=src[:, ROWS * Q : ROWS * (Q + 1), :].bitcast(I32),
                 )
-        nc.gpsimd.memset(bias_rows[:], 0.0)
-        make_identity(nc, ident[:])
+
+        load_packed_planes(doc_scale_win, tab2_scales)
+        for r in range(ROWS):
+            nc.gpsimd.dma_start(
+                out=a2_planes[r:P:32, :, :].bitcast(I32),
+                in_=a2_scales[:, r:BLOCK_ROWS:ROWS, :].rearrange("a q e -> q a e").bitcast(I32),
+            )
 
         nc.sync.dma_start(idx[:], offs)
         nc.sync.dma_start(
             out=tok_scale_win[LAST_QUADRANT:P, :].bitcast(I32), in_=tab_scales.rearrange("a q t -> (a q) t").bitcast(I32)
         )
         load_words(tok_win[0], tab_words[0])
-        for r in range(ROWS):
-            nc.sync.dma_start(
-                out=a2_planes[r:P:32, :, :].bitcast(I32),
-                in_=a2_scales[:, r:BLOCK_ROWS:ROWS, :].rearrange("a q e -> q a e").bitcast(I32),
-            )
         load_words(tok_win[1], tab_words[1])
         nc.sync.dma_start(idx2[:], offs2)
         nc.sync.dma_start(out=a2_codes[:].bitcast(I32), in_=a2_words.rearrange("a p e -> p a e").bitcast(I32))
         nc.vector.tensor_copy(tok_scale_rows[:], tok_scale_win[:].indirect(idx[:]))
-        move_plane(0)
+        move_plane(nc.sync, 0)
+        move_plane(nc.gpsimd, 1)
+        load_packed_planes(bd_planes, bd_scales)
+        nc.gpsimd.memset(bias_rows[:], 0.0)
+        make_identity(nc, ident[:])
         load_rows(a1_raw[0], a1[0:K_PASS, :])
-        move_plane(1)
         load_rows(a1_raw[1], a1[K_PASS:K, :])
         load_words(doc_win[0], tab2_words[0])
         load_words(doc_win[1], tab2_words[1])
@@ -136,9 +139,9 @@ def tile_list_gated_bilinear_decoder_kernel(
         load_words(doc_win[2], tab2_words[2])
         nc.sync.dma_start(out=gate_win[0][:], in_=gate_rows[:, 0, :])
         load_words(bd_last, bd_words[DOC_PASSES - 1])
-        nc.sync.dma_start(out=bias_rows[0 : N // P, :], in_=by.rearrange("(c p) -> c p", p=P))
         for t in range(1, PACK):
             nc.sync.dma_start(out=gate_win[t][:], in_=gate_rows[:, t, :])
+        nc.sync.dma_start(out=bias_rows[0 : N // P, :], in_=by.rearrange("(c p) -> c p", p=P))
         for c in range(CHUNKS):
             load_rows(w_raw[c], w[:, c * CHUNK : (c + 1) * CHUNK])
 

@@ -32,6 +32,7 @@ BLOCK_ROWS = 16
 LAST_QUADRANT = 96
 LIST = 16
 RUN = 4
+GATE_RUN = 2
 CHUNK = 256
 CHUNKS = N // CHUNK
 BLOCKS = CHUNK // P
@@ -262,9 +263,9 @@ def tile_list_gated_bilinear_decoder_kernel(
             for jj in range(PAIR):
                 j = grp * PAIR + jj
                 nc.vector.tensor_tensor(
-                    h[:, jj * P : (jj + 1) * P, :].rearrange("p (c i) t -> p c t i", i=RUN),
-                    sums[j][:].rearrange("p t (c i) -> p c t i", i=RUN),
-                    gate[:, :, j * P : (j + 1) * P].rearrange("p t (c i) -> p c t i", i=RUN),
+                    h[:, jj * P : (jj + 1) * P, :].rearrange("p (c i) t -> p c t i", i=GATE_RUN),
+                    sums[j][:].rearrange("p t (c i) -> p c t i", i=GATE_RUN),
+                    gate[:, :, j * P : (j + 1) * P].rearrange("p t (c i) -> p c t i", i=GATE_RUN),
                     MULT,
                 )
             return h

@@ -80,7 +80,7 @@ def tile_list_gated_bilinear_decoder_kernel(
         nc.gpsimd.memset(doc_scale_win[:].bitcast(I32), 0)
         for dead in (
             tok_scale_win[0:LAST_QUADRANT, :], a2_planes[:].rearrange("p a e -> p (a e)"),
-            tok_planes[0][:], tok_planes[1][:], bd_planes[:],
+            tok_planes[0][:], tok_planes[1][:], bd_planes[:], ident[:], bias_rows[:],
         ):
             words = dead.bitcast(I32)
             nc.vector.memset(words[:, 1:], 0)
@@ -128,8 +128,7 @@ def tile_list_gated_bilinear_decoder_kernel(
         move_plane(nc.sync, 0)
         move_plane(nc.gpsimd, 1)
         load_packed_planes(bd_planes, bd_scales)
-        nc.gpsimd.memset(bias_rows[:], 0.0)
-        make_identity(nc, ident[:])
+        make_identity(nc, ident[:], nomemset=True)
         load_rows(a1_raw[0], a1[0:K_PASS, :])
         load_rows(a1_raw[1], a1[K_PASS:K, :])
         load_words(doc_win[0], tab2_words[0])
@@ -194,7 +193,8 @@ def tile_list_gated_bilinear_decoder_kernel(
         d_halves = [held("d%d" % u, [P, HALF, PACK, P], F32, tag="a1_raw%d" % u) for u in range(2)]
         pq = [pq_halves[j // HALF][:, j % HALF] for j in range(TILES)]
         d = [d_halves[j // HALF][:, j % HALF] for j in range(TILES)]
-        q = [held("q%d" % j, [P, PACK, P], F32) for j in range(TILES)]
+        q_halves = [held("q%d" % u, [P, HALF, PACK, P], F32) for u in range(2)]
+        q = [q_halves[j // HALF][:, j % HALF] for j in range(TILES)]
         a1_ops = [(codes[:].bitcast(FP8X4), scales[:]) for codes, scales in a1_mx]
         a2_ops = [(a2_codes[:, a, :].bitcast(FP4X4), a2_planes[:, a, :]) for a in range(TOKEN_PASSES)]
 
@@ -217,13 +217,16 @@ def tile_list_gated_bilinear_decoder_kernel(
             token_pass(q_open[j], a2_ops, j, 0)
         for j in range(TILES):
             token_pass(q_open[j], a2_ops, j, 1)
-            nc.scalar.activation(q[j][:], dealt(q_open[j]), COPY)
+            nc.scalar.activation(q[j], dealt(q_open[j]), COPY)
         for j in range(TILES):
             acc = bank(j, [P, H])
             for a in range(TOKEN_PASSES):
                 token_pass(acc, a1_ops, j, a)
             nc.scalar.activation(pq[j], dealt(acc), COPY)
-            nc.gpsimd.tensor_tensor(pq[j], pq[j], q[j][:], MULT)
+            if j % PAIR:
+                u, last = divmod(j, HALF)
+                both = pq_halves[u][:, last - 1 : last + 1]
+                nc.gpsimd.tensor_tensor(both, both, q_halves[u][:, last - 1 : last + 1], MULT)
         d_open = [bank(j, [P, H]) for j in range(TILES)]
         for j in range(TILES):
             for a in range(DOC_PASSES - 1):
@@ -270,7 +273,7 @@ def tile_list_gated_bilinear_decoder_kernel(
                 )
             return h
 
-        spent = ["q%d" % j for j in range(TILES)] + ["a1_0_rounded", "a1_1_rounded", "doc_win2", "doc_win1"]
+        spent = [""] * TILES + ["a1_0_rounded", "a1_1_rounded", "doc_win2", "doc_win1"]
 
         def project(grp, c):
             b = free.pop(0)

@@ -159,6 +159,15 @@ def tile_list_gated_bilinear_decoder_kernel(
             u, first = divmod(j * P, S // len(parts))
             return parts[u][:, first : first + P].bitcast(FP8X4)
 
+        def rounded_on_gpsimd(name, raw, width):
+            grouped = held(name + "_rounded", [P, width, PACK], BF16)
+            for first in range(0, width, P):
+                cols = slice(first, first + P)
+                nc.gpsimd.tensor_scalar(
+                    grouped[:, cols, :], raw[:, :, cols].rearrange("p t c -> p c t"), 1.0, 0.0, MULT, ADD
+                )
+            return grouped
+
         def rounded_rows(name, raw, width, on_vector=False):
             grouped = held(name + "_rounded", [P, width, PACK], BF16)
             dst = grouped[:].rearrange("p (c i) t -> p c t i", i=RUN)
@@ -316,7 +325,8 @@ def tile_list_gated_bilinear_decoder_kernel(
 
         def next_chunk():
             c = len(w_mx)
-            w_mx.append(quantized("w%d" % c, rounded_rows("w%d" % c, w_raw[c], CHUNK), CHUNK))
+            rounded = rounded_on_gpsimd if c == 0 else rounded_rows
+            w_mx.append(quantized("w%d" % c, rounded("w%d" % c, w_raw[c], CHUNK), CHUNK))
             for grp in range(len(h_mx)):
                 project(grp, c)
 

from contextlib import ExitStack

import concourse.mybir as mybir
from concourse.masks import make_identity

K, C, H, N, T, S = 1024, 1536, 512, 768, 2048, 1024
FLOPS = 2 * S * H * (2 * K + C + N)

F32 = mybir.dt.float32
BF16 = mybir.dt.bfloat16
I32 = mybir.dt.int32
U32 = mybir.dt.uint32
U16 = mybir.dt.uint16
U8 = mybir.dt.uint8
FP8X4 = mybir.dt.float8_e4m3fn_x4
FP4X4 = mybir.dt.float4_e2m1fn_x4
COPY = mybir.ActivationFunctionType.Copy
IDENTITY = mybir.ActivationFunctionType.Identity
MULT = mybir.AluOpType.mult
ADD = mybir.AluOpType.add

P = 128
PACK = 4
K_PASS = P * PACK
TOKEN_PASSES = K // K_PASS
DOC_PASSES = C // K_PASS
TILES = S // P
HALF = TILES // 2
QUADRANTS = 4
ROWS = 4
BLOCK_ROWS = 16
LAST_QUADRANT = 96
LIST = 16
RUN = 4
GATE_RUN = 2
CHUNK = 256
CHUNKS = N // CHUNK
BLOCKS = CHUNK // P
GROUP = 256
GROUPS = S // GROUP
PAIR = GROUP // P


def tile_list_gated_bilinear_decoder_kernel(
    tc, tab_words, tab_scales, tab2_words, tab2_scales, offs, offs2, a1,
    a2_words, a2_scales, bd_words, bd_scales, gT, w, by, out,
):
    nc = tc.nc
    with ExitStack() as ctx:
        sbuf = ctx.enter_context(tc.tile_pool(name="sbuf", bufs=1))
        psum = ctx.enter_context(tc.psum_pool(name="psum", bufs=1))

        def held(name, shape, dtype, tag=""):
            return sbuf.tile(shape, dtype, name=name, tag=tag or name, align_bytes=64)

        def bank(b, shape):
            return psum.tile(shape, F32, name="bank%d" % b)

        idx = held("idx", [P, S // LIST], U16)
        idx2 = held("idx2", [P, S // LIST], U16)
        tok_scale_win = held("tok_scale_win", [P, T], U8)
        doc_scale_win = held("doc_scale_win", [P, T], U8)
        tok_win = [held("tok_win%d" % a, [P, T], I32) for a in range(TOKEN_PASSES)]
        doc_win = [held("doc_win%d" % a, [P, T], I32) for a in range(DOC_PASSES)]
        gate_win = [held("gate_win%d" % t, [P, T], F32) for t in range(PACK)]
        a1_raw = [held("a1_raw%d" % a, [P, PACK, H], F32) for a in range(TOKEN_PASSES)]
        w_raw = [held("w_raw%d" % c, [P, PACK, CHUNK], F32) for c in range(CHUNKS)]
        a2_codes = held("a2_codes", [P, TOKEN_PASSES, 2 * H], U8)
        bd_first = held("bd_first", [P, DOC_PASSES - 1, H], I32)
        bd_last = held("bd_last", [P, H], I32)
        bd_codes = [bd_first[:, a, :] for a in range(DOC_PASSES - 1)] + [bd_last[:]]
        tok_scale_rows = held("tok_scale_rows", [P, S], U8)
        tok_planes = [held("tok_plane%d" % a, [P, S], U8) for a in range(TOKEN_PASSES)]
        a2_planes = held("a2_planes", [P, TOKEN_PASSES, H], U8)
        bd_planes = held("bd_planes", [P, H], U8)
        bias_rows = held("bias_rows", [P, P], F32)
        bias = held("bias", [P, N // P], F32)
        ident = held("ident", [P, P], F32)

        nc.gpsimd.memset(doc_scale_win[:].bitcast(I32), 0)
        for dead in (
            tok_scale_win[0:LAST_QUADRANT, :], a2_planes[:].rearrange("p a e -> p (a e)"),
            tok_planes[0][:], tok_planes[1][:], bd_planes[:], ident[:], bias_rows[:],
        ):
            words = dead.bitcast(I32)
            nc.vector.memset(words[:, 1:], 0)
            nc.vector.memset(words[:, 0:1], 0)

        def load_words(dst, src):
            nc.sync.dma_start(out=dst[:], in_=src.rearrange("p t i -> p (t i)").bitcast(I32))

        def load_rows(dst, src):
            nc.sync.dma_start(out=dst[:], in_=src.rearrange("(p j) n -> p j n", j=PACK))

        def move_plane(queue, a):
            first = LAST_QUADRANT + BLOCK_ROWS * a
            for r in range(ROWS):
                queue.dma_start(
                    out=tok_planes[a][r:P:32, :].bitcast(I32),
                    in_=tok_scale_rows[first + r : first + BLOCK_ROWS : ROWS, :].bitcast(I32),
                )

        gate_rows = gT.rearrange("(p t) s -> p t s", t=PACK)

        def load_packed_planes(dst, src):
            for Q in range(QUADRANTS):
                nc.gpsimd.dma_start(
                    out=dst[32 * Q + ROWS : 32 * Q + ROWS * (1 + DOC_PASSES), :].bitcast(I32),
                    in_=src[:, ROWS * Q : ROWS * (Q + 1), :].bitcast(I32),
                )

        load_packed_planes(doc_scale_win, tab2_scales)
        for r in range(ROWS):
            nc.gpsimd.dma_start(
                out=a2_planes[r:P:32, :, :].bitcast(I32),
                in_=a2_scales[:, r:BLOCK_ROWS:ROWS, :].rearrange("a q e -> q a e").bitcast(I32),
            )

        nc.sync.dma_start(idx[:], offs)
        nc.sync.dma_start(
            out=tok_scale_win[LAST_QUADRANT:P, :].bitcast(I32), in_=tab_scales.rearrange("a q t -> (a q) t").bitcast(I32)
        )
        load_words(tok_win[0], tab_words[0])
        load_words(tok_win[1], tab_words[1])
        nc.sync.dma_start(idx2[:], offs2)
        nc.sync.dma_start(out=a2_codes[:].bitcast(I32), in_=a2_words.rearrange("a p e -> p a e").bitcast(I32))
        nc.vector.tensor_copy(tok_scale_rows[:], tok_scale_win[:].indirect(idx[:]))
        move_plane(nc.sync, 0)
        move_plane(nc.gpsimd, 1)
        load_packed_planes(bd_planes, bd_scales)
        make_identity(nc, ident[:], nomemset=True)
        load_rows(a1_raw[0], a1[0:K_PASS, :])
        load_rows(a1_raw[1], a1[K_PASS:K, :])
        load_words(doc_win[0], tab2_words[0])
        load_words(doc_win[1], tab2_words[1])
        nc.sync.dma_start(
            out=bd_first[:], in_=bd_words[0 : DOC_PASSES - 1].rearrange("a p e i -> p a (e i)").bitcast(I32)
        )
        load_words(doc_win[2], tab2_words[2])
        nc.sync.dma_start(out=gate_win[0][:], in_=gate_rows[:, 0, :])
        load_words(bd_last, bd_words[DOC_PASSES - 1])
        for t in range(1, PACK):
            nc.sync.dma_start(out=gate_win[t][:], in_=gate_rows[:, t, :])
        nc.sync.dma_start(out=bias_rows[0 : N // P, :], in_=by.rearrange("(c p) -> c p", p=P))
        for c in range(CHUNKS):
            load_rows(w_raw[c], w[:, c * CHUNK : (c + 1) * CHUNK])

        def gather_words(name, win, lst, pieces):
            count = S // pieces
            parts = []
            for u in range(pieces):
                picked = held("%s_%d" % (name, u), [P, count], U32)
                entries = lst[:, u * count // LIST : (u + 1) * count // LIST]
                nc.vector.tensor_copy(picked[:], win[:].bitcast(U32).indirect(entries))
                parts.append(picked)
            return parts

        def token_tile(parts, j):
            u, first = divmod(j * P, S // len(parts))
            return parts[u][:, first : first + P].bitcast(FP8X4)

        def rounded_on_gpsimd(name, raw, width):
            grouped = held(name + "_rounded", [P, width, PACK], BF16)
            for first in range(0, width, P):
                cols = slice(first, first + P)
                nc.gpsimd.tensor_scalar(
                    grouped[:, cols, :], raw[:, :, cols].rearrange("p t c -> p c t"), 1.0, 0.0, MULT, ADD
                )
            return grouped

        def rounded_rows(name, raw, width, on_vector=False):
            grouped = held(name + "_rounded", [P, width, PACK], BF16)
            dst = grouped[:].rearrange("p (c i) t -> p c t i", i=RUN)
            src = raw[:].rearrange("p t (c i) -> p c t i", i=RUN)
            if on_vector:
                nc.vector.tensor_copy(dst, src)
            else:
                nc.scalar.activation(dst, src, COPY)
            return grouped

        def quantized(name, grouped, width):
            codes = held(name + "_codes", [P, width], U32)
            scales = held(name + "_scales", [P, width], U8)
            nc.vector.quantize_mx(
                out=codes[:].bitcast(FP8X4), scales=scales[:], in_=grouped[:].rearrange("p w t -> p (w t)")
            )
            return codes, scales

        tok = [gather_words("tok0", tok_win[0], idx, 1), gather_words("tok1", tok_win[1], idx, 2)]
        doc_planes = held("doc_planes", [P, S], U8)
        nc.vector.tensor_copy(doc_planes[:], doc_scale_win[:].indirect(idx2[:]))
        a1_mx = [
            quantized("a1_%d" % a, rounded_rows("a1_%d" % a, a1_raw[a], H, on_vector=(a == 1)), H)
            for a in range(TOKEN_PASSES)
        ]
        doc = [gather_words("doc%d" % a, doc_win[a], idx2, 2 if a == DOC_PASSES - 1 else 1) for a in range(DOC_PASSES)]

        def dealt(acc):
            return acc[:].rearrange("p (m t) -> p t m", t=PACK)

        pq_halves = [held("pq%d" % u, [P, HALF, PACK, P], F32, tag="tok_win%d" % u) for u in range(2)]
        d_halves = [held("d%d" % u, [P, HALF, PACK, P], F32, tag="a1_raw%d" % u) for u in range(2)]
        pq = [pq_halves[j // HALF][:, j % HALF] for j in range(TILES)]
        d = [d_halves[j // HALF][:, j % HALF] for j in range(TILES)]
        q_halves = [held("q%d" % u, [P, HALF, PACK, P], F32) for u in range(2)]
        q = [q_halves[j // HALF][:, j % HALF] for j in range(TILES)]
        a1_ops = [(codes[:].bitcast(FP8X4), scales[:]) for codes, scales in a1_mx]
        a2_ops = [(a2_codes[:, a, :].bitcast(FP4X4), a2_planes[:, a, :]) for a in range(TOKEN_PASSES)]

        def token_pass(acc, weight, j, a):
            codes, scales = weight[a]
            nc.tensor.matmul_mx(
                out=acc[:], lhsT=token_tile(tok[a], j), lhsT_scale=tok_planes[a][:, j * P : (j + 1) * P],
                rhs=codes, rhs_scale=scales, start=(a == 0), stop=(a == TOKEN_PASSES - 1),
            )

        def doc_pass(acc, j, a):
            nc.tensor.matmul_mx(
                out=acc[:], lhsT=token_tile(doc[a], j), lhsT_scale=doc_planes[ROWS * (a + 1) :, j * P : (j + 1) * P],
                rhs=bd_codes[a].bitcast(FP8X4), rhs_scale=bd_planes[ROWS * (a + 1) :, :],
                start=(a == 0), stop=(a == DOC_PASSES - 1),
            )

        q_open = [bank(j, [P, H]) for j in range(TILES)]
        for j in range(TILES):
            token_pass(q_open[j], a2_ops, j, 0)
        for j in range(TILES):
            token_pass(q_open[j], a2_ops, j, 1)
            nc.scalar.activation(q[j], dealt(q_open[j]), COPY)
        for j in range(TILES):
            acc = bank(j, [P, H])
            for a in range(TOKEN_PASSES):
                token_pass(acc, a1_ops, j, a)
            nc.scalar.activation(pq[j], dealt(acc), COPY)
            if j % PAIR:
                u, last = divmod(j, HALF)
                both = pq_halves[u][:, last - 1 : last + 1]
                nc.gpsimd.tensor_tensor(both, both, q_halves[u][:, last - 1 : last + 1], MULT)
        d_open = [bank(j, [P, H]) for j in range(TILES)]
        for j in range(TILES):
            for a in range(DOC_PASSES - 1):
                doc_pass(d_open[j], j, a)
        for j in range(TILES):
            doc_pass(d_open[j], j, DOC_PASSES - 1)
            nc.scalar.activation(d[j], dealt(d_open[j]), COPY)

        def turned_sum(j):
            total = bank(j, [P, PACK, P])
            for t in range(PACK):
                for term, first in ((d[j], True), (pq[j], False)):
                    nc.tensor.matmul(
                        total[:, t, :], lhsT=term[:, t, :], rhs=ident[:],
                        is_transpose=True, start=first, stop=not first,
                    )
            return total

        sums = [turned_sum(j) for j in range(TILES - 1)]
        turned_bias = bank(TILES - 1, [P, P])
        nc.tensor.transpose(turned_bias[:], bias_rows[:], ident[:])
        nc.scalar.activation(bias[:], turned_bias[:, 0 : N // P], COPY)
        sums.append(turned_sum(TILES - 1))

        gate = held("gate", [P, PACK, S], F32)
        for t in range(PACK - 1):
            nc.vector.tensor_copy(gate[:, t, :], gate_win[t][:].indirect(idx[:]))

        def last_gates(grp):
            nc.vector.tensor_copy(
                gate[:, PACK - 1, grp * GROUP : (grp + 1) * GROUP],
                gate_win[PACK - 1][:].indirect(idx[:, grp * GROUP // LIST : (grp + 1) * GROUP // LIST]),
            )

        def gated_group(grp):
            h = held("h%d" % grp, [P, GROUP, PACK], BF16)
            for jj in range(PAIR):
                j = grp * PAIR + jj
                nc.vector.tensor_tensor(
                    h[:, jj * P : (jj + 1) * P, :].rearrange("p (c i) t -> p c t i", i=GATE_RUN),
                    sums[j][:].rearrange("p t (c i) -> p c t i", i=GATE_RUN),
                    gate[:, :, j * P : (j + 1) * P].rearrange("p t (c i) -> p c t i", i=GATE_RUN),
                    MULT,
                )
            return h

        spent = [""] * TILES + ["a1_0_rounded", "a1_1_rounded", "doc_win2", "doc_win1"]

        def project(grp, c):
            b = free.pop(0)
            on_vector = grp == GROUPS - 1 and c != 1
            h_codes, h_scales = h_mx[grp]
            codes, scales = w_mx[c]
            y = bank(b, [P, BLOCKS, GROUP])
            staged = held("staged%d_%d" % (grp, c), [P, BLOCKS, GROUP], F32, tag=spent[grp * CHUNKS + c])
            for e in range(BLOCKS):
                chans = slice(e * P, (e + 1) * P)
                nc.tensor.matmul_mx(
                    out=y[:, e, :], lhsT=codes[:, chans].bitcast(FP8X4), lhsT_scale=scales[:, chans],
                    rhs=h_codes[:].bitcast(FP8X4), rhs_scale=h_scales[:], start=True, stop=True,
                )
            first = c * BLOCKS
            if on_vector:
                spread = bias[:, first : first + BLOCKS].unsqueeze(2).to_broadcast([P, BLOCKS, GROUP])
                nc.vector.tensor_tensor(staged[:], y[:], spread, ADD)
            else:
                for e in range(BLOCKS):
                    nc.scalar.activation(
                        staged[:, e, :], y[:, e, :], IDENTITY, bias=bias[:, first + e : first + e + 1]
                    )
            nc.sync.dma_start(
                out=out[c * CHUNK : (c + 1) * CHUNK, grp * GROUP : (grp + 1) * GROUP].rearrange(
                    "(e p) s -> p e s", p=P
                ),
                in_=staged[:],
            )
            free.append(b)

        h_mx, w_mx, free = [], [], []

        def next_group():
            grp = len(h_mx)
            h_mx.append(quantized("h%d" % grp, gated_group(grp), GROUP))
            free[0:0] = list(range(grp * PAIR, (grp + 1) * PAIR))
            for c in range(len(w_mx)):
                project(grp, c)

        def next_chunk():
            c = len(w_mx)
            rounded = rounded_on_gpsimd if c == 0 else rounded_rows
            w_mx.append(quantized("w%d" % c, rounded("w%d" % c, w_raw[c], CHUNK), CHUNK))
            for grp in range(len(h_mx)):
                project(grp, c)

        last_gates(0)
        next_group()
        last_gates(1)
        next_chunk()
        next_group()
        next_chunk()
        last_gates(2)
        next_group()
        next_chunk()
        last_gates(3)
        next_group()
